import numpy as np, ml_dtypes
CORES = [10,34,74,98]
N = 4
BF = ml_dtypes.bfloat16
def gentries(a):
    return np.ascontiguousarray(a.reshape(8, 16, -1).transpose(0, 2, 1)).reshape(8, -1)
def gtable(e):
    e = np.asarray(e); return np.ascontiguousarray(e.reshape(8, -1, 16).transpose(0, 2, 1)).reshape(128, -1).astype(np.int32)
V, E, G, P, K, J, RO, CM = 2048, 4096, 256, 4864, 4, 5, 3, 255
NEED = 9
NV = (9, 8, 16, 15, 0, 9, 8, 7)
NI = 2 * (K - 1) + 2 * (N - 1) * K
def cover(rng):
    return ((CM + 1) * (0.5 * rng.random((1, V)) + 0.5 * rng.random((16, V)))).astype(np.int64)
def blank():
    return np.full((K, E), -1), np.ones((K, P), bool)
def put(L, free, i, e, t):
    if L[i, e] < 0 and free[i, t]:
        L[i, e] = t; free[i, t] = False
def pair(L, free, c, l, e, f, up=0, down=0):
    i = (c[e] + l) % K; j = (c[f] + l) % K
    ok = (L[i, e] < 0) & (L[j, f] < 0) & free[i, f + up] & free[j, e + down]
    i, j, e, f = i[ok], j[ok], e[ok], f[ok]
    L[i, e] = f + up; L[j, f] = e + down; free[i, f + up] = False; free[j, e + down] = False
def sides(rng, reads):
    s = rng.integers(0, 2, len(reads)); return 2 * reads + s, 2 * reads + 1 - s
def weave(rng, L, free, c, reads, q):
    a, b = sides(rng, reads); b = np.roll(b, -1); keep = rng.random(len(reads)) >= q; more = keep & (rng.random(len(reads)) < 0.33)
    pair(L, free, c, 0, a[keep], b[keep]); pair(L, free, c, 1, a[more], b[more])
    u = np.concatenate([a[~keep], b[~keep]])
    v = rng.permutation(u[(u < (N - 1) * G) & (u % G < G - 8)])[:8]; k = len(v) // 4
    pair(L, free, c, 0, v[:k], v[k:2 * k], E, E); pair(L, free, c, 0, v[2 * k:3 * k], v[3 * k:4 * k], E, 0)
    for l in range(1, RO):
        u = rng.permutation(u); k = 3 * len(u) // 10; pair(L, free, c, l, u[:k], u[k:2 * k]); u = u[2 * k:]
def fill(rng, L, free, shut):
    free[:, shut] = False
    for i in range(K):
        e = np.flatnonzero(L[i] < 0); L[i, e] = rng.permutation(np.flatnonzero(free[i]))[:len(e)]
def closed(reads, k):
    reads = np.asarray(reads, np.int64)
    return np.concatenate([2 * reads, 2 * reads + 1] + [E + d * G + G - 1 - np.arange(k) for d in range(N - 1)]).astype(np.int64)
def show(rng, pool, last):
    return np.concatenate([rng.permutation(pool)[:G - len(last)], np.array(last, np.int64)])
def join(rng, L, free, c, reads, k):
    s = rng.integers(0, 2, len(reads)); s[k - 1] = reads[k - 1] & 1
    o, n = 2 * reads + s, 2 * reads + 1 - s; pair(L, free, c, 0, o[:-1], n[1:]); return o, n
def duel(rng, L, free, c, X, Y, Z, t, s):
    o, n = join(rng, L, free, c, np.concatenate([X, Y]), len(X)); f, b = int(o[len(X) - 1]), int(n[len(X)])
    o, n = join(rng, L, free, c, Z, len(Z)); e, h = int(o[-1]), int(n[0])
    if (c[e] + t - c[b]) % K == 0: c[e] = K - 1 - c[e]
    for l in range(t, RO): put(L, free, (c[e] + l) % K, e, f)
    for l in range(s, RO): put(L, free, (c[h] + l) % K, h, E + ((N - 2 + l - s) % (N - 1)) * G + G - 1)
    return f, e
def paint(rng, x, X, Y, Z, nv, inv, near):
    hi, lo = (0, CM) if inv else (CM, 0); on = rng.permutation(16)[:nv]
    x[:, X] = hi; x[:, Y] = lo; x[:, Z] = lo
    if near: x[on, Z[-1]] = CM - 1 if inv else 1
    else: x[np.ix_(on, Z)] = hi
def edge(me, mf, mh, d):
    wf = next(w for w in range(CM * mf // 2, 0, -1) if (2 * w * mh * me - d) % mf == 0); s = (2 * wf * mh * me - d) // mf
    we = next(w for w in range(s // mh, 0, -1) if (s - w * mh) % me == 0)
    return we, wf, (s - we * mh) // me
def fine(rng, L, free, c, x, X, Y, Z, t, nv, inv):
    duel(rng, L, free, c, X, Y, Z, t, RO)
    p = np.concatenate([rng.permutation(np.array([0, 1, 14, 15])), 2 + rng.permutation(12)])
    if nv < NEED: p = p[::-1]
    for j in range(16):
        for q, s in zip((Z, X, Y), edge(len(Z), len(X), len(Y), 1 if j < nv else -(j % 2))):
            v = s // len(q) + (np.arange(len(q)) < s % len(q)); x[p[j], q] = CM - v if inv else v
def draw(rng, one):
    t = [[one(rng, r, g) for g in range(8)] for r in range(N)]
    x, c, L, s = [np.stack([np.stack([a[i] for a in row]) for row in t]) for i in range(4)]
    return {"cov": np.ascontiguousarray(x.reshape(N, 128, V)).astype(np.float32).astype(BF), "cand": np.stack([gtable(a.reshape(8, -1)) for a in L]),
            "shown": np.stack([gtable(a) for a in s]), "cur0": np.stack([gtable(a) for a in c])}
def plain(rng, r, g):
    c = rng.integers(0, K, E); L, free = blank()
    weave(rng, L, free, c, rng.permutation(V), rng.choice(np.array([0.01, 0.05, 0.15, 0.3, 0.5]))); fill(rng, L, free, closed([], 0))
    return cover(rng), c, L, show(rng, np.arange(E), [])
def uneven(rng, r, g):
    c = np.minimum((K * rng.random(E) ** rng.choice(np.array([0.25, 1.0, 4.0]))).astype(np.int64), K - 1); L, free = blank()
    weave(rng, L, free, c, rng.permutation(V), rng.choice(np.array([0.02, 0.1, 0.4, 0.8]))); fill(rng, L, free, closed([], 0))
    x = np.exp2(np.log2(CM + 1.0) * rng.random((1, V))) * rng.random((16, V)) ** rng.choice(np.array([0.25, 1.0, 3.0]), (16, 1))
    return np.minimum(x.astype(np.int64), CM), c, L, show(rng, np.arange(E), [])
def atends(rng, r, g):
    n = 2 ** J; m = G // 4; c = (K - 1) * rng.integers(0, 2, E); L, free = blank()
    lx, ly, lz = [n + (int(rng.choice(np.array([0, 0, 1, -1, -3]))) if g < 6 else 0) for i in range(3)]
    a, z = (V - 1, 0) if (r + g) % 2 == 0 else (0, V - 1)
    mid = rng.permutation(np.arange(m, V - m)); k = lx - 1 + ly
    X = np.append(mid[:lx - 1], a); Y = mid[lx - 1:k]; Z = np.append(mid[k:k + lz - 1], z); mid = mid[k + lz - 1:]
    f, e = duel(rng, L, free, c, X, Y, Z, (r + g) % RO, (r + 2 * g) % RO)
    weave(rng, L, free, c, rng.permutation(np.concatenate([mid, np.arange(1, m), np.arange(V - m, V - 1)])), rng.choice(np.array([0.05, 0.2, 0.4])))
    fill(rng, L, free, closed(np.concatenate([X, Y, Z]), 3))
    x = CM * (rng.random((16, V)) < rng.choice(np.array([0.0, 0.1, 0.5, 1.0]), (1, V))).astype(np.int64)
    paint(rng, x, X, Y, Z, NV[(5 * (N - 1 - r) + 7 - g) % 8], g % 2 == 0, False)
    last = [e ^ 1, f ^ 1, f]
    return x, c, L, show(rng, np.setdiff1d(np.concatenate([np.arange(2 * m), np.arange(E - 2 * m, E)]), last), last)
def corner(rng, r, g, role):
    n = 2 ** J; c = np.full(E, (0, 1, 2, 3, K - 1, K - 2)[(r + role) % 6] % K); L, free = blank(); o = rng.permutation(V)
    x = cover(rng); x[:, 0::5] = 0; x[:, 1::5] = CM; pool = np.arange(E); last = []; shut = closed([], 0)
    if role < 2: weave(rng, L, free, c, o, float((r + role) % 2))
    elif role == 2:
        h = V // 2; k = h + h // 2; pair(L, free, c, 0, 2 * o[:h], 2 * o[:h] + 1)
        u = np.concatenate([2 * o[h:k], 2 * o[h:k] + 1])
        for e in u: put(L, free, c[e], e, e)
        u = rng.permutation(u); w = len(u) // 4; pair(L, free, c, 1, u[:w], u[w:2 * w]); weave(rng, L, free, c, o[k:], 0.3)
    elif role == 3:
        k = 0; i = r
        while k < V:
            w = min((1, 2, n - 1, n, n + 1, 3, 2 * n)[i % 7], V - k); a, b = sides(rng, o[k:k + w]); pair(L, free, c, 0, a[:-1], b[1:])
            if rng.random() < 0.4: pair(L, free, c, 0, a[-1:], b[:1])
            k += w; i += 1
        u = rng.permutation(np.flatnonzero(L[c, np.arange(E)] < 0)); w = 3 * len(u) // 10; pair(L, free, c, 1, u[:w], u[w:2 * w])
    else:
        lx, ly, lz = [int(v) for v in rng.choice(np.array([1, 2, n - 1, n, n + 1]), 3)]; k = lx + ly + lz
        X, Y, Z = o[:lx], o[lx:lx + ly], o[lx + ly:k]
        f, e = duel(rng, L, free, c, X, Y, Z, (r + role) % RO, (r + g) % RO); weave(rng, L, free, c, o[k:], 0.3)
        paint(rng, x, X, Y, Z, NV[(3 * r + role) % 8], r % 2 == 1 and role < 6, role % 2 == 1)
        last = [f]; pool = np.concatenate([2 * o[k:], 2 * o[k:] + 1]); shut = closed(o[:k], 1)
    fill(rng, L, free, shut)
    return x, c, L, show(rng, pool, last)
def ballots(rng):
    a, b = K - 1, 2 * (K - 1); v = np.full((N, 8, 4, NI), 8); s = b + K * np.arange(2 * (N - 1))
    first = np.unique(np.concatenate([np.array([0, a - 1, a, b - 1]), s, s + K - 1]))
    one = np.concatenate([rng.permutation(first), rng.permutation(np.setdiff1d(np.arange(NI), first))]); u = rng.permutation(8 * N).reshape(N, 8)
    top = 16
    while 2 * top <= NI: top = 2 * top
    for q in range(N):
        for g in range(8):
            for h in range(4):
                kind = (g + h) % 4; o = rng.permutation(NI)
                if kind == 0: v[q, g, h, o[q % 2:]] = 16
                elif kind == 1: v[q, g, h, one[u[q, g] % NI]] = 9
                elif kind == 3:
                    w = (16, top)[q % 2]; v[q, g, h, o[:w]] = 15 + rng.integers(0, 2, w)
    return v
def crowd(rng, r, g, votes):
    n = 2 ** J; c = rng.integers(0, K, E); L, free = blank(); x = cover(rng); o = rng.permutation(V); k = 0; hubs = []
    for h in range(4):
        lx, ly = [int(v) for v in rng.integers(1, 6, 2)]; xy = o[k:k + lx + ly]; k += lx + ly
        a, b = join(rng, L, free, c, xy, lx); hubs.append((int(a[lx - 1]), int(b[lx]))); x[:, xy[:lx]] = CM; x[:, xy[lx:]] = 0
    lx, ly, lz = ((n - 1, n, n - 3), (n - 1, n - 3, n), (n - 3, n, n - 1), (n - 3, n - 1, n))[(r + g // 2) % 4]; w = o[k:k + lx + ly + lz]; k += len(w)
    fine(rng, L, free, c, x, w[:lx], w[lx:lx + ly], w[lx + ly:], (r + 2 * g) % RO, (9, 8)[(r + g) % 2], rng.random() < 0.5)
    shut = closed(o[:k], 8)
    for h, (f, b) in enumerate(hubs):
        t = h % RO; on = rng.permutation(16); mine = votes[r, g, h]
        jobs = [(i, f, CM, mine[j]) for j, i in enumerate([y for y in range(K) if y != c[b]])]
        jobs += [(i, b, 0, mine[K - 1 + j]) for j, i in enumerate([y for y in range(K) if y != c[f]])]
        jobs += [(i, E + d * G + G - 1 - h - 4 * s, CM * (1 - s), votes[(r - d - 1) % N, (g + 2) % 8, h, 2 * (K - 1) + (s * (N - 1) + d) * K + i]) for s in range(2) for d in range(N - 1) for i in range(K)]
        for j, (i, p, v, nv) in enumerate(jobs):
            z = int(o[k]); k += 1; e = 2 * z + (j + h) % 2; c[e] = (i - t) % K; put(L, free, i, e, p)
            x[:, z] = CM - v; x[on[:nv], z] = v
    weave(rng, L, free, c, o[k:], rng.choice(np.array([0.05, 0.2, 0.4]))); fill(rng, L, free, shut)
    return x, c, L, show(rng, np.concatenate([2 * o[k:], 2 * o[k:] + 1]), [b for f, b in hubs[::-1]] + [f for f, b in hubs[::-1]])
def setup_inputs(rng):
    return draw(rng, plain)
def setup_inputs_spread(rng):
    return draw(rng, uneven)
def setup_inputs_ends(rng):
    return draw(rng, atends)
def setup_inputs_corners(rng):
    role = np.zeros(8, np.int64); p = int(rng.integers(0, 2)); role[p::2] = 4 + rng.permutation(4); role[1 - p::2] = rng.permutation(4)
    return draw(rng, lambda rng, r, g: corner(rng, r, g, int(role[g])))
def setup_inputs_crowd(rng):
    votes = ballots(rng)
    return draw(rng, lambda rng, r, g: crowd(rng, r, g, votes))
def check_inputs(d):
    bad = []
    x = np.asarray(d["cov"]).astype(np.float64)
    if not (np.all(x >= 0) and np.all(x <= CM) and np.all(x == np.floor(x))): bad.append("range of cov")
    for k, hi in (("cand", P - 1), ("shown", E - 1), ("cur0", K - 1)):
        if np.min(d[k]) < 0 or np.max(d[k]) > hi: bad.append("range of " + k)
    for k, m in (("cand", E), ("shown", G)):
        a = np.sort(np.stack([gentries(t) for t in d[k]]).reshape(N, 8, -1, m), axis=-1)
        if np.any(a[..., 1:] == a[..., :-1]): bad.append("a number twice in " + k)
    return bad
def seen(a, sl):
    s = np.take_along_axis(a, sl if a.ndim == 3 else sl[:, :, None, :], -1)
    return np.stack([np.concatenate([a[r]] + [np.roll(s[(r - d) % N], -2, axis=0) for d in range(1, N)], axis=-1) for r in range(N)])
def reference(cov, cand, shown, cur0):
    pick = np.take_along_axis; ar = np.arange(E)
    x = np.repeat(cov.astype(np.float32).astype(np.int32).reshape(N, 8, 16, V), 2, axis=3)
    x = np.concatenate([x, np.zeros((N, 8, 16, 1), np.int32)], axis=3)
    cl = np.stack([gentries(a) for a in cand]).astype(np.int64).reshape(N, 8, K, E)
    sl = np.stack([gentries(a) for a in shown]).astype(np.int64); c = np.stack([gentries(a) for a in cur0]).astype(np.int64)
    for rnd in range(RO):
        b = pick(cl, c[:, :, None, :], 2)[:, :, 0]
        own = b < E
        link = own & (b != ar) & (pick(b, np.where(own, b, ar), 2) == ar)
        nx = np.concatenate([np.where(link, b ^ 1, E), np.full((N, 8, 1), E)], axis=2)
        S = x; n = np.concatenate([np.ones((N, 8, E), np.int32), np.zeros((N, 8, 1), np.int32)], axis=2)
        for j in range(J):
            S = S + pick(S, nx[:, :, None, :], 3); n = n + pick(n, nx, 2); nx = pick(nx, nx, 2)
        w = S[..., ar ^ 1]; m = n[..., ar ^ 1]; pt = np.where(link, b, ar)
        wp = pick(w, pt[:, :, None, :], 3); mp = pick(m, pt, 2)
        bw = b[:, :, None, :]
        wf = pick(seen(w, sl), bw, 3); wh = pick(seen(wp, sl), bw, 3)
        mf = pick(seen(m, sl), b, 2)[:, :, None, :]; mh = pick(seen(mp, sl), b, 2)[:, :, None, :]; lf = pick(seen(link, sl), b, 2)
        m1 = m[:, :, None, :]
        vote = np.abs(w * mf - wf * m1) * mh < np.abs(wh * mf - wf * mh) * m1
        cut = ~link & lf & (np.add.reduce(vote.astype(np.int32), axis=2) >= NEED)
        hit = np.zeros((N, 8, P), bool)
        for r in range(N):
            for g in range(8): hit[r, g, b[r, g][cut[r, g]]] = True
        gone = np.array(hit[:, :, :E])
        for q in range(N):
            for d in range(1, N):
                for g in range(8): gone[q, g, sl[q, g][hit[(q + d) % N, (g - 2) % 8, E + (d - 1) * G:E + d * G]]] = True
        gone = gone | pick(gone, pt, 2)
        c = (c + (~link | gone).astype(np.int64)) % K
    return {"yc": np.stack([gtable(a) for a in c]).astype(np.float32), "ys": np.ascontiguousarray(S[..., :E]).reshape(N, 128, E).astype(np.float32)}

@@ -1,0 +1,552 @@
+from concourse.bass import DstId, RemoteDMATransfer
+from concourse.mybir import AluOpType as OP, ActivationFunctionType as AF
+
+E, GH, P, RO, N = 4096, 256, 4864, 3, 4
+BW = P // 16 + 2
+PB = 16 * BW
+PW = P + 16
+ES = E + 32
+KEYS = 4 * PB
+CA = 112
+S0, S1, Q0, R0, A0, BIGW = 0, ES, 2 * ES, 2 * ES + PW, 2 * ES + 2 * PW, 3 * ES + 2 * PW
+MARGIN = 2.4
+STAMP = (1e10, 1e14, 1e18)
+NDMA = 70
+
+F, B, I, U = "float32", "bfloat16", "int32", "uint16"
+SCRATCH = {
+    "BIG": ("sbuf", [128, BIGW], F), "W1": ("sbuf", [128, KEYS + 16 * (256 - CA)], B), "XB": ("sbuf", [128, ES], F),
+    "P0": ("sbuf", [128, PB], B), "P1": ("sbuf", [128, ES], B), "H": ("sbuf", [128, E + 2 * GH], B),
+    "WW1": ("sbuf", [128, 4 * BW], B), "WW2": ("sbuf", [128, 4 * BW], F),
+    "CI": ("sbuf", [128, 1024], I), "MB": ("sbuf", [128, 1024], B), "MK": ("sbuf", [128, 1024], F),
+    "STB": ("sbuf", [128, 8 * (256 - CA)], B), "STF": ("sbuf", [128, 4 * CA], F),
+    "IW": ("sbuf", [128, 256], F), "IB": ("sbuf", [128, 256], B), "SWN": ("sbuf", [128, 128], F),
+    "ZE": ("sbuf", [128, 144], B), "ZC": ("sbuf", [128, 144], B), "M0": ("sbuf", [128, 256], F), "M1": ("sbuf", [128, 256], B), "CO": ("sbuf", [128, 2048], B),
+    "KT": ("sbuf", [128, 32], F), "RT": ("sbuf", [128, 32], F), "YT": ("sbuf", [128, 32], F),
+    "RH": ("sbuf", [128, RO * 3 * 48], B), "HG": ("sbuf", [128, 48], B),
+    "COL": ("sbuf", [128, 8], F), "COLI": ("sbuf", [128, 8], I),
+    "SH": ("sbuf", [128, 16], I), "SA": ("sbuf", [128, 16], I), "SB": ("sbuf", [128, 16], I), "SF": ("sbuf", [128, 16], F), "SG": ("sbuf", [128, 16], F),
+    "SUM": ("sbuf", [128, 16], F), "SS2": ("sbuf", [128, 16], U), "LW": ("sbuf", [128, 32], U), "LX": ("sbuf", [128, 32], U),
+    "PS": ("sbuf", [128, 512], B), "PG": ("sbuf", [128, 512], F), "PH": ("sbuf", [128, 512], F), "PAY": ("sbuf", [128, 512], F), "SS": ("sbuf", [128, 16], U), "KH": ("sbuf", [128, 32], F), "DH": ("sbuf", [128, 32], F),
+    "TH": ("sbuf", [128, 32], F), "LH": ("sbuf", [128, 32], U), "AH": ("sbuf", [128, 16], B),
+}
+for _n in ("NG", "CB", "I16", "IBW", "SWB", "SW16"):
+    SCRATCH[_n] = ("sbuf", [128, 128], B)
+for _n in ("TB0", "TB1", "TN0", "TN1", "TG"):
+    SCRATCH[_n] = ("sbuf", [128, BW], B)
+for _n in ("LK", "TU", "MV", "MD", "DLO", "TP", "C", "CM"):
+    SCRATCH[_n] = ("sbuf", [128, 256], B)
+for _n in ("EW", "EN", "E1", "DUM", "DQ", "KD", "T1", "T2", "T3", "IO"):
+    SCRATCH[_n] = ("sbuf", [128, 256], F)
+for _n in ("BI", "J1", "J2"):
+    SCRATCH[_n] = ("sbuf", [128, 256], I)
+for _n in ("L0", "L1", "L2", "L3", "L4", "LS"):
+    SCRATCH[_n] = ("sbuf", [128, 258], U)
+for _n in ("LT", "LB", "LU", "LV", "LP", "LC"):
+    SCRATCH[_n] = ("sbuf", [128, 256], U)
+PSUM = ("X0", "X1", "X2", "X3", "SW", "CG", "PT", "SL")
+for _n in PSUM:
+    SCRATCH[_n] = ("psum", [128, 512], F)
+SEMAPHORES = ["cv", "ca", "cp", "cg"] + ["d%d" % i for i in range(NDMA)] + \
+    ["%s%d" % (k, r) for k in ("ac", "ar", "ah", "lc", "lr", "lh") for r in range(RO)]
+
+
+def mean_tables():
+    out = {}
+    for m in range(1, 33):
+        best = None
+        for k in range(1024 // m + 1, 2048 // m + 1):
+            mk = m * k
+            r = (2 ** 35 + mk) // (2 * mk)
+            err = abs(r * mk - 2 ** 34)
+            if r < 2 ** 24 and (best is None or err < best[0]):
+                best = (err, k, r)
+        out[m] = best[1:]
+    return out
+
+
+def rank_program(g, core, T, topo):
+    rank = T.rank_of(core)
+    if rank is None:
+        return
+    eng = {"v": g.vector, "a": g.scalar, "p": g.tensor, "g": g, "s": g.sync}
+    cnt = {"v": 0, "a": 0, "p": 0, "g": 0}
+    rec, waited, total, nd = {}, {}, {}, [0]
+
+    def span(x):
+        if isinstance(x, str):
+            return x, 0, SCRATCH[x][1][1] if x in SCRATCH else PB
+        if x[0] in PSUM:
+            return x[0], 0, 512
+        return x
+
+    def wait(q, ev):
+        s, v = ev
+        if waited.get((q, s), 0) < v:
+            eng[q].wait_ge(T.sem[s], v)
+            waited[(q, s)] = v
+
+    def note(ev, src, R, W):
+        for x in R:
+            n, lo, hi = span(x)
+            rec.setdefault(n, []).append((lo, hi, ev, False, src))
+        for x in W:
+            n, lo, hi = span(x)
+            rec[n] = [r for r in rec.get(n, []) if not (lo <= r[0] and r[1] <= hi)] + [(lo, hi, ev, True, src)]
+        total[ev[0]] = max(total.get(ev[0], 0), ev[1])
+
+    def deps(q, src, R, W):
+        need = {}
+        for x, wr in [(x, False) for x in R] + [(x, True) for x in W]:
+            n, lo, hi = span(x)
+            for r in rec.get(n, []):
+                if r[0] < hi and lo < r[1] and (wr or r[3]):
+                    if r[4] == src and src == "p":
+                        continue
+                    need[r[2][0]] = max(need.get(r[2][0], 0), r[2][1])
+        for s in need:
+            wait(q, (s, need[s]))
+
+    def op(q, fn, R, W, inc=True):
+        W = list(W) + [x for x in R if span(x)[0] in PSUM]
+        R = [x for x in R if span(x)[0] not in PSUM]
+        deps(q, q, R, W)
+        ins = fn()
+        if inc:
+            ins.then_inc(T.sem["c" + q], 1)
+            cnt[q] += 1
+            note(("c" + q, cnt[q]), q, R, W)
+        else:
+            note(("c" + q, cnt[q] + 1), q, R, W)
+
+    def dma(q, out, in_, R, W):
+        s = "d%d" % nd[0]
+        nd[0] += 1
+        deps(q, s, R, W)
+        eng[q].dma_start(out, in_).then_inc(T.sem[s], 16)
+        note((s, 16), s, R, W)
+
+    reach = [topo.engines(core, T.cores[(rank + d) % N]) for d in range(1, N)]
+    engs = [e for e in reach[0] if all(e in x for x in reach)]
+    ne = len(engs)
+
+    def send(parts, arr, loc, step, land):
+        srcs = [p[0] for p in parts]
+        deps("g", loc, srcs, [])
+        ids = []
+        for d in range(1, N):
+            rid, pid = topo.addr(T.cores[(rank + step * d) % N])[:2]
+            ids.append(DstId(rid=rid, pnc=pid))
+        share = ne // len(parts)
+        g.remote_dma_fused([RemoteDMATransfer(dst_ids=ids, dma_engine_mask=sum(1 << e for e in engs[k * share:(k + 1) * share]),
+                                              remote_sem=T.sem[arr], src=ap(src), dsts=[dst_of(d) for d in range(1, N)])
+                            for k, (src, dst_of) in enumerate(parts)], local_sem=T.sem[loc])
+        note((loc, ne), loc, srcs, [])
+        note((arr, ne * (N - 1)), arr, [], land)
+
+    def ap(x):
+        n, lo, hi = (x, 0, SCRATCH[x][1][1]) if isinstance(x, str) else x
+        return T[n][:, lo:hi]
+
+    def ts(out, a, s1, o0, s2=None, o1=None):
+        if o1 is None:
+            op("v", lambda: g.vector.tensor_scalar(ap(out), ap(a), s1, None, o0), [a], [out])
+        else:
+            op("v", lambda: g.vector.tensor_scalar(ap(out), ap(a), s1, s2, o0, o1), [a], [out])
+
+    def tt(out, a, b, o):
+        op("v", lambda: g.vector.tensor_tensor(ap(out), ap(a), ap(b), o), [a, b], [out])
+
+    def cp(out, a):
+        op("v", lambda: g.vector.tensor_copy(ap(out), ap(a)), [a], [out])
+
+    def ms(out, val):
+        op("v", lambda: g.vector.memset(ap(out), val), [], [out])
+
+    def act(out, a, func, bias=0.0, scale=1.0, extra=()):
+        op("a", lambda: g.scalar.activation(ap(out), ap(a), func, bias=bias, scale=scale), [a] + list(extra), [out])
+
+    def gt(out, win, lst, b, o):
+        op("v", lambda: g.vector.tensor_tensor(ap(out), ap(win).indirect(ap(lst)), ap(b), o), [win, lst, b], [out])
+
+    def gv(out, win, lst):
+        op("v", lambda: g.vector.tensor_copy(ap(out), ap(win).indirect(ap(lst))), [win, lst], [out])
+
+    def ga(out, win, lst, func=AF.Copy):
+        op("a", lambda: g.scalar.activation(ap(out), ap(win).indirect(ap(lst)), func), [win, lst], [out])
+
+    def mm(out, lhs, rhs, start, stop, rap=None):
+        r = ap(rhs) if rap is None else rap
+        op("p", lambda: g.tensor.matmul(ap(out), ap(lhs), r, start, stop), [lhs, rhs], [out], inc=stop)
+
+    def lin(out, terms):
+        for k, (lhs, rhs) in enumerate(terms):
+            mm(out, lhs, rhs, k == 0, k == len(terms) - 1)
+
+    def extract(out, row, c0, c1, Z="ZE", flip=0, start=True, stop=True):
+        for i in range(16):
+            j = i ^ flip
+            mm(out, (Z, 16 - j, 144 - j), (row, 16 * c0, 16 * c1), start and i == 0, stop and i == 15,
+               rap=T[row][:, 16 * c0 + i:16 * c1:16])
+
+    def gi(out, oap, pat, base, cm, flt=True):
+        if flt:
+            op("g", lambda: g.iota(oap, pat, base, cm, allow_small_or_imprecise_dtypes=True), [], [out])
+        else:
+            op("g", lambda: g.iota(oap, pat, base, cm), [], [out])
+
+    def gs(out, oap, a, iap, pat, cmp, fill, base, cm):
+        op("g", lambda: g.affine_select(oap, iap, pat, cmp, fill, base, cm), [a], [out])
+
+    def gcopy(out, a):
+        gs(out, ap(out), a, ap(a), [[0, out[2] - out[1]]], OP.is_ge, 0.0, 0, 0)
+
+    def big(o, c0, c1):
+        return ("BIG", o + 16 * c0, o + 16 * c1)
+
+    def upto(n, k=256):
+        return (n, 0, k)
+
+    def row_out(ch, tile):
+        if ch == 0:
+            rec["P0c1"] = list(rec["P0"])
+        dma("s", T.P0[ch:128:16, :], T[tile][:], [tile], ["P0c1" if ch else "P0"])
+
+    ID, IDF = ("IB", 0, 128), ("IW", 0, 128)
+    SL = ("SL", 0, 256)
+
+    def cursors_on():
+        ts("T1", "C", 0.25, OP.add)
+        ts("T2", "C", 0.75, OP.is_lt)
+        tt("CM", "T1", "T2", OP.mult)
+
+    def masks(c):
+        for i in range(4):
+            ts(("MB", 256 * i, 256 * i + 256), c, 0.25 * i, OP.is_equal)
+
+    def select():
+        for i in range(4):
+            blk = (256 * i, 256 * i + 256)
+            tt(("MK",) + blk, ("MB",) + blk, ("CI",) + blk, OP.mult)
+            mm(SL, IDF, ("MK",) + blk, i == 0, i == 3)
+
+    def derive(c0):
+        ts("BI", SL, -float(E), OP.add)
+        tt("T1", SL, "EN", OP.not_equal)
+        ts("J1", "BI", 4, OP.arith_shift_right)
+        ts("T2", "T1", -48.0, OP.mult, 48.0, OP.add)
+        tt("T3", "J1", "T1", OP.mult)
+        ts("J2", "BI", 15, OP.bitwise_and)
+        tt(c0, "T3", "T2", OP.add)
+
+    def derive_other(out):
+        ts("J1", "BI", 1, OP.bitwise_and)
+        ts("T1", "J1", -2.0, OP.mult, 1.0, OP.add)
+        tt(out, "T1", "J2", OP.add)
+
+    dma("s", T.BI[:], T.cur0[:], [], ["BI"])
+    dma("a", T.CI[:, 0:512], T.cand[:, 0:512], [], [("CI", 0, 512)])
+    dma("s", T.CI[:, 512:1024], T.cand[:, 512:1024], [], [("CI", 512, 1024)])
+    dma("s", T.CO[:], T.cov[:], [], ["CO"])
+    dma("s", T.SH[:], T.shown[:], [], ["SH"])
+    gi(("COLI", 0, 1), T.COLI[:, 0:1], [[0, 1]], 0, 1, False)
+    gi("CB", T.CB[:], [[0, 128]], 1, 0)
+    gs(("IB", 0, 128), T.IB[:, 0:128], "CB", T.CB[:], [[-1, 128]], OP.is_equal, 0.0, 0, 1)
+    gs(("IB", 128, 256), T.IB[:, 128:256], "CB", T.CB[:], [[-1, 128]], OP.is_equal, 0.0, 0, 1)
+    gi("IO", T.IO[:], [[16, 256]], -E, 0)
+    gs("SWB", T.SWB[:, 0:128:2], "CB", T.CB[:, 0:64], [[-2, 64]], OP.is_equal, 0.0, -1, 1)
+    gs("SWB", T.SWB[:, 1:128:2], "CB", T.CB[:, 0:64], [[-2, 64]], OP.is_equal, 0.0, 0, 1)
+    gi("ZE", T.ZE[:], [[0, 144]], 0, 0)
+    gs("ZE", T.ZE[:, 0:144:16], "ZE", T.ZE[:, 0:144:16], [[-16, 9]], OP.not_equal, 16.0, 16, 1)
+    gs("ZE", T.ZE[:, 0:144:16], "ZE", T.ZE[:, 0:144:16], [[-16, 9]], OP.not_equal, 1.0, 15, 1)
+    gi("ZC", T.ZC[:], [[0, 144]], 0, 0)
+    gs("ZC", T.ZC[:, 0:144:16], "CB", T.CB[:, 0:9], [[-16, 9]], OP.is_ge, 0.0, 16, 1)
+    gs("ZC", T.ZC[:, 0:144:16], "ZC", T.ZC[:, 0:144:16], [[16, 9]], OP.is_ge, 0.0, -1, -1)
+    tabs = mean_tables()
+    for t in range(32):
+        gi(("KT", t, t + 1), T.KT[:, t:t + 1], [[0, 1]], tabs[32 - t][0], 0)
+        gi(("RT", t, t + 1), T.RT[:, t:t + 1], [[0, 1]], tabs[32 - t][1], 0)
+    gi("YT", T.YT[:], [[-255, 32]], 255 * 32, 0)
+    ts(("COLI", 1, 2), ("COLI", 0, 1), 15, OP.bitwise_and)
+    ts(("COLI", 2, 3), ("COLI", 0, 1), 1, OP.bitwise_and)
+    ms("P0", 0.0)
+    cp(("COL", 0, 1), ("COLI", 1, 2))
+    ts(("COL", 1, 2), ("COLI", 2, 3), -2.0, OP.mult, 1.0, OP.add)
+    for n in ("TB0", "TB1", "TN0", "TN1", "TG"):
+        ms((n, 256, BW), 0.0)
+    tt(("COL", 1, 2), ("COL", 1, 2), ("COL", 0, 1), OP.add)
+    ms(("XB", E, ES), 0.0)
+    ms(("BIG", A0 + E, A0 + ES), 0.0)
+    act("IW", "IB", AF.Copy)
+    act("EW", "IO", AF.Identity, bias=T.COL[:, 0:1], extra=[("COL", 0, 1)])
+    act("EN", "EW", AF.Identity, bias=float(E))
+    act("IBW", ID, AF.Identity, scale=float(BW))
+    act("I16", ID, AF.Identity, scale=16.0)
+    act("SW16", "SWB", AF.Identity, scale=16.0)
+    act("SWN", "SWB", AF.Identity, scale=-1.0)
+    ts("C", "BI", 0.25, OP.mult)
+    masks("C")
+    select()
+    ts(("SF", 0, 2), ("EW", 0, 2), float(E + 1), OP.add, 31.0, OP.min)
+    cp(("SA", 0, 2), ("SF", 0, 2))
+    ts(("SB", 0, 2), ("SA", 0, 2), 4, OP.arith_shift_right)
+    ts(("SA", 2, 4), ("SA", 0, 2), 15, OP.bitwise_and)
+    cp(("TN0", 256, 258), ("SB", 0, 2))
+    cp(("TN1", 256, 258), ("SA", 2, 4))
+    derive(upto("TB0"))
+    row_out(0, "TB0")
+    cp(upto("TB1"), "J2")
+    row_out(1, "TB1")
+    lin(upto("CG"), [(ID, upto("TB0")), ("IBW", upto("TB1"))])
+    derive_other("DLO")
+    ts("LB", upto("CG"), 256.0, OP.add)
+    for h in range(2):
+        op("a", lambda h=h: g.scalar.activation(T.XB[:, h:E:2], T.CO[:], AF.Identity, bias=-127.5), ["CO"], [("XB", 0, E)])
+    ts("SB", "SH", 4, OP.arith_shift_right)
+    ts("SF", "SH", float(BW), OP.mult)
+    ts("SG", "SB", -float(PB - 1), OP.mult)
+    tt("SF", "SF", "SG", OP.add)
+    cp("SS", "SF")
+    cp("SG", "SH")
+    lin(("PT", 16, 32), [("SWN", "SG")])
+    ts("SA", ("PT", 16, 32), -1.0, OP.mult)
+    ts("SB", "SA", 4, OP.arith_shift_right)
+    ts("SF", "SA", float(BW), OP.mult)
+    ts("SG", "SB", -float(PB - 1), OP.mult)
+    ts("SB", "SA", 1, OP.bitwise_and)
+    tt("SF", "SF", "SG", OP.add)
+    ts("SG", "SB", -2.0, OP.mult, 1.0 - E, OP.add)
+    cp("SS2", "SF")
+    tt("SUM", "SG", "SA", OP.add)
+    ts(("LW", 0, 16), "SUM", float(E), OP.add)
+
+    CH = [(0, 64), (64, 128), (128, 192), (192, 256)]
+    CHS = CH[:3] + [(192, 258)]
+    CV = [(0, CA // 2), (CA // 2, CA), (CA, 224), (224, 256)]
+    BK = ["X0", "X1", "X2", "X3"]
+
+    for r in range(RO):
+        last = r == RO - 1
+        stamp = STAMP[r]
+        thr = 0.4 * stamp
+
+        def sums(c0, c1):
+            return ("XB", 16 * c0, 16 * c1) if last else big(S0, c0, c1)
+
+        lin(upto("SW"), [("SW16", upto("TB0")), ("SWB", "DLO")])
+        ts("LU", upto("SW"), float(E), OP.add)
+        for q, (c0, c1) in (("a", (0, 72)), ("v", (120, 200)), ("a", (72, 120)), ("v", (200, 256))):
+            deps(q, q, ["P0c1"], [])
+            (ga if q == "a" else gv)(("P1", 16 * c0, 16 * c1), "P0", ("LB", c0, c1))
+            extract(("X0", c0, c1), "P1", c0, c1)
+        ga(upto("PS"), "P0", "SS")
+        if r == 0:
+            for o in (0, 1024):
+                for h in range(2):
+                    op("a", lambda h=h, o=o: g.scalar.activation(T.BIG[:, A0 + 2 * o + h:A0 + 2 * o + 2048:2], T.CO[:, o:o + 1024], AF.Identity, bias=-127.5),
+                       ["CO"], [("BIG", A0 + 2 * o, A0 + 2 * o + 2048)])
+        tt("LK", upto("X0"), "EW", OP.is_equal)
+        tt(upto("TN0"), "LK", upto("TB0"), OP.mult)
+        row_out(0, "TN0")
+        tt(upto("TN1"), "LK", "DLO", OP.mult)
+        row_out(1, "TN1")
+        lin(upto("CG", 258), [("I16", upto("TN0", 258)), (ID, upto("TN1", 258))])
+        lin(upto("X3", 258), [(ID, upto("TN0", 258)), ("IBW", upto("TN1", 258))])
+        extract(("PT", 0, 16), "PS", 0, 16)
+        if r == 0:
+            act("E1", "IO", AF.Identity, bias=T.COL[:, 1:2], extra=[("COL", 1, 2)])
+            act(("DUM", 0, CA), ("EW", 0, CA), AF.Identity, bias=float(E + KEYS))
+            act(("DUM", CA, 256), ("EW", CA, 256), AF.Identity, bias=float(E + KEYS - 16 * CA))
+            act("DH", ("EW", 0, 32), AF.Identity, bias=float(2 * E))
+            act("DQ", "DUM", AF.Identity, scale=-0.25, bias=256.0)
+        ts("L0", upto("CG", 258), float(E), OP.add)
+        ts("LS", upto("X3", 258), 256.0, OP.add)
+        deps("a", "a", ["P0c1"], [])
+        for s in range(1, 6):
+            src = ("XB", 0) if s == 1 else ("BIG", S0 if s % 2 == 0 else S1)
+            dst = S0 if s % 2 == 1 else S1
+            pin, pout = ("P0", "P1") if s % 2 == 1 else ("P1", "P0")
+            lst = "L%d" % (s - 1)
+            for q, (c0, c1) in enumerate(CHS if s < 5 else CH):
+                if s > 1:
+                    ts((lst, c0, CHS[q][1]), (BK[q], 0, CHS[q][1] - c0), float(E), OP.add)
+                gt(big(dst, c0, c1) if s < 5 else sums(c0, c1), (src[0], src[1], src[1] + ES), (lst, c0, c1), big(A0, c0, c1), OP.add)
+                if s < 5:
+                    if q % 2:
+                        gcopy(big(A0, c0, c1), big(dst, c0, c1))
+                    else:
+                        dma("s", ap(big(A0, c0, c1)), ap(big(dst, c0, c1)), [big(dst, c0, c1)], [big(A0, c0, c1)])
+                ga((pout, 16 * c0, 16 * c1), (pin, 0, PB if s == 1 else ES), ("LS" if s == 1 else lst, c0, c1))
+                extract((BK[q], 0, c1 - c0), pout, c0, c1)
+            if s == 1:
+                tt("T1", "LK", "E1", OP.mult)
+                ga(upto("PS"), "P0", "SS2")
+                extract(("PT", 32, 48), "PS", 0, 16)
+            if s == 2:
+                lin(("SW", 0, 256), [("SW16", upto("TN0")), ("SWB", upto("TN1")), ("SWN", "T1"), (IDF, "EW")])
+                lin(SL, [(ID, upto("TB0")), ("IBW", upto("TB1")), (ID, "C"), (IDF, "DQ")])
+            if s == 3:
+                ts("LV", upto("SW"), float(E), OP.add)
+                ts("SF", ("PT", 32, 48), 0.0, OP.is_lt)
+                tt("SG", ("PT", 32, 48), "SUM", OP.subtract)
+                tt("SG", "SG", "SF", OP.mult)
+                tt("SG", "SG", "SUM", OP.add)
+                ts(("LW", 16, 32), "SG", float(E), OP.add)
+        ga("PS", ("P1", 0, E), "LW")
+        extract(("CG", 0, 32), "PS", 0, 32)
+        ga("PG", sums(0, 256), "LW")
+        act("KD", SL, AF.Identity, scale=4.0)
+        if r == 0:
+            act("RT", "RT", AF.Identity, scale=2.0 ** -17)
+        for q, (c0, c1) in enumerate(CH):
+            ts(("LT", c0, c1), (BK[q], 0, c1 - c0), 0.0, OP.max)
+            gt(big(S1, c0, c1), "KT", ("LT", c0, c1), sums(c0, c1), OP.mult)
+            if q != 1:
+                continue
+            ts("LX", ("CG", 0, 32), 0.0, OP.max)
+            gt("PH", "KT", "LX", "PG", OP.mult)
+            gt("PG", "RT", "LX", "PH", OP.mult)
+            lin(upto("SW"), [(("IW", 32, 160), upto("PG"))])
+            tt(upto("PH"), ("PG", 256, 512), upto("PG"), OP.subtract)
+            act(upto("PAY"), upto("SW"), AF.Copy)
+            send([(upto("PAY"), lambda d: T.BIG[:, Q0 + E + GH * (d - 1):Q0 + E + GH * d])], "ac%d" % r, "lc%d" % r, 1, [("BIG", Q0 + E, Q0 + P)])
+            lin(upto("CG"), [(("IW", 32, 160), upto("PH"))])
+            act(("PAY", 256, 512), upto("CG"), AF.Abs)
+            send([(("PAY", 256, 512), lambda d: T.BIG[:, R0 + E + GH * (d - 1):R0 + E + GH * d])], "ar%d" % r, "lr%d" % r, 1, [("BIG", R0 + E, R0 + P)])
+        if r == 0:
+            gi("H", T.H[:], [[0, E + 2 * GH]], 0, 0)
+            act("YT", "YT", AF.Identity, scale=0.5)
+            act("STF", ("XB", 0, 4 * CA), AF.Identity, scale=0.0, bias=1e20)
+            act("NG", ID, AF.Identity, scale=-16.0)
+            act("WW1", ("XB", 0, 4 * BW), AF.Identity, scale=0.0)
+            act("STB", ("XB", 0, 8 * (256 - CA)), AF.Identity, scale=0.0, bias=stamp)
+            dma("s", T.W1[0:128:16, 0:KEYS], T.WW1[:], ["WW1"], ["W1"])
+        for q, (c0, c1) in enumerate(CH):
+            gt(big(Q0, c0, c1), "RT", ("LT", c0, c1), big(S1, c0, c1), OP.mult)
+            act(big(S1, c0, c1), big(Q0, c0, c1), AF.Copy)
+        QO, QA = ("BIG", Q0, Q0 + E), ("BIG", Q0, Q0 + PW)
+        RA = ("BIG", R0, R0 + PW)
+        for q, (c0, c1) in enumerate(CH):
+            gt(big(R0, c0, c1), QO, ("LV", c0, c1), big(S1, c0, c1), OP.subtract)
+            act(big(R0, c0, c1), big(R0, c0, c1), AF.Abs)
+        ms(("BIG", Q0 + P, Q0 + PW), 0.0)
+        ms(("BIG", R0 + P, R0 + PW), 0.0)
+        if r == 0:
+            tt(("KH", 0, 16), "SH", ("DH", 0, 16), OP.subtract)
+        for c0, c1 in CV:
+            gt(big(A0, c0, c1), QA, ("LU", c0, c1), big(S1, c0, c1), OP.subtract)
+            act(big(A0, c0, c1), big(A0, c0, c1), AF.Abs)
+            act(big(A0, c0, c1), big(A0, c0, c1), AF.Identity, bias=MARGIN)
+
+        def sums_out(chunks):
+            for c0, c1 in chunks:
+                gt(sums(c0, c1), "YT", ("LT", c0, c1), sums(c0, c1), OP.add)
+
+        def offsets(bank, c0, c1):
+            ts(("T1", c0, c1), (bank, 0, c1 - c0), 8.5, OP.is_ge)
+            tt(("T1", c0, c1), ("T1", c0, c1), ("KD", c0, c1), OP.mult)
+            tt(("T1", c0, c1), ("T1", c0, c1), ("DUM", c0, c1), OP.add)
+            cp(("LC", c0, c1), ("T1", c0, c1))
+
+        for q, (c0, c1) in enumerate(CV):
+            bank, b0, b1 = ("X0", 0, CA) if q < 2 else ("X1", CA, 256)
+            if q % 2 == 0:
+                mm((bank, 0, b1 - b0), "NG", ("LK", b0, b1), True, False)
+            gt(("P1", 16 * c0, 16 * c1), RA, ("LU", c0, c1), big(A0, c0, c1), OP.is_gt)
+            extract((bank, c0 - b0, c1 - b0), "P1", c0, c1, "ZC", 1, False, q % 2 == 1)
+            if q == 2:
+                offsets("X0", 0, CA)
+        offsets("X1", CA, 256)
+        for k in range(4):
+            c0 = k * CA // 4
+            op("a", lambda c0=c0: g.scalar.activation(T.BIG[:].indirect(T.LC[:, c0:c0 + CA // 4]), T.STF[:], AF.Silu),
+               ["STF", ("LC", c0, c0 + CA // 4)], ["BIG"])
+        dma("a", T.WW2[:], T.BIG[0:128:16, 0:KEYS], ["BIG"], ["WW2"])
+        hw = (256 - CA) // 2
+        for c0 in (CA, CA + hw):
+            op("v", lambda c0=c0: g.vector.tensor_copy(T.W1[:].indirect(T.LC[:, c0:c0 + hw]), T.STB[:]),
+               ["STB", ("LC", c0, c0 + hw)], ["W1"])
+        dma("s", T.WW1[:], T.W1[0:128:16, 0:KEYS], ["W1"], ["WW1"])
+        tt("TP", "LK", upto("TB1"), OP.mult)
+        lin(upto("CG"), [(ID, upto("TN0")), ("IBW", "TP")])
+        ts("TU", "LK", -stamp, OP.mult, stamp, OP.add)
+        ts("SF", ("PT", 0, 16), float(E), OP.add)
+        ts("LP", upto("CG"), 256.0, OP.add)
+        tt(("KH", 16, 32), "SF", ("DH", 16, 32), OP.subtract)
+        cursors_on()
+        if last:
+            sums_out(CH[:2])
+        else:
+            masks("CM")
+        for w, m in (("WW2", "IW"), ("WW1", "IB")):
+            for k in range(4):
+                mm(("CG", 0, 48), (m, 96, 224), w, (w, k) == ("WW2", 0), (w, k) == ("WW1", 3), rap=T[w][:, 1024 + k:1216:4])
+            for k in range(4):
+                mm(("X2", 0, 256), (m, 0, 128), w, (w, k) == ("WW2", 0), (w, k) == ("WW1", 3), rap=T[w][:, k:1024:4])
+        ts("HG", ("CG", 0, 48), thr, OP.is_ge)
+        send([("HG", lambda d: T.RH[:, (3 * r + d - 1) * 48:(3 * r + d) * 48])], "ah%d" % r, "lh%d" % r, -1, [("RH", 144 * r, 144 * r + 144)])
+        if not last:
+            for c0, c1 in CHS:
+                gcopy(big(A0, c0, c1), ("XB", 16 * c0, 16 * c1))
+        ts(upto("TG"), upto("X2"), thr, OP.is_ge, stamp, OP.mult)
+        dma("s", T.P0[0:128:16, :], T.TG[:], ["TG"], ["P0"])
+        mm(upto("X0"), ID, "TU", True, False)
+        mm(upto("X0"), ID, upto("TG"), False, False)
+        if last:
+            sums_out(CH[2:])
+            for c0, c1 in CH:
+                dma("s", T.ys[:, 16 * c0:16 * c1], T.XB[:, 16 * c0:16 * c1], [("XB", 16 * c0, 16 * c1)], [])
+        for c0, c1 in (CH[:3] if last else CH):
+            ga(("P1", 16 * c0, 16 * c1), "P0", ("LP", c0, c1))
+        if not last:
+            select()
+        tt("CM", "CM", "C", OP.subtract)
+        if last:
+            ts("T2", "C", 4.0, OP.mult)
+            ts("T3", "CM", 4.0, OP.mult)
+            gv(("P1", 16 * 192, 16 * 256), "P0", ("LP", 192, 256))
+        else:
+            derive(upto("M0"))
+        b = 144 * r
+        tt("AH", ("RH", b, b + 16), ("RH", b + 64, b + 80), OP.max)
+        tt("AH", "AH", ("RH", b + 128, b + 144), OP.max)
+        tt(("TH", 0, 16), "AH", ("KH", 0, 16), OP.mult)
+        tt(("TH", 16, 32), "AH", ("KH", 16, 32), OP.mult)
+        tt("TH", "TH", "DH", OP.add)
+        cp("LH", "TH")
+        for c0 in (0, 16):
+            op("v", lambda c0=c0: g.vector.tensor_copy(T.H[:].indirect(T.LH[:, c0:c0 + 16]), T.STB[:, 0:256]),
+               ["STB", ("LH", c0, c0 + 16)], ["H"])
+        for q in ((0, 1, 3, 2) if last else (0, 1, 2)):
+            extract(("X0",) + CH[q], "P1", CH[q][0], CH[q][1], start=False, stop=False)
+        extract(upto("X0"), "H", 0, 256, start=False, stop=last)
+        if not last:
+            extract(("X0",) + CH[3], "P1", CH[3][0], CH[3][1], start=False, stop=True)
+        if not last:
+            tt(upto("M0"), upto("M0"), upto("TB0"), OP.subtract)
+            tt(upto("M1"), "J2", upto("TB1"), OP.subtract)
+            derive_other("MD")
+        ts("MV", upto("X0"), thr, OP.is_ge)
+        if last:
+            tt("T3", "T3", "MV", OP.mult)
+            tt("T2", "T2", "T3", OP.add)
+            dma("s", T.yc[:], T.T2[:], ["T2"], [])
+        else:
+            tt(upto("M0"), upto("M0"), "MV", OP.mult)
+            tt(upto("M1"), upto("M1"), "MV", OP.mult)
+            tt(upto("TB0"), upto("TB0"), upto("M0"), OP.add)
+            row_out(0, "TB0")
+            tt(upto("TB1"), upto("TB1"), upto("M1"), OP.add)
+            row_out(1, "TB1")
+            lin(upto("CG"), [(ID, upto("TB0")), ("IBW", upto("TB1"))])
+            act("STB", ("XB", 0, 8 * (256 - CA)), AF.Identity, scale=0.0, bias=STAMP[r + 1])
+            tt("MD", "MD", "DLO", OP.subtract)
+            ts("LB", upto("CG"), 256.0, OP.add)
+            tt("MD", "MD", "MV", OP.mult)
+            tt("DLO", "DLO", "MD", OP.add)
+            tt("CM", "CM", "MV", OP.mult)
+            tt("C", "C", "CM", OP.add)
+
+    for s in total:
+        if max([0] + [waited[k] for k in waited if k[1] == s]) < total[s]:
+            wait("g", (s, total[s]))

@@ -21,7 +21,7 @@ SCRATCH = {
     "CI": ("sbuf", [128, 1024], I), "MB": ("sbuf", [128, 1024], B), "MK": ("sbuf", [128, 1024], F),
     "STB": ("sbuf", [128, 8 * (256 - CA)], B), "STF": ("sbuf", [128, 4 * CA], F),
     "IW": ("sbuf", [128, 256], F), "IB": ("sbuf", [128, 256], B), "SWN": ("sbuf", [128, 128], F),
-    "ZE": ("sbuf", [128, 144], B), "ZC": ("sbuf", [128, 144], B), "M0": ("sbuf", [128, 256], F), "M1": ("sbuf", [128, 256], B), "CO": ("sbuf", [128, 2048], B),
+    "ZE": ("sbuf", [128, 144], B), "ZC": ("sbuf", [128, 144], B), "M0": ("sbuf", [128, 256], F), "M1": ("sbuf", [128, 256], B), "CO": ("sbuf", [128, 2048], B), "ZG": ("sbuf", [128, 144], B), "IN": ("sbuf", [128, 160], F),
     "KT": ("sbuf", [128, 32], F), "RT": ("sbuf", [128, 32], F), "YT": ("sbuf", [128, 32], F),
     "RH": ("sbuf", [128, RO * 3 * 48], B), "HG": ("sbuf", [128, 48], B),
     "COL": ("sbuf", [128, 8], F), "COLI": ("sbuf", [128, 8], I),
@@ -42,7 +42,7 @@ for _n in ("BI", "J1", "J2"):
     SCRATCH[_n] = ("sbuf", [128, 256], I)
 for _n in ("L0", "L1", "L2", "L3", "L4", "LS"):
     SCRATCH[_n] = ("sbuf", [128, 258], U)
-for _n in ("LT", "LB", "LU", "LV", "LP", "LC"):
+for _n in ("LT", "LB", "LU", "LV", "LC"):
     SCRATCH[_n] = ("sbuf", [128, 256], U)
 PSUM = ("X0", "X1", "X2", "X3", "SW", "CG", "PT", "SL")
 for _n in PSUM:
@@ -224,11 +224,13 @@ def rank_program(g, core, T, topo):
         for i in range(4):
             ts(("MB", 256 * i, 256 * i + 256), c, 0.25 * i, OP.is_equal)
 
-    def select():
-        for i in range(4):
+    def select(i0=0, i1=4, products=True, sums=True):
+        for i in range(i0, i1):
             blk = (256 * i, 256 * i + 256)
-            tt(("MK",) + blk, ("MB",) + blk, ("CI",) + blk, OP.mult)
-            mm(SL, IDF, ("MK",) + blk, i == 0, i == 3)
+            if products:
+                tt(("MK",) + blk, ("MB",) + blk, ("CI",) + blk, OP.mult)
+            if sums:
+                mm(SL, IDF, ("MK",) + blk, i == 0, i == 3)
 
     def derive(c0):
         ts("BI", SL, -float(E), OP.add)
@@ -276,7 +278,6 @@ def rank_program(g, core, T, topo):
         ms((n, 256, BW), 0.0)
     tt(("COL", 1, 2), ("COL", 1, 2), ("COL", 0, 1), OP.add)
     ms(("XB", E, ES), 0.0)
-    ms(("BIG", A0 + E, A0 + ES), 0.0)
     act("IW", "IB", AF.Copy)
     act("EW", "IO", AF.Identity, bias=T.COL[:, 0:1], extra=[("COL", 0, 1)])
     act("EN", "EW", AF.Identity, bias=float(E))
@@ -284,6 +285,10 @@ def rank_program(g, core, T, topo):
     act("I16", ID, AF.Identity, scale=16.0)
     act("SW16", "SWB", AF.Identity, scale=16.0)
     act("SWN", "SWB", AF.Identity, scale=-1.0)
+    act("NG", ID, AF.Identity, scale=-16.0)
+    act("STF", ("P0", 0, 4 * CA), AF.Identity, bias=1e20)
+    act("STB", ("P0", 0, 8 * (256 - CA)), AF.Identity, bias=STAMP[0])
+    act("WW1", ("P0", 0, 4 * BW), AF.Copy)
     ts("C", "BI", 0.25, OP.mult)
     masks("C")
     select()
@@ -322,8 +327,19 @@ def rank_program(g, core, T, topo):
 
     CH = [(0, 64), (64, 128), (128, 192), (192, 256)]
     CHS = CH[:3] + [(192, 258)]
-    CV = [(0, CA // 2), (CA // 2, CA), (CA, 224), (224, 256)]
+    CV = [(0, CA // 2), (CA // 2, CA), (CA, 168), (168, 224), (224, 256)]
     BK = ["X0", "X1", "X2", "X3"]
+
+    def keep(q, o, src=None):
+        c0, c1 = CHS[q]
+        a = big(o, c0, c1) if src is None else (src, 16 * c0, 16 * c1)
+        if (q % 2 == 1) == (src is None):
+            gcopy(big(A0, c0, c1), a)
+        else:
+            dma("s", ap(big(A0, c0, c1)), ap(a), [a], [big(A0, c0, c1)])
+
+    for q in range(4):
+        keep(q, 0, "XB")
 
     for r in range(RO):
         last = r == RO - 1
@@ -333,35 +349,68 @@ def rank_program(g, core, T, topo):
         def sums(c0, c1):
             return ("XB", 16 * c0, 16 * c1) if last else big(S0, c0, c1)
 
-        lin(upto("SW"), [("SW16", upto("TB0")), ("SWB", "DLO")])
-        ts("LU", upto("SW"), float(E), OP.add)
-        for q, (c0, c1) in (("a", (0, 72)), ("v", (120, 200)), ("a", (72, 120)), ("v", (200, 256))):
-            deps(q, q, ["P0c1"], [])
-            (ga if q == "a" else gv)(("P1", 16 * c0, 16 * c1), "P0", ("LB", c0, c1))
-            extract(("X0", c0, c1), "P1", c0, c1)
-        ga(upto("PS"), "P0", "SS")
         if r == 0:
-            for o in (0, 1024):
-                for h in range(2):
-                    op("a", lambda h=h, o=o: g.scalar.activation(T.BIG[:, A0 + 2 * o + h:A0 + 2 * o + 2048:2], T.CO[:, o:o + 1024], AF.Identity, bias=-127.5),
-                       ["CO"], [("BIG", A0 + 2 * o, A0 + 2 * o + 2048)])
-        tt("LK", upto("X0"), "EW", OP.is_equal)
-        tt(upto("TN0"), "LK", upto("TB0"), OP.mult)
+            lin(upto("SW"), [("SW16", upto("TB0")), ("SWB", "DLO")])
+            ts("LU", upto("SW"), float(E), OP.add)
+        for q in (3, 0, 1, 2):
+            c0, c1 = CH[q]
+            e = "v" if q >= 2 else "a"
+            deps(e, e, ["P0c1"], [])
+            (gv if q >= 2 else ga)(("P1", 16 * c0, 16 * c1), "P0", ("LB", c0, c1))
+        ga(upto("PS"), "P0", "SS")
+
+        def links(qs):
+            for q in qs:
+                tt(("LK",) + CH[q], (BK[q], 0, 64), ("EW",) + CH[q], OP.is_equal)
+            for q in qs:
+                c0, c1 = CH[q]
+                tt(("TN0", c0, c1), ("LK", c0, c1), ("TB0", c0, c1), OP.mult)
+                tt(("TN1", c0, c1), ("LK", c0, c1), ("DLO", c0, c1), OP.mult)
+                c1 = CHS[q][1]
+                lin((BK[q], 128, 128 + c1 - c0), [("I16", ("TN0", c0, c1)), (ID, ("TN1", c0, c1))])
+
+        def first_list(q):
+            c0, c1 = CHS[q]
+            ts(("L0", c0, c1), (BK[q], 128, 128 + c1 - c0), float(E), OP.add)
+
+        def first(q):
+            c0, c1 = CHS[q]
+            gt(big(S0, c0, c1), "XB", ("L0", c0, c1), big(A0, c0, c1), OP.add)
+            keep(q, S0)
+
+        for q in (3, 0, 1, 2):
+            extract((BK[q], 0, 64), "P1", *CH[q])
+        links((3, 0))
+        links((1, 2))
         row_out(0, "TN0")
-        tt(upto("TN1"), "LK", "DLO", OP.mult)
         row_out(1, "TN1")
-        lin(upto("CG", 258), [("I16", upto("TN0", 258)), (ID, upto("TN1", 258))])
-        lin(upto("X3", 258), [(ID, upto("TN0", 258)), ("IBW", upto("TN1", 258))])
+        lin(upto("CG", 258), [(ID, upto("TN0", 258)), ("IBW", upto("TN1", 258))])
         extract(("PT", 0, 16), "PS", 0, 16)
+        first_list(0)
+        first_list(3)
+        ts("TP", "LK", -1.0, OP.add)
+        first(0)
+        ts("LS", upto("CG", 258), 256.0, OP.add)
+        first_list(1)
+        first_list(2)
+        first(1)
+        first(2)
+        first(3)
         if r == 0:
             act("E1", "IO", AF.Identity, bias=T.COL[:, 1:2], extra=[("COL", 1, 2)])
             act(("DUM", 0, CA), ("EW", 0, CA), AF.Identity, bias=float(E + KEYS))
             act(("DUM", CA, 256), ("EW", CA, 256), AF.Identity, bias=float(E + KEYS - 16 * CA))
             act("DH", ("EW", 0, 32), AF.Identity, bias=float(2 * E))
             act("DQ", "DUM", AF.Identity, scale=-0.25, bias=256.0)
-        ts("L0", upto("CG", 258), float(E), OP.add)
-        ts("LS", upto("X3", 258), 256.0, OP.add)
+        tt("T1", "TP", "E1", OP.mult)
         deps("a", "a", ["P0c1"], [])
+        def offs(s, q):
+            c0, c1 = CHS[q] if s < 5 else CH[q]
+            if s < 5:
+                ts(("L%d" % s, c0, c1), (BK[q], 0, c1 - c0), float(E), OP.add)
+            else:
+                ts(("LT", c0, c1), (BK[q], 0, c1 - c0), 0.0, OP.max)
+
         for s in range(1, 6):
             src = ("XB", 0) if s == 1 else ("BIG", S0 if s % 2 == 0 else S1)
             dst = S0 if s % 2 == 1 else S1
@@ -369,57 +418,68 @@ def rank_program(g, core, T, topo):
             lst = "L%d" % (s - 1)
             for q, (c0, c1) in enumerate(CHS if s < 5 else CH):
                 if s > 1:
-                    ts((lst, c0, CHS[q][1]), (BK[q], 0, CHS[q][1] - c0), float(E), OP.add)
-                gt(big(dst, c0, c1) if s < 5 else sums(c0, c1), (src[0], src[1], src[1] + ES), (lst, c0, c1), big(A0, c0, c1), OP.add)
-                if s < 5:
-                    if q % 2:
-                        gcopy(big(A0, c0, c1), big(dst, c0, c1))
-                    else:
-                        dma("s", ap(big(A0, c0, c1)), ap(big(dst, c0, c1)), [big(dst, c0, c1)], [big(A0, c0, c1)])
+                    if (s, q) == (2, 0):
+                        offs(1, 0)
+                    offs(s - 1, q + 1) if q < 3 else offs(s, 0)
+                    gt(big(dst, c0, c1) if s < 5 else sums(c0, c1), (src[0], src[1], src[1] + ES), (lst, c0, c1), big(A0, c0, c1), OP.add)
+                    if s < 5:
+                        keep(q, dst)
                 ga((pout, 16 * c0, 16 * c1), (pin, 0, PB if s == 1 else ES), ("LS" if s == 1 else lst, c0, c1))
                 extract((BK[q], 0, c1 - c0), pout, c0, c1)
+                if (s, q) == (2, 0):
+                    extract(("PT", 32, 48), "PS", 0, 16)
+                if (s, q) == (2, 1):
+                    lin(("SW", 0, 256), [("SW16", upto("TN0")), ("SWB", upto("TN1")), ("SWN", "T1")])
+                if (s, q) == (2, 2):
+                    lin(SL, [(ID, upto("TB0")), ("IBW", upto("TB1")), (ID, "C"), (IDF, "DQ")])
             if s == 1:
-                tt("T1", "LK", "E1", OP.mult)
                 ga(upto("PS"), "P0", "SS2")
-                extract(("PT", 32, 48), "PS", 0, 16)
-            if s == 2:
-                lin(("SW", 0, 256), [("SW16", upto("TN0")), ("SWB", upto("TN1")), ("SWN", "T1"), (IDF, "EW")])
-                lin(SL, [(ID, upto("TB0")), ("IBW", upto("TB1")), (ID, "C"), (IDF, "DQ")])
             if s == 3:
+                ts("SF", ("PT", 32, 48), 0.0, OP.is_ge)
+                ts("SG", ("PT", 32, 48), float(E), OP.add)
+                tt("SF", "SF", "SUM", OP.mult)
                 ts("LV", upto("SW"), float(E), OP.add)
-                ts("SF", ("PT", 32, 48), 0.0, OP.is_lt)
-                tt("SG", ("PT", 32, 48), "SUM", OP.subtract)
-                tt("SG", "SG", "SF", OP.mult)
-                tt("SG", "SG", "SUM", OP.add)
-                ts(("LW", 16, 32), "SG", float(E), OP.add)
+                tt("SG", "SG", "SF", OP.add)
+            if s == 4:
+                cp(("LW", 16, 32), "SG")
         ga("PS", ("P1", 0, E), "LW")
         extract(("CG", 0, 32), "PS", 0, 32)
         ga("PG", sums(0, 256), "LW")
         act("KD", SL, AF.Identity, scale=4.0)
         if r == 0:
             act("RT", "RT", AF.Identity, scale=2.0 ** -17)
-        for q, (c0, c1) in enumerate(CH):
-            ts(("LT", c0, c1), (BK[q], 0, c1 - c0), 0.0, OP.max)
+            act("IN", ("IW", 0, 160), AF.Identity, scale=-1.0)
+        def scaled(c0, c1):
             gt(big(S1, c0, c1), "KT", ("LT", c0, c1), sums(c0, c1), OP.mult)
-            if q != 1:
-                continue
-            ts("LX", ("CG", 0, 32), 0.0, OP.max)
-            gt("PH", "KT", "LX", "PG", OP.mult)
-            gt("PG", "RT", "LX", "PH", OP.mult)
-            lin(upto("SW"), [(("IW", 32, 160), upto("PG"))])
-            tt(upto("PH"), ("PG", 256, 512), upto("PG"), OP.subtract)
-            act(upto("PAY"), upto("SW"), AF.Copy)
-            send([(upto("PAY"), lambda d: T.BIG[:, Q0 + E + GH * (d - 1):Q0 + E + GH * d])], "ac%d" % r, "lc%d" % r, 1, [("BIG", Q0 + E, Q0 + P)])
-            lin(upto("CG"), [(("IW", 32, 160), upto("PH"))])
-            act(("PAY", 256, 512), upto("CG"), AF.Abs)
-            send([(("PAY", 256, 512), lambda d: T.BIG[:, R0 + E + GH * (d - 1):R0 + E + GH * d])], "ar%d" % r, "lr%d" % r, 1, [("BIG", R0 + E, R0 + P)])
+
+        offs(5, 1)
+        scaled(0, 64)
+        offs(5, 2)
+        scaled(64, 112)
+        ts("LX", ("CG", 0, 32), 0.0, OP.max)
+        offs(5, 3)
+        scaled(112, 128)
+        gt("PH", "KT", "LX", "PG", OP.mult)
+        scaled(128, 144)
+        gt("PG", "RT", "LX", "PH", OP.mult)
+        lin(upto("SW"), [(("IW", 32, 160), upto("PG"))])
+        act(upto("PAY"), upto("SW"), AF.Copy)
+        send([(upto("PAY"), lambda d: T.BIG[:, Q0 + E + GH * (d - 1):Q0 + E + GH * d])], "ac%d" % r, "lc%d" % r, 1, [("BIG", Q0 + E, Q0 + P)])
+        lin(upto("CG"), [(("IW", 32, 160), ("PG", 256, 512)), (("IN", 32, 160), upto("PG"))])
+        act(("PAY", 256, 512), upto("CG"), AF.Abs)
+        send([(("PAY", 256, 512), lambda d: T.BIG[:, R0 + E + GH * (d - 1):R0 + E + GH * d])], "ar%d" % r, "lr%d" % r, 1, [("BIG", R0 + E, R0 + P)])
+        scaled(144, 256)
+        for o in (Q0, R0):
+            gi(("BIG", o + P, o + PW), T.BIG[:, o + P:o + PW], [[0, PW - P]], 0, 0)
         if r == 0:
+            gi("ZG", T.ZG[:], [[0, 144]], 0, 0)
+            gs("ZG", T.ZG[:, 0:144:16], "ZG", T.ZG[:, 0:144:16], [[-16, 9]], OP.not_equal, 1.0, 48, 1)
+            gs("ZG", T.ZG[:, 0:144:16], "ZG", T.ZG[:, 0:144:16], [[-16, 9]], OP.not_equal, 1.0, -80, 1)
+            for i in range(16):
+                o = 4 * BW * i + 1024
+                gi(("W1", o, o + 192), T.W1[:, o:o + 192], [[0, 192]], 0, 0)
             gi("H", T.H[:], [[0, E + 2 * GH]], 0, 0)
             act("YT", "YT", AF.Identity, scale=0.5)
-            act("STF", ("XB", 0, 4 * CA), AF.Identity, scale=0.0, bias=1e20)
-            act("NG", ID, AF.Identity, scale=-16.0)
-            act("WW1", ("XB", 0, 4 * BW), AF.Identity, scale=0.0)
-            act("STB", ("XB", 0, 8 * (256 - CA)), AF.Identity, scale=0.0, bias=stamp)
             dma("s", T.W1[0:128:16, 0:KEYS], T.WW1[:], ["WW1"], ["W1"])
         for q, (c0, c1) in enumerate(CH):
             gt(big(Q0, c0, c1), "RT", ("LT", c0, c1), big(S1, c0, c1), OP.mult)
@@ -429,8 +489,6 @@ def rank_program(g, core, T, topo):
         for q, (c0, c1) in enumerate(CH):
             gt(big(R0, c0, c1), QO, ("LV", c0, c1), big(S1, c0, c1), OP.subtract)
             act(big(R0, c0, c1), big(R0, c0, c1), AF.Abs)
-        ms(("BIG", Q0 + P, Q0 + PW), 0.0)
-        ms(("BIG", R0 + P, R0 + PW), 0.0)
         if r == 0:
             tt(("KH", 0, 16), "SH", ("DH", 0, 16), OP.subtract)
         for c0, c1 in CV:
@@ -443,17 +501,21 @@ def rank_program(g, core, T, topo):
                 gt(sums(c0, c1), "YT", ("LT", c0, c1), sums(c0, c1), OP.add)
 
         def offsets(bank, c0, c1):
+            halves = ((c0, (c0 + c1) // 2), ((c0 + c1) // 2, c1))
             ts(("T1", c0, c1), (bank, 0, c1 - c0), 8.5, OP.is_ge)
-            tt(("T1", c0, c1), ("T1", c0, c1), ("KD", c0, c1), OP.mult)
-            tt(("T1", c0, c1), ("T1", c0, c1), ("DUM", c0, c1), OP.add)
-            cp(("LC", c0, c1), ("T1", c0, c1))
+            for h in halves:
+                tt(("T1",) + h, ("T1",) + h, ("KD",) + h, OP.mult)
+            for h in halves:
+                tt(("T1",) + h, ("T1",) + h, ("DUM",) + h, OP.add)
+            for h in halves:
+                cp(("LC",) + h, ("T1",) + h)
 
         for q, (c0, c1) in enumerate(CV):
             bank, b0, b1 = ("X0", 0, CA) if q < 2 else ("X1", CA, 256)
-            if q % 2 == 0:
+            if q in (0, 2):
                 mm((bank, 0, b1 - b0), "NG", ("LK", b0, b1), True, False)
             gt(("P1", 16 * c0, 16 * c1), RA, ("LU", c0, c1), big(A0, c0, c1), OP.is_gt)
-            extract((bank, c0 - b0, c1 - b0), "P1", c0, c1, "ZC", 1, False, q % 2 == 1)
+            extract((bank, c0 - b0, c1 - b0), "P1", c0, c1, "ZC", 1, False, q in (1, 4))
             if q == 2:
                 offsets("X0", 0, CA)
         offsets("X1", CA, 256)
@@ -467,45 +529,50 @@ def rank_program(g, core, T, topo):
             op("v", lambda c0=c0: g.vector.tensor_copy(T.W1[:].indirect(T.LC[:, c0:c0 + hw]), T.STB[:]),
                ["STB", ("LC", c0, c0 + hw)], ["W1"])
         dma("s", T.WW1[:], T.W1[0:128:16, 0:KEYS], ["W1"], ["WW1"])
-        tt("TP", "LK", upto("TB1"), OP.mult)
-        lin(upto("CG"), [(ID, upto("TN0")), ("IBW", "TP")])
-        ts("TU", "LK", -stamp, OP.mult, stamp, OP.add)
+        act("TU", "LK", AF.Identity, scale=-stamp, bias=stamp)
+        for i in range(16):
+            for k in range(4):
+                o = 4 * BW * i + 1024
+                mm(("CG", 0, 48), ("ZG", 16 - i, 144 - i), "W1", i + k == 0, False, rap=T.W1[:, o + k:o + 192:4])
+        for k in range(4):
+            mm(("CG", 0, 48), ("IW", 96, 224), "WW2", False, k == 3, rap=T.WW2[:, 1024 + k:1216:4])
         ts("SF", ("PT", 0, 16), float(E), OP.add)
-        ts("LP", upto("CG"), 256.0, OP.add)
-        tt(("KH", 16, 32), "SF", ("DH", 16, 32), OP.subtract)
         cursors_on()
+        tt(("KH", 16, 32), "SF", ("DH", 16, 32), OP.subtract)
         if last:
-            sums_out(CH[:2])
-        else:
-            masks("CM")
-        for w, m in (("WW2", "IW"), ("WW1", "IB")):
-            for k in range(4):
-                mm(("CG", 0, 48), (m, 96, 224), w, (w, k) == ("WW2", 0), (w, k) == ("WW1", 3), rap=T[w][:, 1024 + k:1216:4])
-            for k in range(4):
-                mm(("X2", 0, 256), (m, 0, 128), w, (w, k) == ("WW2", 0), (w, k) == ("WW1", 3), rap=T[w][:, k:1024:4])
-        ts("HG", ("CG", 0, 48), thr, OP.is_ge)
-        send([("HG", lambda d: T.RH[:, (3 * r + d - 1) * 48:(3 * r + d) * 48])], "ah%d" % r, "lh%d" % r, -1, [("RH", 144 * r, 144 * r + 144)])
-        if not last:
-            for c0, c1 in CHS:
-                gcopy(big(A0, c0, c1), ("XB", 16 * c0, 16 * c1))
-        ts(upto("TG"), upto("X2"), thr, OP.is_ge, stamp, OP.mult)
-        dma("s", T.P0[0:128:16, :], T.TG[:], ["TG"], ["P0"])
-        mm(upto("X0"), ID, "TU", True, False)
-        mm(upto("X0"), ID, upto("TG"), False, False)
-        if last:
-            sums_out(CH[2:])
-            for c0, c1 in CH:
-                dma("s", T.ys[:, 16 * c0:16 * c1], T.XB[:, 16 * c0:16 * c1], [("XB", 16 * c0, 16 * c1)], [])
-        for c0, c1 in (CH[:3] if last else CH):
-            ga(("P1", 16 * c0, 16 * c1), "P0", ("LP", c0, c1))
-        if not last:
-            select()
-        tt("CM", "CM", "C", OP.subtract)
-        if last:
+            tt("CM", "CM", "C", OP.subtract)
             ts("T2", "C", 4.0, OP.mult)
             ts("T3", "CM", 4.0, OP.mult)
-            gv(("P1", 16 * 192, 16 * 256), "P0", ("LP", 192, 256))
         else:
+            masks("CM")
+        ts("HG", ("CG", 0, 48), thr, OP.is_ge)
+        send([("HG", lambda d: T.RH[:, (3 * r + d - 1) * 48:(3 * r + d) * 48])], "ah%d" % r, "lh%d" % r, -1, [("RH", 144 * r, 144 * r + 144)])
+        if last:
+            sums_out(CH[:1])
+        else:
+            select(0, 2, sums=False)
+        act(upto("P1", 1024), upto("WW2", 1024), AF.Copy)
+        for w in ("P1", "WW1"):
+            for k in range(4):
+                mm(("X2", 0, 256), "SWB", upto(w, 1024), (w, k) == ("P1", 0), (w, k) == ("WW1", 3), rap=T[w][:, k:1024:4])
+        if not last:
+            select(0, 2, products=False)
+            for q in range(4):
+                gcopy(big(A0, *CHS[q]), ("XB", 16 * CHS[q][0], 16 * CHS[q][1]))
+        ts(upto("TG"), upto("X2"), thr, OP.is_ge, stamp, OP.mult)
+        dma("s", T.P0[0:128:16, :], T.TG[:], ["TG"], ["P0"])
+        if not last:
+            select(2, 4)
+        mm(upto("X0"), ID, "TU", True, False)
+        mm(upto("X0"), "SWB", upto("TG"), False, False)
+        if last:
+            sums_out(CH[1:])
+            for c0, c1 in CH:
+                dma("s", T.ys[:, 16 * c0:16 * c1], T.XB[:, 16 * c0:16 * c1], [("XB", 16 * c0, 16 * c1)], [])
+        for c0, c1 in CH:
+            ga(("P1", 16 * c0, 16 * c1), "P0", ("LS", c0, c1))
+        if not last:
+            tt("CM", "CM", "C", OP.subtract)
             derive(upto("M0"))
         b = 144 * r
         tt("AH", ("RH", b, b + 16), ("RH", b + 64, b + 80), OP.max)
@@ -517,15 +584,15 @@ def rank_program(g, core, T, topo):
         for c0 in (0, 16):
             op("v", lambda c0=c0: g.vector.tensor_copy(T.H[:].indirect(T.LH[:, c0:c0 + 16]), T.STB[:, 0:256]),
                ["STB", ("LH", c0, c0 + 16)], ["H"])
-        for q in ((0, 1, 3, 2) if last else (0, 1, 2)):
-            extract(("X0",) + CH[q], "P1", CH[q][0], CH[q][1], start=False, stop=False)
-        extract(upto("X0"), "H", 0, 256, start=False, stop=last)
-        if not last:
-            extract(("X0",) + CH[3], "P1", CH[3][0], CH[3][1], start=False, stop=True)
+        extract(("X0", 0, 128), "P1", 0, 128, start=False, stop=False)
+        extract(upto("X0"), "H", 0, 256, start=False, stop=False)
+        for q in (2, 3):
+            extract(("X0",) + CH[q], "P1", CH[q][0], CH[q][1], start=False, stop=q == 3)
         if not last:
             tt(upto("M0"), upto("M0"), upto("TB0"), OP.subtract)
             tt(upto("M1"), "J2", upto("TB1"), OP.subtract)
             derive_other("MD")
+            tt("MD", "MD", "DLO", OP.subtract)
         ts("MV", upto("X0"), thr, OP.is_ge)
         if last:
             tt("T3", "T3", "MV", OP.mult)
@@ -540,12 +607,13 @@ def rank_program(g, core, T, topo):
             row_out(1, "TB1")
             lin(upto("CG"), [(ID, upto("TB0")), ("IBW", upto("TB1"))])
             act("STB", ("XB", 0, 8 * (256 - CA)), AF.Identity, scale=0.0, bias=STAMP[r + 1])
-            tt("MD", "MD", "DLO", OP.subtract)
-            ts("LB", upto("CG"), 256.0, OP.add)
             tt("MD", "MD", "MV", OP.mult)
+            ts("LB", upto("CG"), 256.0, OP.add)
             tt("DLO", "DLO", "MD", OP.add)
             tt("CM", "CM", "MV", OP.mult)
+            lin(upto("SW"), [("SW16", upto("TB0")), ("SWB", "DLO")])
             tt("C", "C", "CM", OP.add)
+            ts("LU", upto("SW"), float(E), OP.add)
 
     for s in total:
         if max([0] + [waited[k] for k in waited if k[1] == s]) < total[s]:

@@ -2,47 +2,62 @@ from concourse.bass import DstId, RemoteDMATransfer
 from concourse.mybir import AluOpType as OP, ActivationFunctionType as AF
 
 E, GH, P, RO, N = 4096, 256, 4864, 3, 4
-BW = P // 16 + 2
-PB = 16 * BW
-PW = P + 16
+BW = P // 16
 ES = E + 32
-KEYS = 4 * PB
-CA = 112
-S0, S1, Q0, R0, A0, BIGW = 0, ES, 2 * ES, 2 * ES + PW, 2 * ES + 2 * PW, 3 * ES + 2 * PW
-MARGIN = 2.4
+G0 = 4 * (P - E)
+KEYS = G0 + 4 * E
+CA = 136
+S0, S1, Q0, R0, A0, BIGW = 0, ES, 2 * ES, 2 * ES + P, 2 * ES + 2 * P, 3 * ES + 2 * P
+SCALE10 = 168199201
+MARGIN = 2.2
+K = 65536.0
 STAMP = (1e10, 1e14, 1e18)
-NDMA = 70
+NDMA = 80
+ALL = 0xFFFF
+CH = [(0, 64), (64, 128), (128, 192), (192, 256)]
+CHS = CH[:3] + [(192, 258)]
+HALF = [(0, 128), (128, 256)]
+C1 = [(0, 16), (16, 80), (80, 144), (144, 208), (208, 240), (240, 256)]
+C2 = [(0, 32), (32, 80), (80, CA), (CA, 192), (192, 240), (240, 256)]
+SHARE_A, SHARE_H = 32, 32
 
 F, B, I, U = "float32", "bfloat16", "int32", "uint16"
 SCRATCH = {
     "BIG": ("sbuf", [128, BIGW], F), "W1": ("sbuf", [128, KEYS + 16 * (256 - CA)], B), "XB": ("sbuf", [128, ES], F),
-    "P0": ("sbuf", [128, PB], B), "P1": ("sbuf", [128, ES], B), "H": ("sbuf", [128, E + 2 * GH], B),
-    "WW1": ("sbuf", [128, 4 * BW], B), "WW2": ("sbuf", [128, 4 * BW], F),
-    "CI": ("sbuf", [128, 1024], I), "MB": ("sbuf", [128, 1024], B), "MK": ("sbuf", [128, 1024], F),
+    "XC": ("sbuf", [128, ES], B), "P0": ("sbuf", [128, 2 * P], B), "P1": ("sbuf", [128, ES], B),
+    "WG1": ("sbuf", [128, 192], B), "WG2": ("sbuf", [128, 192], F),
+    "CI": ("sbuf", [128, 1024], I), "MK": ("sbuf", [128, 1024], F), "CO": ("sbuf", [128, 2048], B),
     "STB": ("sbuf", [128, 8 * (256 - CA)], B), "STF": ("sbuf", [128, 4 * CA], F),
-    "IW": ("sbuf", [128, 256], F), "IB": ("sbuf", [128, 256], B), "SWN": ("sbuf", [128, 128], F),
-    "ZE": ("sbuf", [128, 144], B), "ZC": ("sbuf", [128, 144], B), "M0": ("sbuf", [128, 256], F), "M1": ("sbuf", [128, 256], B), "CO": ("sbuf", [128, 2048], B), "ZG": ("sbuf", [128, 144], B), "IN": ("sbuf", [128, 160], F),
-    "KT": ("sbuf", [128, 32], F), "RT": ("sbuf", [128, 32], F), "YT": ("sbuf", [128, 32], F),
+    "IW": ("sbuf", [128, 256], F), "IB": ("sbuf", [128, 256], B), "SWN": ("sbuf", [128, 128], F), "IN": ("sbuf", [128, 160], F),
+    "RT": ("sbuf", [128, 32], F), "YT": ("sbuf", [128, 32], F),
     "RH": ("sbuf", [128, RO * 3 * 48], B), "HG": ("sbuf", [128, 48], B),
     "COL": ("sbuf", [128, 8], F), "COLI": ("sbuf", [128, 8], I),
-    "SH": ("sbuf", [128, 16], I), "SA": ("sbuf", [128, 16], I), "SB": ("sbuf", [128, 16], I), "SF": ("sbuf", [128, 16], F), "SG": ("sbuf", [128, 16], F),
-    "SUM": ("sbuf", [128, 16], F), "SS2": ("sbuf", [128, 16], U), "LW": ("sbuf", [128, 32], U), "LX": ("sbuf", [128, 32], U),
-    "PS": ("sbuf", [128, 512], B), "PG": ("sbuf", [128, 512], F), "PH": ("sbuf", [128, 512], F), "PAY": ("sbuf", [128, 512], F), "SS": ("sbuf", [128, 16], U), "KH": ("sbuf", [128, 32], F), "DH": ("sbuf", [128, 32], F),
-    "TH": ("sbuf", [128, 32], F), "LH": ("sbuf", [128, 32], U), "AH": ("sbuf", [128, 16], B),
+    "LW": ("sbuf", [128, 32], U), "LX": ("sbuf", [128, 32], U), "LY": ("sbuf", [128, 32], U), "LH": ("sbuf", [128, 32], U), "SS": ("sbuf", [128, 16], U),
+    "PS": ("sbuf", [128, 512], B), "PG": ("sbuf", [128, 512], F), "PH": ("sbuf", [128, 512], F), "PAY": ("sbuf", [128, 512], F),
+    "KH": ("sbuf", [128, 32], F), "DH": ("sbuf", [128, 32], F), "TH": ("sbuf", [128, 32], F),
 }
-for _n in ("NG", "CB", "I16", "IBW", "SWB", "SW16"):
+for _n in ("SH", "SA", "SB"):
+    SCRATCH[_n] = ("sbuf", [128, 16], I)
+for _n in ("SF", "SG", "SUM"):
+    SCRATCH[_n] = ("sbuf", [128, 16], F)
+for _n in ("ZE", "ZA", "ZG", "ZC", "ZH"):
+    SCRATCH[_n] = ("sbuf", [128, 144], B)
+DIAG = {"I16": 16.0, "IBW": float(BW), "IK": K, "IP": -float(P), "IA": 4.0 * E, "IC": 4.0 * E - 192.0, "ID15": 15.0, "ID191": -191.0, "IM": -1.0}
+for _n in ("CB", "SWB", "SW16") + tuple(DIAG):
     SCRATCH[_n] = ("sbuf", [128, 128], B)
-for _n in ("TB0", "TB1", "TN0", "TN1", "TG"):
+for _n in ("TN0", "TN1", "AL0", "AL1", "NMV", "NGT", "ON"):
     SCRATCH[_n] = ("sbuf", [128, BW], B)
-for _n in ("LK", "TU", "MV", "MD", "DLO", "TP", "C", "CM"):
+for _n in ("TB0", "DLO", "LK"):
+    SCRATCH[_n] = ("sbuf", [128, 264], B)
+for _n in ("TU", "C", "DC", "ALO", "SELF", "D1", "GT", "SN"):
     SCRATCH[_n] = ("sbuf", [128, 256], B)
-for _n in ("EW", "EN", "E1", "DUM", "DQ", "KD", "T1", "T2", "T3", "IO"):
+for _n in ("EW", "EN", "D0", "DUM", "KEY", "T1", "T2", "T3"):
     SCRATCH[_n] = ("sbuf", [128, 256], F)
 for _n in ("BI", "J1", "J2"):
     SCRATCH[_n] = ("sbuf", [128, 256], I)
 for _n in ("L0", "L1", "L2", "L3", "L4", "LS"):
     SCRATCH[_n] = ("sbuf", [128, 258], U)
-for _n in ("LT", "LB", "LU", "LV", "LC"):
+for _n in ("LT", "LB", "LU", "LC"):
     SCRATCH[_n] = ("sbuf", [128, 256], U)
 PSUM = ("X0", "X1", "X2", "X3", "SW", "CG", "PT", "SL")
 for _n in PSUM:
@@ -51,17 +66,13 @@ SEMAPHORES = ["cv", "ca", "cp", "cg"] + ["d%d" % i for i in range(NDMA)] + \
     ["%s%d" % (k, r) for k in ("ac", "ar", "ah", "lc", "lr", "lh") for r in range(RO)]
 
 
-def mean_tables():
+def mean_table():
     out = {}
     for m in range(1, 33):
-        best = None
-        for k in range(1024 // m + 1, 2048 // m + 1):
-            mk = m * k
-            r = (2 ** 35 + mk) // (2 * mk)
-            err = abs(r * mk - 2 ** 34)
-            if r < 2 ** 24 and (best is None or err < best[0]):
-                best = (err, k, r)
-        out[m] = best[1:]
+        e = 0
+        while SCALE10 * 2 ** e < 2 ** 23 * 1280 * m:
+            e += 1
+        out[m] = ((2 * SCALE10 * 2 ** e + 1280 * m) // (2 * 1280 * m), e)
     return out
 
 
@@ -75,10 +86,10 @@ def rank_program(g, core, T, topo):
 
     def span(x):
         if isinstance(x, str):
-            return x, 0, SCRATCH[x][1][1] if x in SCRATCH else PB
+            x = (x, 0, SCRATCH[x][1][1])
         if x[0] in PSUM:
-            return x[0], 0, 512
-        return x
+            return x[0], 0, 512, ALL
+        return x if len(x) == 4 else x + (ALL,)
 
     def wait(q, ev):
         s, v = ev
@@ -88,19 +99,19 @@ def rank_program(g, core, T, topo):
 
     def note(ev, src, R, W):
         for x in R:
-            n, lo, hi = span(x)
-            rec.setdefault(n, []).append((lo, hi, ev, False, src))
+            n, lo, hi, ch = span(x)
+            rec.setdefault(n, []).append((lo, hi, ev, False, src, ch))
         for x in W:
-            n, lo, hi = span(x)
-            rec[n] = [r for r in rec.get(n, []) if not (lo <= r[0] and r[1] <= hi)] + [(lo, hi, ev, True, src)]
+            n, lo, hi, ch = span(x)
+            rec[n] = [r for r in rec.get(n, []) if not (lo <= r[0] and r[1] <= hi and r[5] & ch == r[5])] + [(lo, hi, ev, True, src, ch)]
         total[ev[0]] = max(total.get(ev[0], 0), ev[1])
 
     def deps(q, src, R, W):
         need = {}
         for x, wr in [(x, False) for x in R] + [(x, True) for x in W]:
-            n, lo, hi = span(x)
+            n, lo, hi, ch = span(x)
             for r in rec.get(n, []):
-                if r[0] < hi and lo < r[1] and (wr or r[3]):
+                if r[0] < hi and lo < r[1] and r[5] & ch and (wr or r[3]):
                     if r[4] == src and src == "p":
                         continue
                     need[r[2][0]] = max(need.get(r[2][0], 0), r[2][1])
@@ -130,22 +141,19 @@ def rank_program(g, core, T, topo):
     engs = [e for e in reach[0] if all(e in x for x in reach)]
     ne = len(engs)
 
-    def send(parts, arr, loc, step, land):
-        srcs = [p[0] for p in parts]
-        deps("g", loc, srcs, [])
+    def send(src, dst_of, arr, loc, step, land, freed=()):
+        deps("g", loc, [src], list(freed))
         ids = []
         for d in range(1, N):
             rid, pid = topo.addr(T.cores[(rank + step * d) % N])[:2]
             ids.append(DstId(rid=rid, pnc=pid))
-        share = ne // len(parts)
-        g.remote_dma_fused([RemoteDMATransfer(dst_ids=ids, dma_engine_mask=sum(1 << e for e in engs[k * share:(k + 1) * share]),
-                                              remote_sem=T.sem[arr], src=ap(src), dsts=[dst_of(d) for d in range(1, N)])
-                            for k, (src, dst_of) in enumerate(parts)], local_sem=T.sem[loc])
-        note((loc, ne), loc, srcs, [])
+        g.remote_dma_fused([RemoteDMATransfer(dst_ids=ids, dma_engine_mask=sum(1 << e for e in engs), remote_sem=T.sem[arr],
+                                              src=ap(src), dsts=[dst_of(d) for d in range(1, N)])], local_sem=T.sem[loc])
+        note((loc, ne), loc, [src], [])
         note((arr, ne * (N - 1)), arr, [], land)
 
     def ap(x):
-        n, lo, hi = (x, 0, SCRATCH[x][1][1]) if isinstance(x, str) else x
+        n, lo, hi = (x, 0, SCRATCH[x][1][1]) if isinstance(x, str) else x[:3]
         return T[n][:, lo:hi]
 
     def ts(out, a, s1, o0, s2=None, o1=None):
@@ -172,8 +180,11 @@ def rank_program(g, core, T, topo):
     def gv(out, win, lst):
         op("v", lambda: g.vector.tensor_copy(ap(out), ap(win).indirect(ap(lst))), [win, lst], [out])
 
-    def ga(out, win, lst, func=AF.Copy):
-        op("a", lambda: g.scalar.activation(ap(out), ap(win).indirect(ap(lst)), func), [win, lst], [out])
+    def ga(out, win, lst):
+        op("a", lambda: g.scalar.activation(ap(out), ap(win).indirect(ap(lst)), AF.Copy), [win, lst], [out])
+
+    def put(win, lst, src):
+        op("v", lambda: g.vector.tensor_copy(ap(win).indirect(ap(lst)), ap(src)), [src, lst], [win])
 
     def mm(out, lhs, rhs, start, stop, rap=None):
         r = ap(rhs) if rap is None else rap
@@ -201,145 +212,169 @@ def rank_program(g, core, T, topo):
     def gcopy(out, a):
         gs(out, ap(out), a, ap(a), [[0, out[2] - out[1]]], OP.is_ge, 0.0, 0, 0)
 
+    def picker(Z, weights):
+        gi(Z, T[Z][:], [[0, 144]], 0, 0)
+        for ch in weights:
+            gs(Z, T[Z][:, 0:144:16], Z, T[Z][:, 0:144:16], [[-16, 9]], OP.not_equal, weights[ch], 16 - ch, 1)
+
     def big(o, c0, c1):
         return ("BIG", o + 16 * c0, o + 16 * c1)
 
     def upto(n, k=256):
         return (n, 0, k)
 
-    def row_out(ch, tile):
-        if ch == 0:
-            rec["P0c1"] = list(rec["P0"])
-        dma("s", T.P0[ch:128:16, :], T[tile][:], [tile], ["P0c1" if ch else "P0"])
+    def row_out(q, region, ch, tile):
+        dma(q, T.P0[ch:128:16, region * P:(region + 1) * P], T[tile][:], [tile], [("P0", region * P, (region + 1) * P, 1 << ch)])
 
     ID, IDF = ("IB", 0, 128), ("IW", 0, 128)
     SL = ("SL", 0, 256)
-
-    def cursors_on():
-        ts("T1", "C", 0.25, OP.add)
-        ts("T2", "C", 0.75, OP.is_lt)
-        tt("CM", "T1", "T2", OP.mult)
-
-    def masks(c):
-        for i in range(4):
-            ts(("MB", 256 * i, 256 * i + 256), c, 0.25 * i, OP.is_equal)
-
-    def select(i0=0, i1=4, products=True, sums=True):
-        for i in range(i0, i1):
-            blk = (256 * i, 256 * i + 256)
-            if products:
-                tt(("MK",) + blk, ("MB",) + blk, ("CI",) + blk, OP.mult)
-            if sums:
-                mm(SL, IDF, ("MK",) + blk, i == 0, i == 3)
-
-    def derive(c0):
-        ts("BI", SL, -float(E), OP.add)
-        tt("T1", SL, "EN", OP.not_equal)
-        ts("J1", "BI", 4, OP.arith_shift_right)
-        ts("T2", "T1", -48.0, OP.mult, 48.0, OP.add)
-        tt("T3", "J1", "T1", OP.mult)
-        ts("J2", "BI", 15, OP.bitwise_and)
-        tt(c0, "T3", "T2", OP.add)
-
-    def derive_other(out):
-        ts("J1", "BI", 1, OP.bitwise_and)
-        ts("T1", "J1", -2.0, OP.mult, 1.0, OP.add)
-        tt(out, "T1", "J2", OP.add)
-
-    dma("s", T.BI[:], T.cur0[:], [], ["BI"])
-    dma("a", T.CI[:, 0:512], T.cand[:, 0:512], [], [("CI", 0, 512)])
-    dma("s", T.CI[:, 512:1024], T.cand[:, 512:1024], [], [("CI", 512, 1024)])
-    dma("s", T.CO[:], T.cov[:], [], ["CO"])
-    dma("s", T.SH[:], T.shown[:], [], ["SH"])
-    gi(("COLI", 0, 1), T.COLI[:, 0:1], [[0, 1]], 0, 1, False)
-    gi("CB", T.CB[:], [[0, 128]], 1, 0)
-    gs(("IB", 0, 128), T.IB[:, 0:128], "CB", T.CB[:], [[-1, 128]], OP.is_equal, 0.0, 0, 1)
-    gs(("IB", 128, 256), T.IB[:, 128:256], "CB", T.CB[:], [[-1, 128]], OP.is_equal, 0.0, 0, 1)
-    gi("IO", T.IO[:], [[16, 256]], -E, 0)
-    gs("SWB", T.SWB[:, 0:128:2], "CB", T.CB[:, 0:64], [[-2, 64]], OP.is_equal, 0.0, -1, 1)
-    gs("SWB", T.SWB[:, 1:128:2], "CB", T.CB[:, 0:64], [[-2, 64]], OP.is_equal, 0.0, 0, 1)
-    gi("ZE", T.ZE[:], [[0, 144]], 0, 0)
-    gs("ZE", T.ZE[:, 0:144:16], "ZE", T.ZE[:, 0:144:16], [[-16, 9]], OP.not_equal, 16.0, 16, 1)
-    gs("ZE", T.ZE[:, 0:144:16], "ZE", T.ZE[:, 0:144:16], [[-16, 9]], OP.not_equal, 1.0, 15, 1)
-    gi("ZC", T.ZC[:], [[0, 144]], 0, 0)
-    gs("ZC", T.ZC[:, 0:144:16], "CB", T.CB[:, 0:9], [[-16, 9]], OP.is_ge, 0.0, 16, 1)
-    gs("ZC", T.ZC[:, 0:144:16], "ZC", T.ZC[:, 0:144:16], [[16, 9]], OP.is_ge, 0.0, -1, -1)
-    tabs = mean_tables()
-    for t in range(32):
-        gi(("KT", t, t + 1), T.KT[:, t:t + 1], [[0, 1]], tabs[32 - t][0], 0)
-        gi(("RT", t, t + 1), T.RT[:, t:t + 1], [[0, 1]], tabs[32 - t][1], 0)
-    gi("YT", T.YT[:], [[-255, 32]], 255 * 32, 0)
-    ts(("COLI", 1, 2), ("COLI", 0, 1), 15, OP.bitwise_and)
-    ts(("COLI", 2, 3), ("COLI", 0, 1), 1, OP.bitwise_and)
-    ms("P0", 0.0)
-    cp(("COL", 0, 1), ("COLI", 1, 2))
-    ts(("COL", 1, 2), ("COLI", 2, 3), -2.0, OP.mult, 1.0, OP.add)
-    for n in ("TB0", "TB1", "TN0", "TN1", "TG"):
-        ms((n, 256, BW), 0.0)
-    tt(("COL", 1, 2), ("COL", 1, 2), ("COL", 0, 1), OP.add)
-    ms(("XB", E, ES), 0.0)
-    act("IW", "IB", AF.Copy)
-    act("EW", "IO", AF.Identity, bias=T.COL[:, 0:1], extra=[("COL", 0, 1)])
-    act("EN", "EW", AF.Identity, bias=float(E))
-    act("IBW", ID, AF.Identity, scale=float(BW))
-    act("I16", ID, AF.Identity, scale=16.0)
-    act("SW16", "SWB", AF.Identity, scale=16.0)
-    act("SWN", "SWB", AF.Identity, scale=-1.0)
-    act("NG", ID, AF.Identity, scale=-16.0)
-    act("STF", ("P0", 0, 4 * CA), AF.Identity, bias=1e20)
-    act("STB", ("P0", 0, 8 * (256 - CA)), AF.Identity, bias=STAMP[0])
-    act("WW1", ("P0", 0, 4 * BW), AF.Copy)
-    ts("C", "BI", 0.25, OP.mult)
-    masks("C")
-    select()
-    ts(("SF", 0, 2), ("EW", 0, 2), float(E + 1), OP.add, 31.0, OP.min)
-    cp(("SA", 0, 2), ("SF", 0, 2))
-    ts(("SB", 0, 2), ("SA", 0, 2), 4, OP.arith_shift_right)
-    ts(("SA", 2, 4), ("SA", 0, 2), 15, OP.bitwise_and)
-    cp(("TN0", 256, 258), ("SB", 0, 2))
-    cp(("TN1", 256, 258), ("SA", 2, 4))
-    derive(upto("TB0"))
-    row_out(0, "TB0")
-    cp(upto("TB1"), "J2")
-    row_out(1, "TB1")
-    lin(upto("CG"), [(ID, upto("TB0")), ("IBW", upto("TB1"))])
-    derive_other("DLO")
-    ts("LB", upto("CG"), 256.0, OP.add)
-    for h in range(2):
-        op("a", lambda h=h: g.scalar.activation(T.XB[:, h:E:2], T.CO[:], AF.Identity, bias=-127.5), ["CO"], [("XB", 0, E)])
-    ts("SB", "SH", 4, OP.arith_shift_right)
-    ts("SF", "SH", float(BW), OP.mult)
-    ts("SG", "SB", -float(PB - 1), OP.mult)
-    tt("SF", "SF", "SG", OP.add)
-    cp("SS", "SF")
-    cp("SG", "SH")
-    lin(("PT", 16, 32), [("SWN", "SG")])
-    ts("SA", ("PT", 16, 32), -1.0, OP.mult)
-    ts("SB", "SA", 4, OP.arith_shift_right)
-    ts("SF", "SA", float(BW), OP.mult)
-    ts("SG", "SB", -float(PB - 1), OP.mult)
-    ts("SB", "SA", 1, OP.bitwise_and)
-    tt("SF", "SF", "SG", OP.add)
-    ts("SG", "SB", -2.0, OP.mult, 1.0 - E, OP.add)
-    cp("SS2", "SF")
-    tt("SUM", "SG", "SA", OP.add)
-    ts(("LW", 0, 16), "SUM", float(E), OP.add)
-
-    CH = [(0, 64), (64, 128), (128, 192), (192, 256)]
-    CHS = CH[:3] + [(192, 258)]
-    CV = [(0, CA // 2), (CA // 2, CA), (CA, 168), (168, 224), (224, 256)]
+    NAMES = ("P0", P, 2 * P)
     BK = ["X0", "X1", "X2", "X3"]
+    S16 = ("BIG", S1, S1 + ES)
+    QA, RA = ("BIG", Q0, Q0 + P), ("BIG", R0, R0 + P)
+    QG, RG = ("BIG", Q0 + E, Q0 + P), ("BIG", R0 + E, R0 + P)
+    tab = mean_table()
 
-    def keep(q, o, src=None):
+    def product(step, i):
+        blk = (256 * i, 256 * i + 256)
+        ts(upto("PT"), "C", 0.25 * ((i - step) % 4), OP.is_equal)
+        tt(("MK",) + blk, upto("PT"), ("CI",) + blk, OP.mult)
+
+    def chosen(i):
+        mm(SL, IDF, ("MK", 256 * i, 256 * i + 256), i == 0, i == 3)
+
+    def channels():
+        cp("BI", SL)
+        tt("SELF", SL, "EN", OP.is_equal)
+        ts("J1", "BI", 4, OP.arith_shift_right)
+        ts("J2", "BI", 15, OP.bitwise_and)
+        ts(upto("AL0"), "J1", -256.0, OP.add)
+        row_out("s", 1, 3, "AL0")
+        cp(upto("AL1"), "J2")
+        row_out("s", 1, 6, "AL1")
+        lin(upto("SW"), [(ID, upto("AL0")), ("IBW", upto("AL1"))])
+
+    def lookup(other):
+        ts("J1", "BI", 14, OP.bitwise_and)
+        ts("LB", upto("SW"), 256.0, OP.add)
+        ts(upto("PT"), "J1", 2.0, OP.mult, 1.0, OP.add)
+        tt(other, upto("PT"), upto("AL1"), OP.subtract)
+
+    def stamps(r):
+        act("STB", ("XC", 0, 8 * (256 - CA)), AF.Identity, scale=0.0, bias=STAMP[r])
+
+    def key_constants():
+        act("SWN", "SWB", AF.Identity, scale=-1.0)
+        act("SW16", "SWB", AF.Identity, scale=16.0)
+        act(("IW", 128, 256), ID, AF.Copy)
+        act("IN", ("IW", 0, 160), AF.Identity, scale=-1.0)
+        for n in ("IA", "IC", "ID15", "ID191"):
+            act(n, ID, AF.Identity, scale=DIAG[n])
+
+    def vote_constants():
+        act("ZC", "ZC", AF.Identity, scale=-K)
+        act(("DUM", 0, CA), ("EW", 0, CA), AF.Identity, bias=float(E + KEYS))
+        act(("DUM", CA, 256), ("EW", CA, 256), AF.Identity, bias=float(E + KEYS - 16 * CA))
+        act("STF", ("XC", 0, 4 * CA), AF.Silu, scale=0.0, bias=1e20)
+
+    def cut_constants():
+        act("IM", ID, AF.Identity, scale=DIAG["IM"])
+        act("DH", ("EW", 0, 32), AF.Identity, bias=float(E + ES))
+        act("YT", "YT", AF.Identity, scale=0.5)
+
+    def table_scales():
+        for e in sorted(set(tab[m][1] for m in tab)):
+            t = [t for t in range(32) if tab[32 - t][1] == e]
+            act(("RT", t[0], t[-1] + 1), ("RT", t[0], t[-1] + 1), AF.Identity, scale=2.0 ** -e)
+
+    def shown_lists():
+        cp("SG", "SH")
+        lin(("PT", 16, 32), [("SWN", "SG")])
+        ts("SA", ("PT", 16, 32), -1.0, OP.mult)
+        ts("SB", "SA", 4, OP.arith_shift_right)
+        ts("SF", "SA", float(BW), OP.mult)
+        ts("SG", "SB", -float(P - 1), OP.mult)
+        ts("SB", "SA", 1, OP.bitwise_and)
+        tt("SF", "SF", "SG", OP.add)
+        ts("SG", "SB", -2.0, OP.mult, 1.0 - E, OP.add)
+        cp("SS", "SF")
+        tt("SUM", "SG", "SA", OP.add)
+        ts(("LW", 0, 16), "SUM", float(E), OP.add)
+        ts(("KH", 0, 16), "SUM", float(E), OP.add)
+
+    def keep(q, o):
         c0, c1 = CHS[q]
-        a = big(o, c0, c1) if src is None else (src, 16 * c0, 16 * c1)
-        if (q % 2 == 1) == (src is None):
+        a = big(o, c0, c1)
+        if q % 2 == 0:
             gcopy(big(A0, c0, c1), a)
         else:
             dma("s", ap(big(A0, c0, c1)), ap(a), [a], [big(A0, c0, c1)])
 
-    for q in range(4):
-        keep(q, 0, "XB")
+    def shared(win, lst, share):
+        for c0, c1 in CH:
+            gv(("P1", 16 * c0, 16 * (c0 + share)), win, (lst, c0, c0 + share))
+            ga(("P1", 16 * (c0 + share), 16 * c1), win, (lst, c0 + share, c1))
+
+    dma("s", T.BI[:], T.cur0[:], [], ["BI"])
+    dma("a", T.CI[:, 0:512], T.cand[:, 0:512], [], [("CI", 0, 512)])
+    dma("s", T.CI[:, 512:1024], T.cand[:, 512:1024], [], [("CI", 512, 1024)])
+    dma("a", T.CO[:], T.cov[:], [], ["CO"])
+    dma("s", T.SH[:], T.shown[:], [], ["SH"])
+    gi(("COLI", 0, 1), T.COLI[:, 0:1], [[0, 1]], 0, 1, False)
+    gi("CB", T.CB[:], [[0, 128]], 1, 0)
+    gs(("IB", 0, 128), T.IB[:, 0:128], "CB", T.CB[:], [[-1, 128]], OP.is_equal, 0.0, 0, 1)
+    gi("T3", T.T3[:], [[16, 256]], -E, 0)
+    gs(("IB", 128, 256), T.IB[:, 128:256], "CB", T.CB[:], [[-1, 128]], OP.is_equal, 0.0, 0, 1)
+    picker("ZA", {3: 16.0, 6: 1.0, 7: 2.0 * E})
+    gs("SWB", T.SWB[:, 0:128:2], "CB", T.CB[:, 0:64], [[-2, 64]], OP.is_equal, 0.0, -1, 1)
+    gs("SWB", T.SWB[:, 1:128:2], "CB", T.CB[:, 0:64], [[-2, 64]], OP.is_equal, 0.0, 0, 1)
+    gi("ON", T.ON[:], [[0, BW]], 1, 0)
+    picker("ZE", {0: 16.0, 1: 1.0})
+    picker("ZG", {2: 16.0})
+    gi("YT", T.YT[:], [[-255, 32]], 255 * 32, 0)
+    gi("ZC", T.ZC[:], [[0, 144]], 0, 0)
+    gs("ZC", T.ZC[:, 0:144:16], "CB", T.CB[:, 0:9], [[-16, 9]], OP.is_ge, 0.0, 16, 1)
+    gs("ZC", T.ZC[:, 0:144:16], "ZC", T.ZC[:, 0:144:16], [[16, 9]], OP.is_ge, 0.0, -1, -1)
+    picker("ZH", {ch: 1.0 for ch in range(16) if ch % 4 < 2})
+    ms(NAMES, 0.0)
+    dma("a", T.W1[0:128:16, 0:KEYS], T.P0[:, P:P + KEYS // 16], [("P0", P, P + KEYS // 16)], ["W1"])
+    ts(("COLI", 1, 2), ("COLI", 0, 1), 15, OP.bitwise_and)
+    for n in ("AL0", "AL1", "TN0", "TN1", "NMV", "NGT"):
+        ms((n, 256, BW), 0.0)
+    cp(("COL", 0, 1), ("COLI", 1, 2))
+    ts("C", "BI", 0.25, OP.mult)
+    act(IDF, ID, AF.Copy)
+    act("EW", "T3", AF.Identity, bias=T.COL[:, 0:1], extra=[("COL", 0, 1)])
+    act("EN", "EW", AF.Identity, bias=float(E))
+    for n in ("IBW", "IK", "I16", "IP"):
+        act(n, ID, AF.Identity, scale=DIAG[n])
+    for i in range(4):
+        product(0, i)
+        chosen(i)
+    for h in range(2):
+        op("a", lambda h=h: g.scalar.activation(T.XB[:, h:E:2], T.CO[:], AF.Identity, bias=-127.5), ["CO"], [("XB", 0, E)])
+    channels()
+    lookup(upto("DLO"))
+    row_out("s", 1, 1, "ON")
+    dma("s", T.P0[:, P // 2:P], T.P0[:, P:P + P // 2], [("P0", P, P + P // 2)], [("P0", P // 2, P)])
+    act(upto("TB0"), upto("AL0"), AF.Copy)
+    for h in range(2):
+        op("a", lambda h=h: g.scalar.activation(T.XC[:, h:E // 2:2], T.CO[:, 0:E // 4], AF.Identity, bias=-127.5), ["CO"], [("XC", 0, E // 2)])
+    ms(("XB", E, ES), 0.0)
+    ms(("LK", 256, 258), 1.0)
+    ts(("SF", 0, 2), ("EW", 0, 2), float(E + 1), OP.add, 31.0, OP.min)
+    cp(("SA", 0, 2), ("SF", 0, 2))
+    ts(("SB", 0, 2), ("SA", 0, 2), 4, OP.arith_shift_right)
+    ts(("SA", 2, 4), ("SA", 0, 2), 15, OP.bitwise_and)
+    for n in ("TN0", "TB0"):
+        cp((n, 256, 258), ("SB", 0, 2))
+    for n in ("TN1", "DLO"):
+        cp((n, 256, 258), ("SA", 2, 4))
+    gcopy(("XC", E // 2, 3 * E // 4), ("XB", E // 2, 3 * E // 4))
+    gcopy(("XC", 3 * E // 4, ES), ("XB", 3 * E // 4, ES))
+    ms(("P0", 0, P // 2), 0.0)
+    for t in range(32):
+        gi(("RT", t, t + 1), T.RT[:, t:t + 1], [[0, 1]], tab[32 - t][0], 0)
 
     for r in range(RO):
         last = r == RO - 1
@@ -349,61 +384,52 @@ def rank_program(g, core, T, topo):
         def sums(c0, c1):
             return ("XB", 16 * c0, 16 * c1) if last else big(S0, c0, c1)
 
+        for h, (c0, c1) in enumerate(HALF):
+            mm((BK[h], 0, 128), "IK", ("SELF", c0, c1), True, False)
+        shared(NAMES, "LB", SHARE_A)
+        for q, (c0, c1) in enumerate(CH):
+            extract((BK[q // 2], c0 % 128, c0 % 128 + 64), "P1", c0, c1, "ZA", start=False, stop=q % 2 == 1)
         if r == 0:
-            lin(upto("SW"), [("SW16", upto("TB0")), ("SWB", "DLO")])
-            ts("LU", upto("SW"), float(E), OP.add)
-        for q in (3, 0, 1, 2):
-            c0, c1 = CH[q]
-            e = "v" if q >= 2 else "a"
-            deps(e, e, ["P0c1"], [])
-            (gv if q >= 2 else ga)(("P1", 16 * c0, 16 * c1), "P0", ("LB", c0, c1))
-        ga(upto("PS"), "P0", "SS")
-
-        def links(qs):
-            for q in qs:
-                tt(("LK",) + CH[q], (BK[q], 0, 64), ("EW",) + CH[q], OP.is_equal)
-            for q in qs:
-                c0, c1 = CH[q]
-                tt(("TN0", c0, c1), ("LK", c0, c1), ("TB0", c0, c1), OP.mult)
-                tt(("TN1", c0, c1), ("LK", c0, c1), ("DLO", c0, c1), OP.mult)
-                c1 = CHS[q][1]
-                lin((BK[q], 128, 128 + c1 - c0), [("I16", ("TN0", c0, c1)), (ID, ("TN1", c0, c1))])
-
-        def first_list(q):
-            c0, c1 = CHS[q]
-            ts(("L0", c0, c1), (BK[q], 128, 128 + c1 - c0), float(E), OP.add)
+            key_constants()
+        act("SN", upto("TB0"), AF.Sign, bias=0.5)
+        for h, (c0, c1) in enumerate(HALF):
+            lk = (BK[h], 128, 256)
+            tt(lk, (BK[h], 0, 128), ("EW", c0, c1), OP.is_equal)
+            if r > 0:
+                tt(lk, lk, ("NMV", c0, c1), OP.max)
+            tt(("TN0", c0, c1), lk, ("TB0", c0, c1), OP.mult)
+            tt(("TN1", c0, c1), lk, ("DLO", c0, c1), OP.mult)
+            cp(("LK", c0, c1), lk)
+            c2 = c1 + 2 * h
+            lin((BK[2 + h], 0, c2 - c0), [("I16", ("TN0", c0, c2)), (ID, ("TN1", c0, c2))])
+        row_out("s", 0, 0, "TN0")
+        row_out("s", 0, 1, "TN1")
+        lin(upto("SW"), [("SWB", upto("LK"))])
+        act(upto("NGT"), upto("SW"), AF.Identity, scale=-1.0, bias=1.0)
+        row_out("a", 1, 2, "NGT")
+        lin(upto("CG", 258), [(ID, upto("TB0", 258)), ("IBW", upto("DLO", 258)), ("IP", upto("LK", 258))])
+        lin(SL, [("IC", "C"), ("ID15", upto("TB0")), ("ID191", upto("DLO")), ("IK", "SN")])
+        act("T1", SL, AF.Relu, bias=G0 + E - K)
+        lin(SL, [("IA", "C"), ("I16", upto("TB0")), (ID, upto("DLO")), (("IN", 0, 128), "T1")])
+        act("KEY", SL, AF.Identity, bias=float(G0 + E))
 
         def first(q):
             c0, c1 = CHS[q]
-            gt(big(S0, c0, c1), "XB", ("L0", c0, c1), big(A0, c0, c1), OP.add)
+            gt(big(S0, c0, c1), "XB", ("L0", c0, c1), ("XC", 16 * c0, 16 * c1), OP.add)
             keep(q, S0)
 
-        for q in (3, 0, 1, 2):
-            extract((BK[q], 0, 64), "P1", *CH[q])
-        links((3, 0))
-        links((1, 2))
-        row_out(0, "TN0")
-        row_out(1, "TN1")
-        lin(upto("CG", 258), [(ID, upto("TN0", 258)), ("IBW", upto("TN1", 258))])
-        extract(("PT", 0, 16), "PS", 0, 16)
-        first_list(0)
-        first_list(3)
-        ts("TP", "LK", -1.0, OP.add)
+        ts(("L0", 0, 128), ("X2", 0, 128), float(E), OP.add)
+        ts(("L0", 128, 258), ("X3", 0, 130), float(E), OP.add)
         first(0)
-        ts("LS", upto("CG", 258), 256.0, OP.add)
-        first_list(1)
-        first_list(2)
-        first(1)
-        first(2)
-        first(3)
+        ts("LS", upto("CG", 258), 256.0 + P, OP.add)
         if r == 0:
-            act("E1", "IO", AF.Identity, bias=T.COL[:, 1:2], extra=[("COL", 1, 2)])
-            act(("DUM", 0, CA), ("EW", 0, CA), AF.Identity, bias=float(E + KEYS))
-            act(("DUM", CA, 256), ("EW", CA, 256), AF.Identity, bias=float(E + KEYS - 16 * CA))
-            act("DH", ("EW", 0, 32), AF.Identity, bias=float(2 * E))
-            act("DQ", "DUM", AF.Identity, scale=-0.25, bias=256.0)
-        tt("T1", "TP", "E1", OP.mult)
-        deps("a", "a", ["P0c1"], [])
+            shown_lists()
+        first(1)
+        lin(upto("SW"), [("SW16", upto("TB0")), ("SWB", upto("DLO"))])
+        first(2)
+        ts("LU", upto("SW"), float(E), OP.add)
+        first(3)
+
         def offs(s, q):
             c0, c1 = CHS[q] if s < 5 else CH[q]
             if s < 5:
@@ -412,208 +438,187 @@ def rank_program(g, core, T, topo):
                 ts(("LT", c0, c1), (BK[q], 0, c1 - c0), 0.0, OP.max)
 
         for s in range(1, 6):
-            src = ("XB", 0) if s == 1 else ("BIG", S0 if s % 2 == 0 else S1)
+            src = S0 if s % 2 == 0 else S1
             dst = S0 if s % 2 == 1 else S1
             pin, pout = ("P0", "P1") if s % 2 == 1 else ("P1", "P0")
             lst = "L%d" % (s - 1)
+
+            def pointers(q):
+                c0, c1 = (CHS if s < 5 else CH)[q]
+                ga((pout, 16 * c0, 16 * c1), (pin, 0, 2 * P if s == 1 else ES), ("LS" if s == 1 else lst, c0, c1))
+                extract((BK[q], 0, c1 - c0), pout, c0, c1)
+
+            if s == 1:
+                mm(upto("CG"), "I16", upto("LK"), True, False)
+            if s == 5:
+                ga("PS", ("P0", 0, ES), "LW")
+                extract(("CG", 0, 32), "PS", 0, 32)
+                ga("PG", S16, "LW")
             for q, (c0, c1) in enumerate(CHS if s < 5 else CH):
                 if s > 1:
                     if (s, q) == (2, 0):
                         offs(1, 0)
-                    offs(s - 1, q + 1) if q < 3 else offs(s, 0)
-                    gt(big(dst, c0, c1) if s < 5 else sums(c0, c1), (src[0], src[1], src[1] + ES), (lst, c0, c1), big(A0, c0, c1), OP.add)
+                    if q < 3:
+                        offs(s - 1, q + 1)
+                    elif s < 5:
+                        offs(s, 0)
+                    if (s, q) == (5, 1):
+                        ts("LX", ("CG", 0, 32), float(E), OP.add)
+                        ga("PS", ("P0", 0, ES), "LX")
+                        extract(("CG", 0, 32), "PS", 0, 32)
+                        pointers(1)
+                    if (s, q) == (5, 2):
+                        gt("PH", S16, "LX", "PG", OP.add)
+                    if (s, q) == (5, 3):
+                        ts("LY", ("CG", 0, 32), 0.0, OP.max)
+                        gt("PG", "RT", "LY", "PH", OP.mult)
+                        pointers(2)
+                        lin(upto("SW"), [(("IW", 32, 160), upto("PG"))])
+                        act(upto("PAY"), upto("SW"), AF.Copy)
+                        send(upto("PAY"), lambda d: T.BIG[:, Q0 + E + GH * (d - 1):Q0 + E + GH * d], "ac%d" % r, "lc%d" % r, 1, [QG])
+                        lin(upto("CG"), [(("IW", 32, 160), ("PG", 256, 512)), (("IN", 32, 160), upto("PG"))])
+                        pointers(3)
+                        act(("PAY", 256, 512), upto("CG"), AF.Abs)
+                        send(("PAY", 256, 512), lambda d: T.BIG[:, R0 + E + GH * (d - 1):R0 + E + GH * d], "ar%d" % r, "lr%d" % r, 1, [RG])
+                    gt(big(dst, c0, c1) if s < 5 else sums(c0, c1), ("BIG", src, src + ES), (lst, c0, c1), big(A0, c0, c1), OP.add)
                     if s < 5:
                         keep(q, dst)
-                ga((pout, 16 * c0, 16 * c1), (pin, 0, PB if s == 1 else ES), ("LS" if s == 1 else lst, c0, c1))
-                extract((BK[q], 0, c1 - c0), pout, c0, c1)
-                if (s, q) == (2, 0):
-                    extract(("PT", 32, 48), "PS", 0, 16)
-                if (s, q) == (2, 1):
-                    lin(("SW", 0, 256), [("SW16", upto("TN0")), ("SWB", upto("TN1")), ("SWN", "T1")])
-                if (s, q) == (2, 2):
-                    lin(SL, [(ID, upto("TB0")), ("IBW", upto("TB1")), (ID, "C"), (IDF, "DQ")])
+                if s < 5 or q == 0:
+                    pointers(q)
+                if s == 1:
+                    extract(("CG",) + CH[q], "P1", CH[q][0], CH[q][1], "ZG", start=False, stop=q == 3)
             if s == 1:
-                ga(upto("PS"), "P0", "SS2")
+                ga(upto("PS"), ("P0", 0, P), "SS")
+                extract(("PT", 32, 48), "PS", 0, 16)
+            if s == 2:
+                act("GT", upto("CG"), AF.Identity, bias=8.5)
             if s == 3:
                 ts("SF", ("PT", 32, 48), 0.0, OP.is_ge)
                 ts("SG", ("PT", 32, 48), float(E), OP.add)
                 tt("SF", "SF", "SUM", OP.mult)
-                ts("LV", upto("SW"), float(E), OP.add)
-                tt("SG", "SG", "SF", OP.add)
-            if s == 4:
-                cp(("LW", 16, 32), "SG")
-        ga("PS", ("P1", 0, E), "LW")
-        extract(("CG", 0, 32), "PS", 0, 32)
-        ga("PG", sums(0, 256), "LW")
-        act("KD", SL, AF.Identity, scale=4.0)
-        if r == 0:
-            act("RT", "RT", AF.Identity, scale=2.0 ** -17)
-            act("IN", ("IW", 0, 160), AF.Identity, scale=-1.0)
-        def scaled(c0, c1):
-            gt(big(S1, c0, c1), "KT", ("LT", c0, c1), sums(c0, c1), OP.mult)
-
-        offs(5, 1)
-        scaled(0, 64)
-        offs(5, 2)
-        scaled(64, 112)
-        ts("LX", ("CG", 0, 32), 0.0, OP.max)
-        offs(5, 3)
-        scaled(112, 128)
-        gt("PH", "KT", "LX", "PG", OP.mult)
-        scaled(128, 144)
-        gt("PG", "RT", "LX", "PH", OP.mult)
-        lin(upto("SW"), [(("IW", 32, 160), upto("PG"))])
-        act(upto("PAY"), upto("SW"), AF.Copy)
-        send([(upto("PAY"), lambda d: T.BIG[:, Q0 + E + GH * (d - 1):Q0 + E + GH * d])], "ac%d" % r, "lc%d" % r, 1, [("BIG", Q0 + E, Q0 + P)])
-        lin(upto("CG"), [(("IW", 32, 160), ("PG", 256, 512)), (("IN", 32, 160), upto("PG"))])
-        act(("PAY", 256, 512), upto("CG"), AF.Abs)
-        send([(("PAY", 256, 512), lambda d: T.BIG[:, R0 + E + GH * (d - 1):R0 + E + GH * d])], "ar%d" % r, "lr%d" % r, 1, [("BIG", R0 + E, R0 + P)])
-        scaled(144, 256)
-        for o in (Q0, R0):
-            gi(("BIG", o + P, o + PW), T.BIG[:, o + P:o + PW], [[0, PW - P]], 0, 0)
-        if r == 0:
-            gi("ZG", T.ZG[:], [[0, 144]], 0, 0)
-            gs("ZG", T.ZG[:, 0:144:16], "ZG", T.ZG[:, 0:144:16], [[-16, 9]], OP.not_equal, 1.0, 48, 1)
-            gs("ZG", T.ZG[:, 0:144:16], "ZG", T.ZG[:, 0:144:16], [[-16, 9]], OP.not_equal, 1.0, -80, 1)
-            for i in range(16):
-                o = 4 * BW * i + 1024
-                gi(("W1", o, o + 192), T.W1[:, o:o + 192], [[0, 192]], 0, 0)
-            gi("H", T.H[:], [[0, E + 2 * GH]], 0, 0)
-            act("YT", "YT", AF.Identity, scale=0.5)
-            dma("s", T.W1[0:128:16, 0:KEYS], T.WW1[:], ["WW1"], ["W1"])
+                if r == 0:
+                    table_scales()
+                tt(("KH", 16, 32), "SG", "SF", OP.add)
+                cp(("LW", 16, 32), ("KH", 16, 32))
+        offs(5, 0)
         for q, (c0, c1) in enumerate(CH):
-            gt(big(Q0, c0, c1), "RT", ("LT", c0, c1), big(S1, c0, c1), OP.mult)
-            act(big(S1, c0, c1), big(Q0, c0, c1), AF.Copy)
-        QO, QA = ("BIG", Q0, Q0 + E), ("BIG", Q0, Q0 + PW)
-        RA = ("BIG", R0, R0 + PW)
-        for q, (c0, c1) in enumerate(CH):
-            gt(big(R0, c0, c1), QO, ("LV", c0, c1), big(S1, c0, c1), OP.subtract)
-            act(big(R0, c0, c1), big(R0, c0, c1), AF.Abs)
-        if r == 0:
-            tt(("KH", 0, 16), "SH", ("DH", 0, 16), OP.subtract)
-        for c0, c1 in CV:
-            gt(big(A0, c0, c1), QA, ("LU", c0, c1), big(S1, c0, c1), OP.subtract)
-            act(big(A0, c0, c1), big(A0, c0, c1), AF.Abs)
-            act(big(A0, c0, c1), big(A0, c0, c1), AF.Identity, bias=MARGIN)
+            if q < 3:
+                offs(5, q + 1)
+            gt(big(Q0, c0, c1), "RT", ("LT", c0, c1), sums(c0, c1), OP.mult)
+            if q < 2:
+                act(big(S1, c0, c1), big(Q0, c0, c1), AF.Copy)
+            elif q == 2:
+                gcopy(big(S1, c0, c1), big(Q0, c0, c1))
+            else:
+                dma("s", ap(big(S1, c0, c1)), ap(big(Q0, c0, c1)), [big(Q0, c0, c1)], [big(S1, c0, c1)])
+            if (q, r) == (1, 0):
+                vote_constants()
 
-        def sums_out(chunks):
-            for c0, c1 in chunks:
-                gt(sums(c0, c1), "YT", ("LT", c0, c1), sums(c0, c1), OP.add)
+        def margin(c0, c1):
+            act(big(A0, c0, c1), big(R0, c0, c1), AF.Identity, bias=MARGIN)
+
+        for q, (c0, c1) in enumerate(C1):
+            gt(big(S1, c0, c1), QA, ("LU", c0, c1), big(S1, c0, c1), OP.subtract)
+            act(big(R0, c0, c1), big(S1, c0, c1), AF.Abs)
+            if q == 1:
+                margin(*C2[0])
+        for c in C2[1:]:
+            margin(*c)
+        act("TU", upto("LK"), AF.Identity, scale=-stamp, bias=stamp)
+        if r == 0:
+            stamps(0)
 
         def offsets(bank, c0, c1):
-            halves = ((c0, (c0 + c1) // 2), ((c0 + c1) // 2, c1))
-            ts(("T1", c0, c1), (bank, 0, c1 - c0), 8.5, OP.is_ge)
-            for h in halves:
-                tt(("T1",) + h, ("T1",) + h, ("KD",) + h, OP.mult)
-            for h in halves:
-                tt(("T1",) + h, ("T1",) + h, ("DUM",) + h, OP.add)
-            for h in halves:
-                cp(("LC",) + h, ("T1",) + h)
+            t = (bank, 256, 256 + c1 - c0)
+            tt(t, (bank, 0, c1 - c0), ("KEY", c0, c1), OP.max)
+            tt(t, t, ("DUM", c0, c1), OP.min)
+            cp(("LC", c0, c1), t)
 
-        for q, (c0, c1) in enumerate(CV):
-            bank, b0, b1 = ("X0", 0, CA) if q < 2 else ("X1", CA, 256)
-            if q in (0, 2):
-                mm((bank, 0, b1 - b0), "NG", ("LK", b0, b1), True, False)
+        def sums_out(c0, c1):
+            gt(sums(c0, c1), "YT", ("LT", c0, c1), sums(c0, c1), OP.add)
+            dma("a", T.ys[:, 16 * c0:16 * c1], T.XB[:, 16 * c0:16 * c1], [sums(c0, c1)], [])
+
+        for q, (c0, c1) in enumerate(C2):
+            bank, b0, b1 = ("X0", 0, CA) if q < 3 else ("X1", CA, 256)
+            if q in (0, 3):
+                mm((bank, 0, b1 - b0), "IK", ("GT", b0, b1), True, False)
             gt(("P1", 16 * c0, 16 * c1), RA, ("LU", c0, c1), big(A0, c0, c1), OP.is_gt)
-            extract((bank, c0 - b0, c1 - b0), "P1", c0, c1, "ZC", 1, False, q in (1, 4))
-            if q == 2:
+            extract((bank, c0 - b0, c1 - b0), "P1", c0, c1, "ZC", 1, False, q in (2, 5))
+            if q == 4:
                 offsets("X0", 0, CA)
+        ts("DC", "C", 0.6, OP.is_lt, 0.75, OP.subtract)
+        if not last:
+            product(1, 0)
+            chosen(0)
         offsets("X1", CA, 256)
         for k in range(4):
             c0 = k * CA // 4
             op("a", lambda c0=c0: g.scalar.activation(T.BIG[:].indirect(T.LC[:, c0:c0 + CA // 4]), T.STF[:], AF.Silu),
                ["STF", ("LC", c0, c0 + CA // 4)], ["BIG"])
-        dma("a", T.WW2[:], T.BIG[0:128:16, 0:KEYS], ["BIG"], ["WW2"])
+        dma("a", T.WG2[:], T.BIG[0:128:16, 0:G0], [("BIG", 0, G0)], ["WG2"])
+        dma("g", T.P0[1:128:4, 0:E], T.BIG[0:128:16, G0:KEYS], [("BIG", G0, KEYS)], [("P0", 0, E, 0x2222)])
         hw = (256 - CA) // 2
         for c0 in (CA, CA + hw):
-            op("v", lambda c0=c0: g.vector.tensor_copy(T.W1[:].indirect(T.LC[:, c0:c0 + hw]), T.STB[:]),
-               ["STB", ("LC", c0, c0 + hw)], ["W1"])
-        dma("s", T.WW1[:], T.W1[0:128:16, 0:KEYS], ["W1"], ["WW1"])
-        act("TU", "LK", AF.Identity, scale=-stamp, bias=stamp)
-        for i in range(16):
-            for k in range(4):
-                o = 4 * BW * i + 1024
-                mm(("CG", 0, 48), ("ZG", 16 - i, 144 - i), "W1", i + k == 0, False, rap=T.W1[:, o + k:o + 192:4])
+            put("W1", ("LC", c0, c0 + hw), "STB")
+        dma("s", T.WG1[:], T.W1[0:128:16, 0:G0], [("W1", 0, G0)], ["WG1"])
+        dma("s", T.P0[0:128:4, 0:E], T.W1[0:128:16, G0:KEYS], [("W1", G0, KEYS)], [("P0", 0, E, 0x1111)])
+        if r == 0:
+            cut_constants()
+        if last:
+            sums_out(0, 64)
+            sums_out(64, 96)
+        else:
+            for i in range(1, 4):
+                product(1, i)
+                chosen(i)
         for k in range(4):
-            mm(("CG", 0, 48), ("IW", 96, 224), "WW2", False, k == 3, rap=T.WW2[:, 1024 + k:1216:4])
-        ts("SF", ("PT", 0, 16), float(E), OP.add)
-        cursors_on()
-        tt(("KH", 16, 32), "SF", ("DH", 16, 32), OP.subtract)
+            mm(("CG", 0, 48), ("IW", 96, 224), ("WG2", 48 * k, 48 * k + 48), k == 0, False)
+        for k in range(4):
+            mm(("CG", 0, 48), ("IB", 96, 224), ("WG1", 48 * k, 48 * k + 48), False, k == 3)
+        ts("HG", ("CG", 0, 48), thr, OP.is_ge, -1.0, OP.mult)
+        send("HG", lambda d: T.RH[:, (3 * r + d - 1) * 48:(3 * r + d) * 48], "ah%d" % r, "lh%d" % r, -1, [("RH", 144 * r, 144 * r + 144)], [QG, RG])
         if last:
-            tt("CM", "CM", "C", OP.subtract)
-            ts("T2", "C", 4.0, OP.mult)
-            ts("T3", "CM", 4.0, OP.mult)
+            sums_out(96, 128)
         else:
-            masks("CM")
-        ts("HG", ("CG", 0, 48), thr, OP.is_ge)
-        send([("HG", lambda d: T.RH[:, (3 * r + d - 1) * 48:(3 * r + d) * 48])], "ah%d" % r, "lh%d" % r, -1, [("RH", 144 * r, 144 * r + 144)])
-        if last:
-            sums_out(CH[:1])
-        else:
-            select(0, 2, sums=False)
-        act(upto("P1", 1024), upto("WW2", 1024), AF.Copy)
-        for w in ("P1", "WW1"):
-            for k in range(4):
-                mm(("X2", 0, 256), "SWB", upto(w, 1024), (w, k) == ("P1", 0), (w, k) == ("WW1", 3), rap=T[w][:, k:1024:4])
-        if not last:
-            select(0, 2, products=False)
-            for q in range(4):
-                gcopy(big(A0, *CHS[q]), ("XB", 16 * CHS[q][0], 16 * CHS[q][1]))
-        ts(upto("TG"), upto("X2"), thr, OP.is_ge, stamp, OP.mult)
-        dma("s", T.P0[0:128:16, :], T.TG[:], ["TG"], ["P0"])
-        if not last:
-            select(2, 4)
+            channels()
+        mm(("X2", 0, 32), IDF, "DH", True, False)
         mm(upto("X0"), ID, "TU", True, False)
-        mm(upto("X0"), "SWB", upto("TG"), False, False)
-        if last:
-            sums_out(CH[1:])
-            for c0, c1 in CH:
-                dma("s", T.ys[:, 16 * c0:16 * c1], T.XB[:, 16 * c0:16 * c1], [("XB", 16 * c0, 16 * c1)], [])
-        for c0, c1 in CH:
-            ga(("P1", 16 * c0, 16 * c1), "P0", ("LS", c0, c1))
-        if not last:
-            tt("CM", "CM", "C", OP.subtract)
-            derive(upto("M0"))
+        shared(("P0", 0, ES), "L0", SHARE_H)
+        for c0, c1 in CH[:2]:
+            extract(("X0", c0, c1), "P1", c0, c1, "ZH", start=False, stop=False)
         b = 144 * r
-        tt("AH", ("RH", b, b + 16), ("RH", b + 64, b + 80), OP.max)
-        tt("AH", "AH", ("RH", b + 128, b + 144), OP.max)
-        tt(("TH", 0, 16), "AH", ("KH", 0, 16), OP.mult)
-        tt(("TH", 16, 32), "AH", ("KH", 16, 32), OP.mult)
-        tt("TH", "TH", "DH", OP.add)
+        for h in range(2):
+            for d in range(3):
+                mm(("X2", 16 * h, 16 * h + 16), "IK", ("RH", b + 64 * d, b + 64 * d + 16), False, (h, d) == (1, 2))
+        for c0, c1 in CH[2:]:
+            extract(("X0", c0, c1), "P1", c0, c1, "ZH", start=False, stop=False)
+        if not last:
+            lin(upto("CG"), [(ID, upto("AL0")), ("IM", upto("TB0"))])
+            act("D0", upto("CG"), AF.Copy)
+        tt("TH", ("X2", 0, 32), "KH", OP.max)
         cp("LH", "TH")
         for c0 in (0, 16):
-            op("v", lambda c0=c0: g.vector.tensor_copy(T.H[:].indirect(T.LH[:, c0:c0 + 16]), T.STB[:, 0:256]),
-               ["STB", ("LH", c0, c0 + 16)], ["H"])
-        extract(("X0", 0, 128), "P1", 0, 128, start=False, stop=False)
-        extract(upto("X0"), "H", 0, 256, start=False, stop=False)
-        for q in (2, 3):
-            extract(("X0",) + CH[q], "P1", CH[q][0], CH[q][1], start=False, stop=q == 3)
-        if not last:
-            tt(upto("M0"), upto("M0"), upto("TB0"), OP.subtract)
-            tt(upto("M1"), "J2", upto("TB1"), OP.subtract)
-            derive_other("MD")
-            tt("MD", "MD", "DLO", OP.subtract)
-        ts("MV", upto("X0"), thr, OP.is_ge)
+            put(("P0", 0, P), ("LH", c0, c0 + 16), upto("STB"))
+        extract(upto("X0"), "P0", 0, 256, "ZH", 1, start=False)
         if last:
-            tt("T3", "T3", "MV", OP.mult)
-            tt("T2", "T2", "T3", OP.add)
+            ts("T2", "C", 4.0, OP.mult)
+            ts("T3", "DC", 4.0, OP.mult)
+            sums_out(128, 192)
+            ts(upto("PT"), upto("X0"), thr, OP.is_ge)
+            tt(upto("PT"), upto("PT"), "T3", OP.mult)
+            tt("T2", upto("PT"), "T2", OP.add)
             dma("s", T.yc[:], T.T2[:], ["T2"], [])
+            sums_out(192, 256)
         else:
-            tt(upto("M0"), upto("M0"), "MV", OP.mult)
-            tt(upto("M1"), upto("M1"), "MV", OP.mult)
-            tt(upto("TB0"), upto("TB0"), upto("M0"), OP.add)
-            row_out(0, "TB0")
-            tt(upto("TB1"), upto("TB1"), upto("M1"), OP.add)
-            row_out(1, "TB1")
-            lin(upto("CG"), [(ID, upto("TB0")), ("IBW", upto("TB1"))])
-            act("STB", ("XB", 0, 8 * (256 - CA)), AF.Identity, scale=0.0, bias=STAMP[r + 1])
-            tt("MD", "MD", "MV", OP.mult)
-            ts("LB", upto("CG"), 256.0, OP.add)
-            tt("DLO", "DLO", "MD", OP.add)
-            tt("CM", "CM", "MV", OP.mult)
-            lin(upto("SW"), [("SW16", upto("TB0")), ("SWB", "DLO")])
-            tt("C", "C", "CM", OP.add)
-            ts("LU", upto("SW"), float(E), OP.add)
+            stamps(r + 1)
+            lookup("ALO")
+            tt("D1", "ALO", upto("DLO"), OP.subtract)
+            ts(upto("NMV"), upto("X0"), thr, OP.is_lt)
+            row_out("s", 1, 7, "NMV")
+            ts(("PT", 256, 512), upto("X0"), thr, OP.is_ge)
+            for d, cur in (("DC", "C"), ("D0", upto("TB0")), ("D1", upto("DLO"))):
+                tt(upto("PT"), ("PT", 256, 512), d, OP.mult)
+                tt(cur, upto("PT"), cur, OP.add)
 
     for s in total:
         if max([0] + [waited[k] for k in waited if k[1] == s]) < total[s]:

@@ -6,7 +6,8 @@ BW = P // 16
 ES = E + 32
 G0 = 4 * (P - E)
 KEYS = G0 + 4 * E
-CA = 136
+CA = 120
+NST = 16 * max(192 - CA, 64)
 S0, S1, Q0, R0, A0, BIGW = 0, ES, 2 * ES, 2 * ES + P, 2 * ES + 2 * P, 3 * ES + 2 * P
 SCALE10 = 168199201
 MARGIN = 2.2
@@ -17,23 +18,23 @@ ALL = 0xFFFF
 CH = [(0, 64), (64, 128), (128, 192), (192, 256)]
 CHS = CH[:3] + [(192, 258)]
 HALF = [(0, 128), (128, 256)]
-C1 = [(0, 16), (16, 80), (80, 144), (144, 208), (208, 240), (240, 256)]
-C2 = [(0, 32), (32, 80), (80, CA), (CA, 192), (192, 240), (240, 256)]
-SHARE_A, SHARE_H = 32, 32
+C1 = [(0, 64), (64, 112), (112, 160), (160, 200), (200, 232), (232, 256)]
+C2 = [(0, 40), (40, 88), (88, 144), (144, 192), (192, 240), (240, 256)]
+SHARE_A, SHARE_H = (32, 32, 32, 32), (40, 40, 16, 0)
 
 F, B, I, U = "float32", "bfloat16", "int32", "uint16"
 SCRATCH = {
     "BIG": ("sbuf", [128, BIGW], F), "W1": ("sbuf", [128, KEYS + 16 * (256 - CA)], B), "XB": ("sbuf", [128, ES], F),
     "XC": ("sbuf", [128, ES], B), "P0": ("sbuf", [128, 2 * P], B), "P1": ("sbuf", [128, ES], B),
     "WG1": ("sbuf", [128, 192], B), "WG2": ("sbuf", [128, 192], F),
-    "CI": ("sbuf", [128, 1024], I), "MK": ("sbuf", [128, 1024], F), "CO": ("sbuf", [128, 2048], B),
-    "STB": ("sbuf", [128, 8 * (256 - CA)], B), "STF": ("sbuf", [128, 4 * CA], F),
+    "CI": ("sbuf", [128, 1024], I), "MK": ("sbuf", [128, 512], F), "P2": ("sbuf", [128, E + 512], B),
+    "STB": ("sbuf", [128, NST], B), "STF": ("sbuf", [128, 4 * CA], F),
     "IW": ("sbuf", [128, 256], F), "IB": ("sbuf", [128, 256], B), "SWN": ("sbuf", [128, 128], F), "IN": ("sbuf", [128, 160], F),
     "RT": ("sbuf", [128, 32], F), "YT": ("sbuf", [128, 32], F),
     "RH": ("sbuf", [128, RO * 3 * 48], B), "HG": ("sbuf", [128, 48], B),
     "COL": ("sbuf", [128, 8], F), "COLI": ("sbuf", [128, 8], I),
     "LW": ("sbuf", [128, 32], U), "LX": ("sbuf", [128, 32], U), "LY": ("sbuf", [128, 32], U), "LH": ("sbuf", [128, 32], U), "SS": ("sbuf", [128, 16], U),
-    "PS": ("sbuf", [128, 512], B), "PG": ("sbuf", [128, 512], F), "PH": ("sbuf", [128, 512], F), "PAY": ("sbuf", [128, 512], F),
+    "PS": ("sbuf", [128, 512], B), "PG": ("sbuf", [128, 512], F), "PAY": ("sbuf", [128, 512], F),
     "KH": ("sbuf", [128, 32], F), "DH": ("sbuf", [128, 32], F), "TH": ("sbuf", [128, 32], F),
 }
 for _n in ("SH", "SA", "SB"):
@@ -51,7 +52,7 @@ for _n in ("TB0", "DLO", "LK"):
     SCRATCH[_n] = ("sbuf", [128, 264], B)
 for _n in ("TU", "C", "DC", "ALO", "SELF", "D1", "GT", "SN"):
     SCRATCH[_n] = ("sbuf", [128, 256], B)
-for _n in ("EW", "EN", "D0", "DUM", "KEY", "T1", "T2", "T3"):
+for _n in ("EW", "EN", "D0", "DUM", "KEY", "T1"):
     SCRATCH[_n] = ("sbuf", [128, 256], F)
 for _n in ("BI", "J1", "J2"):
     SCRATCH[_n] = ("sbuf", [128, 256], I)
@@ -63,7 +64,8 @@ PSUM = ("X0", "X1", "X2", "X3", "SW", "CG", "PT", "SL")
 for _n in PSUM:
     SCRATCH[_n] = ("psum", [128, 512], F)
 SEMAPHORES = ["cv", "ca", "cp", "cg"] + ["d%d" % i for i in range(NDMA)] + \
-    ["%s%d" % (k, r) for k in ("ac", "ar", "ah", "lc", "lr", "lh") for r in range(RO)]
+    ["%s%d" % (k, r) for k in ("a0", "a1", "ah", "l0", "l1", "lh", "h0", "h1") for r in range(RO)]
+DIRECT = [((1, 2, 3), (3,))] + [((1, 2), (3,))] * (RO - 1)
 
 
 def mean_table():
@@ -76,9 +78,54 @@ def mean_table():
     return out
 
 
+def helper_of(rank, T, topo):
+    core = T.cores[rank]
+    return [c for c in topo.cores_of(core) if topo.die(c) != topo.die(core)
+            and all(topo.may_write(c, o) for o in T.cores if o != core)][0]
+
+
+def far_engines(core, rank, T, topo):
+    reach = [topo.engines(core, T.cores[(rank + d) % N]) for d in range(1, N)]
+    return [e for e in reach[0] if all(e in x for x in reach)]
+
+
+def transfer(topo, cores, engines, sem, src, dsts):
+    ids = [DstId(rid=topo.addr(c)[0], pnc=topo.addr(c)[1]) for c in cores]
+    return RemoteDMATransfer(dst_ids=ids, dma_engine_mask=sum(1 << e for e in engines), remote_sem=sem, src=src, dsts=dsts)
+
+
+def ghost_place(T, k, d):
+    o = (Q0, R0)[k] + E + GH * (d - 1)
+    return T.BIG[:, o:o + GH]
+
+
+def relay_place(T, k, r):
+    o = GH * (2 * r + k)
+    return T.BIG[:, o:o + GH]
+
+
+def helper_program(g, core, rank, T, topo):
+    engs = far_engines(core, rank, T, topo)
+    near = [e for e in topo.engines(T.cores[rank], core) if e not in far_engines(T.cores[rank], rank, T, topo)]
+    sent = []
+    for r in range(RO):
+        for k in range(2):
+            ds = [d for d in range(1, N) if d not in DIRECT[r][k]]
+            if ds:
+                g.wait_ge(T.sem["h%d%d" % (k, r)], len(near))
+                g.remote_dma_fused([transfer(topo, [T.cores[(rank + d) % N] for d in ds], engs, T.sem["a%d%d" % (k, r)],
+                                             relay_place(T, k, r), [ghost_place(T, k, d) for d in ds])], local_sem=T.sem["l%d%d" % (k, r)])
+                sent.append("l%d%d" % (k, r))
+    for s in sent:
+        g.wait_ge(T.sem[s], len(engs))
+
+
 def rank_program(g, core, T, topo):
     rank = T.rank_of(core)
     if rank is None:
+        for k in range(N):
+            if core == helper_of(k, T, topo):
+                helper_program(g, core, k, T, topo)
         return
     eng = {"v": g.vector, "a": g.scalar, "p": g.tensor, "g": g, "s": g.sync}
     cnt = {"v": 0, "a": 0, "p": 0, "g": 0}
@@ -87,8 +134,6 @@ def rank_program(g, core, T, topo):
     def span(x):
         if isinstance(x, str):
             x = (x, 0, SCRATCH[x][1][1])
-        if x[0] in PSUM:
-            return x[0], 0, 512, ALL
         return x if len(x) == 4 else x + (ALL,)
 
     def wait(q, ev):
@@ -111,16 +156,17 @@ def rank_program(g, core, T, topo):
         for x, wr in [(x, False) for x in R] + [(x, True) for x in W]:
             n, lo, hi, ch = span(x)
             for r in rec.get(n, []):
-                if r[0] < hi and lo < r[1] and r[5] & ch and (wr or r[3]):
-                    if r[4] == src and src == "p":
-                        continue
+                meet = r[0] < hi and lo < r[1] and r[5] & ch
+                if r[4] == src:
+                    must = meet and (wr or r[3]) and src != "p"
+                else:
+                    must = n in PSUM or (meet and (wr or r[3]))
+                if must:
                     need[r[2][0]] = max(need.get(r[2][0], 0), r[2][1])
         for s in need:
             wait(q, (s, need[s]))
 
     def op(q, fn, R, W, inc=True):
-        W = list(W) + [x for x in R if span(x)[0] in PSUM]
-        R = [x for x in R if span(x)[0] not in PSUM]
         deps(q, q, R, W)
         ins = fn()
         if inc:
@@ -137,20 +183,24 @@ def rank_program(g, core, T, topo):
         eng[q].dma_start(out, in_).then_inc(T.sem[s], 16)
         note((s, 16), s, R, W)
 
-    reach = [topo.engines(core, T.cores[(rank + d) % N]) for d in range(1, N)]
-    engs = [e for e in reach[0] if all(e in x for x in reach)]
+    engs = far_engines(core, rank, T, topo)
+    aide = helper_of(rank, T, topo)
+    near = [e for e in topo.engines(core, aide) if e not in engs]
     ne = len(engs)
 
-    def send(src, dst_of, arr, loc, step, land, freed=()):
+    def send(src, ds, dst_of, arr, loc, step, land, freed=(), relay=None):
         deps("g", loc, [src], list(freed))
-        ids = []
-        for d in range(1, N):
-            rid, pid = topo.addr(T.cores[(rank + step * d) % N])[:2]
-            ids.append(DstId(rid=rid, pnc=pid))
-        g.remote_dma_fused([RemoteDMATransfer(dst_ids=ids, dma_engine_mask=sum(1 << e for e in engs), remote_sem=T.sem[arr],
-                                              src=ap(src), dsts=[dst_of(d) for d in range(1, N)])], local_sem=T.sem[loc])
-        note((loc, ne), loc, [src], [])
+        parts = [transfer(topo, [T.cores[(rank + step * d) % N] for d in ds], engs, T.sem[arr], ap(src), [dst_of(d) for d in ds])] if ds else []
+        if relay is not None:
+            parts.append(transfer(topo, [aide], near, T.sem[relay[0]], ap(src), [relay[1]]))
+        g.remote_dma_fused(parts, local_sem=T.sem[loc])
+        note((loc, (ne if ds else 0) + (len(near) if relay else 0)), loc, [src], [])
         note((arr, ne * (N - 1)), arr, [], land)
+
+    def show(k, r, land):
+        src = ("PAY", GH * k, GH * k + GH)
+        relay = ("h%d%d" % (k, r), relay_place(T, k, r)) if len(DIRECT[r][k]) < N - 1 else None
+        send(src, DIRECT[r][k], lambda d: ghost_place(T, k, d), "a%d%d" % (k, r), "l%d%d" % (k, r), 1, [land], relay=relay)
 
     def ap(x):
         n, lo, hi = (x, 0, SCRATCH[x][1][1]) if isinstance(x, str) else x[:3]
@@ -186,9 +236,9 @@ def rank_program(g, core, T, topo):
     def put(win, lst, src):
         op("v", lambda: g.vector.tensor_copy(ap(win).indirect(ap(lst)), ap(src)), [src, lst], [win])
 
-    def mm(out, lhs, rhs, start, stop, rap=None):
+    def mm(out, lhs, rhs, start, stop, rap=None, inc=False):
         r = ap(rhs) if rap is None else rap
-        op("p", lambda: g.tensor.matmul(ap(out), ap(lhs), r, start, stop), [lhs, rhs], [out], inc=stop)
+        op("p", lambda: g.tensor.matmul(ap(out), ap(lhs), r, start, stop), [lhs, rhs], [out], inc=stop or inc)
 
     def lin(out, terms):
         for k, (lhs, rhs) in enumerate(terms):
@@ -235,51 +285,47 @@ def rank_program(g, core, T, topo):
     QG, RG = ("BIG", Q0 + E, Q0 + P), ("BIG", R0 + E, R0 + P)
     tab = mean_table()
 
-    def product(step, i):
-        blk = (256 * i, 256 * i + 256)
-        ts(upto("PT"), "C", 0.25 * ((i - step) % 4), OP.is_equal)
-        tt(("MK",) + blk, upto("PT"), ("CI",) + blk, OP.mult)
+    def products(step, pair):
+        for i in pair:
+            ts(("PT", 256 * (i % 2), 256 * (i % 2) + 256), "C", 0.25 * ((i - step) % 4), OP.is_equal)
+        for i in pair:
+            h = (256 * (i % 2), 256 * (i % 2) + 256)
+            tt(("MK",) + h, ("PT",) + h, ("CI", 256 * i, 256 * i + 256), OP.mult)
 
-    def chosen(i):
-        mm(SL, IDF, ("MK", 256 * i, 256 * i + 256), i == 0, i == 3)
+    def chosen(pair):
+        for i in pair:
+            mm(SL, IDF, ("MK", 256 * (i % 2), 256 * (i % 2) + 256), i == 0, i == 3, inc=True)
 
-    def channels():
+    def digits():
         cp("BI", SL)
         tt("SELF", SL, "EN", OP.is_equal)
         ts("J1", "BI", 4, OP.arith_shift_right)
+
+    def channels():
         ts("J2", "BI", 15, OP.bitwise_and)
         ts(upto("AL0"), "J1", -256.0, OP.add)
         row_out("s", 1, 3, "AL0")
+        ts("J1", "BI", 14, OP.bitwise_and)
         cp(upto("AL1"), "J2")
         row_out("s", 1, 6, "AL1")
         lin(upto("SW"), [(ID, upto("AL0")), ("IBW", upto("AL1"))])
-
-    def lookup(other):
-        ts("J1", "BI", 14, OP.bitwise_and)
-        ts("LB", upto("SW"), 256.0, OP.add)
         ts(upto("PT"), "J1", 2.0, OP.mult, 1.0, OP.add)
+
+    def other_end(other):
         tt(other, upto("PT"), upto("AL1"), OP.subtract)
 
     def stamps(r):
-        act("STB", ("XC", 0, 8 * (256 - CA)), AF.Identity, scale=0.0, bias=STAMP[r])
-
-    def key_constants():
-        act("SWN", "SWB", AF.Identity, scale=-1.0)
-        act("SW16", "SWB", AF.Identity, scale=16.0)
-        act(("IW", 128, 256), ID, AF.Copy)
-        act("IN", ("IW", 0, 160), AF.Identity, scale=-1.0)
-        for n in ("IA", "IC", "ID15", "ID191"):
-            act(n, ID, AF.Identity, scale=DIAG[n])
+        act("STB", ("XC", 0, NST), AF.Identity, scale=0.0, bias=STAMP[r])
 
     def vote_constants():
-        act("ZC", "ZC", AF.Identity, scale=-K)
-        act(("DUM", 0, CA), ("EW", 0, CA), AF.Identity, bias=float(E + KEYS))
-        act(("DUM", CA, 256), ("EW", CA, 256), AF.Identity, bias=float(E + KEYS - 16 * CA))
+        dma("s", T.P2[:, E // 2:E], T.XC[:, 0:E // 2], [("XC", 0, E // 2)], [("P2", E // 2, E)])
         act("STF", ("XC", 0, 4 * CA), AF.Silu, scale=0.0, bias=1e20)
 
     def cut_constants():
-        act("IM", ID, AF.Identity, scale=DIAG["IM"])
-        act("DH", ("EW", 0, 32), AF.Identity, bias=float(E + ES))
+        act("ZC", "ZC", AF.Identity, scale=-K)
+        act(("DUM", 0, CA), ("EW", 0, CA), AF.Identity, bias=float(E + KEYS))
+        act(("DUM", CA, 256), ("EW", CA, 256), AF.Identity, bias=float(E + KEYS - 16 * CA))
+        act("DH", ("EW", 0, 32), AF.Identity, bias=float(2 * E))
         act("YT", "YT", AF.Identity, scale=0.5)
 
     def table_scales():
@@ -288,9 +334,7 @@ def rank_program(g, core, T, topo):
             act(("RT", t[0], t[-1] + 1), ("RT", t[0], t[-1] + 1), AF.Identity, scale=2.0 ** -e)
 
     def shown_lists():
-        cp("SG", "SH")
-        lin(("PT", 16, 32), [("SWN", "SG")])
-        ts("SA", ("PT", 16, 32), -1.0, OP.mult)
+        ts("SA", ("CG", 0, 16), -1.0, OP.mult)
         ts("SB", "SA", 4, OP.arith_shift_right)
         ts("SF", "SA", float(BW), OP.mult)
         ts("SG", "SB", -float(P - 1), OP.mult)
@@ -310,20 +354,24 @@ def rank_program(g, core, T, topo):
         else:
             dma("s", ap(big(A0, c0, c1)), ap(a), [a], [big(A0, c0, c1)])
 
-    def shared(win, lst, share):
-        for c0, c1 in CH:
-            gv(("P1", 16 * c0, 16 * (c0 + share)), win, (lst, c0, c0 + share))
-            ga(("P1", 16 * (c0 + share), 16 * c1), win, (lst, c0 + share, c1))
+    def shared(win, lst, share, qs=range(4)):
+        for q in qs:
+            c0, c1 = CH[q]
+            c = c0 + share[q]
+            if c > c0:
+                gv(("P1", 16 * c0, 16 * c), win, (lst, c0, c))
+            ga(("P1", 16 * c, 16 * c1), win, (lst, c, c1))
 
     dma("s", T.BI[:], T.cur0[:], [], ["BI"])
     dma("a", T.CI[:, 0:512], T.cand[:, 0:512], [], [("CI", 0, 512)])
     dma("s", T.CI[:, 512:1024], T.cand[:, 512:1024], [], [("CI", 512, 1024)])
-    dma("a", T.CO[:], T.cov[:], [], ["CO"])
+    COV = ("P2", 0, E // 2)
+    dma("s", ap(COV), T.cov[:], [], [COV])
     dma("s", T.SH[:], T.shown[:], [], ["SH"])
     gi(("COLI", 0, 1), T.COLI[:, 0:1], [[0, 1]], 0, 1, False)
     gi("CB", T.CB[:], [[0, 128]], 1, 0)
     gs(("IB", 0, 128), T.IB[:, 0:128], "CB", T.CB[:], [[-1, 128]], OP.is_equal, 0.0, 0, 1)
-    gi("T3", T.T3[:], [[16, 256]], -E, 0)
+    gi("T1", T.T1[:], [[16, 256]], -E, 0)
     gs(("IB", 128, 256), T.IB[:, 128:256], "CB", T.CB[:], [[-1, 128]], OP.is_equal, 0.0, 0, 1)
     picker("ZA", {3: 16.0, 6: 1.0, 7: 2.0 * E})
     gs("SWB", T.SWB[:, 0:128:2], "CB", T.CB[:, 0:64], [[-2, 64]], OP.is_equal, 0.0, -1, 1)
@@ -336,31 +384,41 @@ def rank_program(g, core, T, topo):
     gs("ZC", T.ZC[:, 0:144:16], "CB", T.CB[:, 0:9], [[-16, 9]], OP.is_ge, 0.0, 16, 1)
     gs("ZC", T.ZC[:, 0:144:16], "ZC", T.ZC[:, 0:144:16], [[16, 9]], OP.is_ge, 0.0, -1, -1)
     picker("ZH", {ch: 1.0 for ch in range(16) if ch % 4 < 2})
-    ms(NAMES, 0.0)
-    dma("a", T.W1[0:128:16, 0:KEYS], T.P0[:, P:P + KEYS // 16], [("P0", P, P + KEYS // 16)], ["W1"])
     ts(("COLI", 1, 2), ("COLI", 0, 1), 15, OP.bitwise_and)
+    cp(("COL", 0, 1), ("COLI", 1, 2))
+    ms(NAMES, 0.0)
     for n in ("AL0", "AL1", "TN0", "TN1", "NMV", "NGT"):
         ms((n, 256, BW), 0.0)
-    cp(("COL", 0, 1), ("COLI", 1, 2))
     ts("C", "BI", 0.25, OP.mult)
     act(IDF, ID, AF.Copy)
-    act("EW", "T3", AF.Identity, bias=T.COL[:, 0:1], extra=[("COL", 0, 1)])
-    act("EN", "EW", AF.Identity, bias=float(E))
-    for n in ("IBW", "IK", "I16", "IP"):
+    for n in DIAG:
         act(n, ID, AF.Identity, scale=DIAG[n])
-    for i in range(4):
-        product(0, i)
-        chosen(i)
-    for h in range(2):
-        op("a", lambda h=h: g.scalar.activation(T.XB[:, h:E:2], T.CO[:], AF.Identity, bias=-127.5), ["CO"], [("XB", 0, E)])
-    channels()
-    lookup(upto("DLO"))
+    act("EW", "T1", AF.Identity, bias=T.COL[:, 0:1], extra=[("COL", 0, 1)])
+    act("EN", "EW", AF.Identity, bias=float(E))
+    act("SWN", "SWB", AF.Identity, scale=-1.0)
+    act("SW16", "SWB", AF.Identity, scale=16.0)
+    act(("IW", 128, 256), ID, AF.Copy)
+    act("IN", ("IW", 0, 160), AF.Identity, scale=-1.0)
+    dma("s", T.W1[0:128:16, 0:KEYS], T.P0[:, P:P + KEYS // 16], [("P0", P, P + KEYS // 16)], ["W1"])
     row_out("s", 1, 1, "ON")
-    dma("s", T.P0[:, P // 2:P], T.P0[:, P:P + P // 2], [("P0", P, P + P // 2)], [("P0", P // 2, P)])
-    act(upto("TB0"), upto("AL0"), AF.Copy)
-    for h in range(2):
-        op("a", lambda h=h: g.scalar.activation(T.XC[:, h:E // 2:2], T.CO[:, 0:E // 4], AF.Identity, bias=-127.5), ["CO"], [("XC", 0, E // 2)])
+    for pair in ((0, 1), (2, 3)):
+        products(0, pair)
+        chosen(pair)
     ms(("XB", E, ES), 0.0)
+    ms(("P0", 0, P // 4), 0.0)
+    for c0, c1 in ((0, E // 2), (E // 2, E)):
+        for h in range(2):
+            op("a", lambda h=h: g.scalar.activation(T.XB[:, c0 + h:c1:2], T.P2[:, c0 // 2:c1 // 2], AF.Identity, bias=-127.5), [COV], [("XB", c0, c1)])
+        c1 += ES - E if c0 else 0
+        dma("g", T.XC[:, c0:c1], T.XB[:, c0:c1], [("XB", c0, c1)], [("XC", c0, c1)])
+    digits()
+    channels()
+    cp("SG", "SH")
+    lin(("CG", 0, 16), [("SWN", "SG")])
+    ts("LB", upto("SW"), 256.0, OP.add)
+    other_end(upto("DLO"))
+    dma("s", T.P0[:, P // 4:P], T.P0[:, P:P + 3 * P // 4], [("P0", P, P + 3 * P // 4)], [("P0", P // 4, P)])
+    act(upto("TB0"), upto("AL0"), AF.Copy)
     ms(("LK", 256, 258), 1.0)
     ts(("SF", 0, 2), ("EW", 0, 2), float(E + 1), OP.add, 31.0, OP.min)
     cp(("SA", 0, 2), ("SF", 0, 2))
@@ -370,9 +428,7 @@ def rank_program(g, core, T, topo):
         cp((n, 256, 258), ("SB", 0, 2))
     for n in ("TN1", "DLO"):
         cp((n, 256, 258), ("SA", 2, 4))
-    gcopy(("XC", E // 2, 3 * E // 4), ("XB", E // 2, 3 * E // 4))
-    gcopy(("XC", 3 * E // 4, ES), ("XB", 3 * E // 4, ES))
-    ms(("P0", 0, P // 2), 0.0)
+    shown_lists()
     for t in range(32):
         gi(("RT", t, t + 1), T.RT[:, t:t + 1], [[0, 1]], tab[32 - t][0], 0)
 
@@ -390,13 +446,16 @@ def rank_program(g, core, T, topo):
         for q, (c0, c1) in enumerate(CH):
             extract((BK[q // 2], c0 % 128, c0 % 128 + 64), "P1", c0, c1, "ZA", start=False, stop=q % 2 == 1)
         if r == 0:
-            key_constants()
+            cut_constants()
         act("SN", upto("TB0"), AF.Sign, bias=0.5)
         for h, (c0, c1) in enumerate(HALF):
             lk = (BK[h], 128, 256)
             tt(lk, (BK[h], 0, 128), ("EW", c0, c1), OP.is_equal)
             if r > 0:
+                moved = ("PT", c0, c1)
+                tt(moved, ("PT", 256 + c0, 256 + c1), ("DC", c0, c1), OP.mult)
                 tt(lk, lk, ("NMV", c0, c1), OP.max)
+                tt(("C", c0, c1), moved, ("C", c0, c1), OP.add)
             tt(("TN0", c0, c1), lk, ("TB0", c0, c1), OP.mult)
             tt(("TN1", c0, c1), lk, ("DLO", c0, c1), OP.mult)
             cp(("LK", c0, c1), lk)
@@ -411,7 +470,6 @@ def rank_program(g, core, T, topo):
         lin(SL, [("IC", "C"), ("ID15", upto("TB0")), ("ID191", upto("DLO")), ("IK", "SN")])
         act("T1", SL, AF.Relu, bias=G0 + E - K)
         lin(SL, [("IA", "C"), ("I16", upto("TB0")), (ID, upto("DLO")), (("IN", 0, 128), "T1")])
-        act("KEY", SL, AF.Identity, bias=float(G0 + E))
 
         def first(q):
             c0, c1 = CHS[q]
@@ -422,8 +480,6 @@ def rank_program(g, core, T, topo):
         ts(("L0", 128, 258), ("X3", 0, 130), float(E), OP.add)
         first(0)
         ts("LS", upto("CG", 258), 256.0 + P, OP.add)
-        if r == 0:
-            shown_lists()
         first(1)
         lin(upto("SW"), [("SW16", upto("TB0")), ("SWB", upto("DLO"))])
         first(2)
@@ -449,11 +505,11 @@ def rank_program(g, core, T, topo):
                 extract((BK[q], 0, c1 - c0), pout, c0, c1)
 
             if s == 1:
-                mm(upto("CG"), "I16", upto("LK"), True, False)
+                mm(("SL", 256, 512), "I16", upto("LK"), True, False)
             if s == 5:
                 ga("PS", ("P0", 0, ES), "LW")
                 extract(("CG", 0, 32), "PS", 0, 32)
-                ga("PG", S16, "LW")
+                ga(("P1", 0, 512), ("P0", 0, ES), ("L4", 0, 32))
             for q, (c0, c1) in enumerate(CHS if s < 5 else CH):
                 if s > 1:
                     if (s, q) == (2, 0):
@@ -462,36 +518,35 @@ def rank_program(g, core, T, topo):
                         offs(s - 1, q + 1)
                     elif s < 5:
                         offs(s, 0)
-                    if (s, q) == (5, 1):
+                    if (s, q) == (5, 2):
                         ts("LX", ("CG", 0, 32), float(E), OP.add)
                         ga("PS", ("P0", 0, ES), "LX")
                         extract(("CG", 0, 32), "PS", 0, 32)
-                        pointers(1)
-                    if (s, q) == (5, 2):
-                        gt("PH", S16, "LX", "PG", OP.add)
-                    if (s, q) == (5, 3):
+                        gv("PG", S16, "LW")
+                        gt("MK", S16, "LX", "PG", OP.add)
                         ts("LY", ("CG", 0, 32), 0.0, OP.max)
-                        gt("PG", "RT", "LY", "PH", OP.mult)
-                        pointers(2)
+                        gt("PG", "RT", "LY", "MK", OP.mult)
+                        ga(("P1", 512, 1024), ("P0", 0, ES), ("L4", 32, 64))
+                        extract(("X0", 0, 64), "P1", 0, 64)
                         lin(upto("SW"), [(("IW", 32, 160), upto("PG"))])
+                        pointers(1)
                         act(upto("PAY"), upto("SW"), AF.Copy)
-                        send(upto("PAY"), lambda d: T.BIG[:, Q0 + E + GH * (d - 1):Q0 + E + GH * d], "ac%d" % r, "lc%d" % r, 1, [QG])
+                        show(0, r, QG)
                         lin(upto("CG"), [(("IW", 32, 160), ("PG", 256, 512)), (("IN", 32, 160), upto("PG"))])
-                        pointers(3)
+                        pointers(2)
                         act(("PAY", 256, 512), upto("CG"), AF.Abs)
-                        send(("PAY", 256, 512), lambda d: T.BIG[:, R0 + E + GH * (d - 1):R0 + E + GH * d], "ar%d" % r, "lr%d" % r, 1, [RG])
+                        show(1, r, RG)
+                        pointers(3)
                     gt(big(dst, c0, c1) if s < 5 else sums(c0, c1), ("BIG", src, src + ES), (lst, c0, c1), big(A0, c0, c1), OP.add)
                     if s < 5:
                         keep(q, dst)
-                if s < 5 or q == 0:
+                if s < 5:
                     pointers(q)
                 if s == 1:
-                    extract(("CG",) + CH[q], "P1", CH[q][0], CH[q][1], "ZG", start=False, stop=q == 3)
+                    extract(("SL", 256 + CH[q][0], 256 + CH[q][1]), "P1", CH[q][0], CH[q][1], "ZG", start=False, stop=q == 3)
             if s == 1:
                 ga(upto("PS"), ("P0", 0, P), "SS")
                 extract(("PT", 32, 48), "PS", 0, 16)
-            if s == 2:
-                act("GT", upto("CG"), AF.Identity, bias=8.5)
             if s == 3:
                 ts("SF", ("PT", 32, 48), 0.0, OP.is_ge)
                 ts("SG", ("PT", 32, 48), float(E), OP.add)
@@ -511,17 +566,20 @@ def rank_program(g, core, T, topo):
                 gcopy(big(S1, c0, c1), big(Q0, c0, c1))
             else:
                 dma("s", ap(big(S1, c0, c1)), ap(big(Q0, c0, c1)), [big(Q0, c0, c1)], [big(S1, c0, c1)])
-            if (q, r) == (1, 0):
-                vote_constants()
+            if q == 1:
+                act("GT", ("SL", 256, 512), AF.Identity, bias=8.5)
+                act("KEY", SL, AF.Identity, bias=float(G0 + E))
+                if r == 0:
+                    vote_constants()
 
         def margin(c0, c1):
             act(big(A0, c0, c1), big(R0, c0, c1), AF.Identity, bias=MARGIN)
 
+        ts("DC", "C", 0.6, OP.is_lt, 0.75, OP.subtract)
         for q, (c0, c1) in enumerate(C1):
             gt(big(S1, c0, c1), QA, ("LU", c0, c1), big(S1, c0, c1), OP.subtract)
             act(big(R0, c0, c1), big(S1, c0, c1), AF.Abs)
-            if q == 1:
-                margin(*C2[0])
+        ts(big(A0, *C2[0]), big(R0, *C2[0]), MARGIN, OP.add)
         for c in C2[1:]:
             margin(*c)
         act("TU", upto("LK"), AF.Identity, scale=-stamp, bias=stamp)
@@ -529,96 +587,102 @@ def rank_program(g, core, T, topo):
             stamps(0)
 
         def offsets(bank, c0, c1):
-            t = (bank, 256, 256 + c1 - c0)
-            tt(t, (bank, 0, c1 - c0), ("KEY", c0, c1), OP.max)
-            tt(t, t, ("DUM", c0, c1), OP.min)
-            cp(("LC", c0, c1), t)
+            halves = [(c0, (c0 + c1) // 2), ((c0 + c1) // 2, c1)]
+            for a, b in halves:
+                tt((bank, 256 + a - c0, 256 + b - c0), (bank, a - c0, b - c0), ("KEY", a, b), OP.max)
+            for a, b in halves:
+                tt((bank, 256 + a - c0, 256 + b - c0), (bank, 256 + a - c0, 256 + b - c0), ("DUM", a, b), OP.min)
+            for a, b in halves:
+                cp(("LC", a, b), (bank, 256 + a - c0, 256 + b - c0))
 
         def sums_out(c0, c1):
             gt(sums(c0, c1), "YT", ("LT", c0, c1), sums(c0, c1), OP.add)
             dma("a", T.ys[:, 16 * c0:16 * c1], T.XB[:, 16 * c0:16 * c1], [sums(c0, c1)], [])
 
         for q, (c0, c1) in enumerate(C2):
-            bank, b0, b1 = ("X0", 0, CA) if q < 3 else ("X1", CA, 256)
-            if q in (0, 3):
+            bank, b0, b1 = ("X0", 0, 192) if q < 4 else ("X1", 192, 256)
+            if q in (0, 4):
                 mm((bank, 0, b1 - b0), "IK", ("GT", b0, b1), True, False)
             gt(("P1", 16 * c0, 16 * c1), RA, ("LU", c0, c1), big(A0, c0, c1), OP.is_gt)
-            extract((bank, c0 - b0, c1 - b0), "P1", c0, c1, "ZC", 1, False, q in (2, 5))
+            extract((bank, c0 - b0, c1 - b0), "P1", c0, c1, "ZC", 1, False, q in (3, 5))
             if q == 4:
-                offsets("X0", 0, CA)
-        ts("DC", "C", 0.6, OP.is_lt, 0.75, OP.subtract)
-        if not last:
-            product(1, 0)
-            chosen(0)
-        offsets("X1", CA, 256)
+                offsets("X0", 0, 192)
         for k in range(4):
             c0 = k * CA // 4
             op("a", lambda c0=c0: g.scalar.activation(T.BIG[:].indirect(T.LC[:, c0:c0 + CA // 4]), T.STF[:], AF.Silu),
                ["STF", ("LC", c0, c0 + CA // 4)], ["BIG"])
         dma("a", T.WG2[:], T.BIG[0:128:16, 0:G0], [("BIG", 0, G0)], ["WG2"])
         dma("g", T.P0[1:128:4, 0:E], T.BIG[0:128:16, G0:KEYS], [("BIG", G0, KEYS)], [("P0", 0, E, 0x2222)])
-        hw = (256 - CA) // 2
-        for c0 in (CA, CA + hw):
-            put("W1", ("LC", c0, c0 + hw), "STB")
+        dma("a", T.P2[1:128:4, 0:E], T.P0[1:128:4, 0:E], [("P0", 0, E, 0x2222)], [("P2", 0, E, 0x2222)])
+        put("W1", ("LC", CA, 192), ("STB", 0, 16 * (192 - CA)))
+        offsets("X1", 192, 256)
+        put("W1", ("LC", 192, 256), ("STB", 0, 1024))
         dma("s", T.WG1[:], T.W1[0:128:16, 0:G0], [("W1", 0, G0)], ["WG1"])
-        dma("s", T.P0[0:128:4, 0:E], T.W1[0:128:16, G0:KEYS], [("W1", G0, KEYS)], [("P0", 0, E, 0x1111)])
-        if r == 0:
-            cut_constants()
+        for n in ("P0", "P2"):
+            dma("s", T[n][0:128:4, 0:E], T.W1[0:128:16, G0:KEYS], [("W1", G0, KEYS)], [(n, 0, E, 0x1111)])
         if last:
-            sums_out(0, 64)
-            sums_out(64, 96)
+            sums_out(0, 96)
         else:
-            for i in range(1, 4):
-                product(1, i)
-                chosen(i)
+            products(1, (0, 1))
+            chosen((0, 1))
+            products(1, (2, 3))
         for k in range(4):
             mm(("CG", 0, 48), ("IW", 96, 224), ("WG2", 48 * k, 48 * k + 48), k == 0, False)
         for k in range(4):
             mm(("CG", 0, 48), ("IB", 96, 224), ("WG1", 48 * k, 48 * k + 48), False, k == 3)
         ts("HG", ("CG", 0, 48), thr, OP.is_ge, -1.0, OP.mult)
-        send("HG", lambda d: T.RH[:, (3 * r + d - 1) * 48:(3 * r + d) * 48], "ah%d" % r, "lh%d" % r, -1, [("RH", 144 * r, 144 * r + 144)], [QG, RG])
+        send("HG", range(1, N), lambda d: T.RH[:, (3 * r + d - 1) * 48:(3 * r + d) * 48], "ah%d" % r, "lh%d" % r, -1, [("RH", 144 * r, 144 * r + 144)], [QG, RG])
         if last:
-            sums_out(96, 128)
+            sums_out(96, 144)
+            act("KEY", "C", AF.Identity, scale=4.0)
+            act("T1", "DC", AF.Identity, scale=4.0)
         else:
-            channels()
+            chosen((2, 3))
         mm(("X2", 0, 32), IDF, "DH", True, False)
         mm(upto("X0"), ID, "TU", True, False)
+
+        def partners(q, stop=False):
+            extract(("X0",) + CH[q], "P1", CH[q][0], CH[q][1], "ZH", start=False, stop=stop)
+
         shared(("P0", 0, ES), "L0", SHARE_H)
-        for c0, c1 in CH[:2]:
-            extract(("X0", c0, c1), "P1", c0, c1, "ZH", start=False, stop=False)
+        partners(0)
         b = 144 * r
         for h in range(2):
             for d in range(3):
                 mm(("X2", 16 * h, 16 * h + 16), "IK", ("RH", b + 64 * d, b + 64 * d + 16), False, (h, d) == (1, 2))
-        for c0, c1 in CH[2:]:
-            extract(("X0", c0, c1), "P1", c0, c1, "ZH", start=False, stop=False)
-        if not last:
-            lin(upto("CG"), [(ID, upto("AL0")), ("IM", upto("TB0"))])
-            act("D0", upto("CG"), AF.Copy)
-        tt("TH", ("X2", 0, 32), "KH", OP.max)
-        cp("LH", "TH")
+        partners(1)
+        partners(2)
+        partners(3)
         for c0 in (0, 16):
-            put(("P0", 0, P), ("LH", c0, c0 + 16), upto("STB"))
-        extract(upto("X0"), "P0", 0, 256, "ZH", 1, start=False)
+            tt(("TH", c0, c0 + 16), ("X2", c0, c0 + 16), ("KH", c0, c0 + 16), OP.max)
+        for c0 in (0, 16):
+            cp(("LH", c0, c0 + 16), ("TH", c0, c0 + 16))
+        for c0 in (0, 16):
+            put("P2", ("LH", c0, c0 + 16), upto("STB"))
+        extract(upto("X0"), "P2", 0, 256, "ZH", 1, start=False)
         if last:
-            ts("T2", "C", 4.0, OP.mult)
-            ts("T3", "DC", 4.0, OP.mult)
-            sums_out(128, 192)
+            sums_out(144, 256)
             ts(upto("PT"), upto("X0"), thr, OP.is_ge)
-            tt(upto("PT"), upto("PT"), "T3", OP.mult)
-            tt("T2", upto("PT"), "T2", OP.add)
-            dma("s", T.yc[:], T.T2[:], ["T2"], [])
-            sums_out(192, 256)
+            tt(upto("PT"), upto("PT"), "T1", OP.mult)
+            tt("KEY", upto("PT"), "KEY", OP.add)
+            dma("s", T.yc[:], T.KEY[:], ["KEY"], [])
         else:
             stamps(r + 1)
-            lookup("ALO")
-            tt("D1", "ALO", upto("DLO"), OP.subtract)
+            digits()
+            channels()
+            lin(upto("CG"), [(ID, upto("AL0")), ("IM", upto("TB0"))])
+            act("D0", upto("CG"), AF.Copy)
             ts(upto("NMV"), upto("X0"), thr, OP.is_lt)
             row_out("s", 1, 7, "NMV")
+            other_end("ALO")
+            lin(SL, [(ID, "ALO"), ("IM", upto("DLO"))])
+            act("D1", SL, AF.Copy)
             ts(("PT", 256, 512), upto("X0"), thr, OP.is_ge)
-            for d, cur in (("DC", "C"), ("D0", upto("TB0")), ("D1", upto("DLO"))):
-                tt(upto("PT"), ("PT", 256, 512), d, OP.mult)
-                tt(cur, upto("PT"), cur, OP.add)
+            ts("LB", upto("SW"), 256.0, OP.add)
+            tt(upto("PT"), ("PT", 256, 512), "D0", OP.mult)
+            tt(upto("X3"), ("PT", 256, 512), "D1", OP.mult)
+            tt(upto("TB0"), upto("PT"), upto("TB0"), OP.add)
+            tt(upto("DLO"), upto("X3"), upto("DLO"), OP.add)
 
     for s in total:
         if max([0] + [waited[k] for k in waited if k[1] == s]) < total[s]:

@@ -6,59 +6,70 @@ BW = P // 16
 ES = E + 32
 G0 = 4 * (P - E)
 KEYS = G0 + 4 * E
-CA = 120
-NST = 16 * max(192 - CA, 64)
-S0, S1, Q0, R0, A0, BIGW = 0, ES, 2 * ES, 2 * ES + P, 2 * ES + 2 * P, 3 * ES + 2 * P
+SC = [(0, 48), (48, 96), (216, 256), (192, 216)]
+VC = [(96, 128), (128, 160), (160, 192)]
+GR = [(0, 48), (48, 128), (128, 216), (216, 256)]
+NSA, NSV = 16 * max(b - a for a, b in SC), 16 * max(b - a for a, b in VC)
+SP = 112
+S0, S1, A0, PG0, Q0, BIGW = 0, ES, 2 * ES, 3 * ES, KEYS - E, KEYS + NSA + SP
 SCALE10 = 168199201
 MARGIN = 2.2
 K = 65536.0
+UNL = 8192.0
 STAMP = (1e10, 1e14, 1e18)
 NDMA = 80
 ALL = 0xFFFF
 CH = [(0, 64), (64, 128), (128, 192), (192, 256)]
 CHS = CH[:3] + [(192, 258)]
 HALF = [(0, 128), (128, 256)]
-C1 = [(0, 64), (64, 112), (112, 160), (160, 200), (200, 232), (232, 256)]
-C2 = [(0, 40), (40, 88), (88, 144), (144, 192), (192, 240), (240, 256)]
-SHARE_A, SHARE_H = (32, 32, 32, 32), (40, 40, 16, 0)
+LATE = (0, 2, 3, 1)
+C1 = [(0, 64), (128, 192), (192, 256), (64, 104), (104, 128)]
+SHARE_0, SHARE_A, SHARE_H = (32, 32, 32, 32), (32, 32, 32, 24), (0, 32, 40, 40)
+HELP, MV, MS = 0, 48, 48
+XA, XB, YA, PGS, SPLIT, QS, VADD = 128, 136, 192, 0, 3, 2, 1
+EARLYM, LATEM = {}, [(48, 112), (112, 180), (180, 256)]
+FLAG = 7
 
 F, B, I, U = "float32", "bfloat16", "int32", "uint16"
 SCRATCH = {
-    "BIG": ("sbuf", [128, BIGW], F), "W1": ("sbuf", [128, KEYS + 16 * (256 - CA)], B), "XB": ("sbuf", [128, ES], F),
-    "XC": ("sbuf", [128, ES], B), "P0": ("sbuf", [128, 2 * P], B), "P1": ("sbuf", [128, ES], B),
-    "WG1": ("sbuf", [128, 192], B), "WG2": ("sbuf", [128, 192], F),
-    "CI": ("sbuf", [128, 1024], I), "MK": ("sbuf", [128, 512], F), "P2": ("sbuf", [128, E + 512], B),
-    "STB": ("sbuf", [128, NST], B), "STF": ("sbuf", [128, 4 * CA], F),
-    "IW": ("sbuf", [128, 256], F), "IB": ("sbuf", [128, 256], B), "SWN": ("sbuf", [128, 128], F), "IN": ("sbuf", [128, 160], F),
-    "RT": ("sbuf", [128, 32], F), "YT": ("sbuf", [128, 32], F),
-    "RH": ("sbuf", [128, RO * 3 * 48], B), "HG": ("sbuf", [128, 48], B),
+    "BIG": ("sbuf", [128, BIGW], F), "RB": ("sbuf", [128, P], F), "MB": ("sbuf", [128, E], F),
+    "W1": ("sbuf", [128, KEYS + NSV + SP], B), "XB": ("sbuf", [128, ES], F),
+    "XC": ("sbuf", [128, ES], B), "P0": ("sbuf", [128, 2 * P + GH + SP], B), "P1": ("sbuf", [128, ES + GH + SP], B),
+    "WG1": ("sbuf", [128, 192], B), "CI": ("sbuf", [128, 1024], I), "STF": ("sbuf", [128, NSA], F), "STB": ("sbuf", [128, NSV], B),
+    "IW": ("sbuf", [128, 256], F), "IB": ("sbuf", [128, 256], B), "IN": ("sbuf", [128, 160], F),
+    "RT": ("sbuf", [128, 33], F), "YT": ("sbuf", [128, 33], F),
+    "RH": ("sbuf", [128, 3 * 48], B), "HG": ("sbuf", [128, 48], B),
     "COL": ("sbuf", [128, 8], F), "COLI": ("sbuf", [128, 8], I),
-    "LW": ("sbuf", [128, 32], U), "LX": ("sbuf", [128, 32], U), "LY": ("sbuf", [128, 32], U), "LH": ("sbuf", [128, 32], U), "SS": ("sbuf", [128, 16], U),
-    "PS": ("sbuf", [128, 512], B), "PG": ("sbuf", [128, 512], F), "PAY": ("sbuf", [128, 512], F),
-    "KH": ("sbuf", [128, 32], F), "DH": ("sbuf", [128, 32], F), "TH": ("sbuf", [128, 32], F),
+    "PS": ("sbuf", [128, 512], B), "SS": ("sbuf", [128, 16], U),
 }
+for _n in ("LW", "LX", "LY", "KU", "LH"):
+    SCRATCH[_n] = ("sbuf", [128, 32], U)
+SCRATCH["TH"] = ("sbuf", [128, 32], F)
+for _n in ("KB", "DB"):
+    SCRATCH[_n] = ("sbuf", [128, 64], F)
 for _n in ("SH", "SA", "SB"):
     SCRATCH[_n] = ("sbuf", [128, 16], I)
-for _n in ("SF", "SG", "SUM"):
+for _n in ("SF", "SG"):
     SCRATCH[_n] = ("sbuf", [128, 16], F)
-for _n in ("ZE", "ZA", "ZG", "ZC", "ZH"):
+for _n in ("ZE", "ZA", "ZB", "ZC", "ZH"):
     SCRATCH[_n] = ("sbuf", [128, 144], B)
-DIAG = {"I16": 16.0, "IBW": float(BW), "IK": K, "IP": -float(P), "IA": 4.0 * E, "IC": 4.0 * E - 192.0, "ID15": 15.0, "ID191": -191.0, "IM": -1.0}
-for _n in ("CB", "SWB", "SW16") + tuple(DIAG):
+DIAG = {"IK": K, "IBW": float(BW), "I16": 16.0}
+LATER = {"IA": float(E), "IC": E - 48.0, "ID15": 15.0, "ID191": -191.0, "IM": -1.0, "I8K": 8.5 * K, "I16K": 16 * K}
+SWAP = {"SW16": 16.0, "SWK": -UNL}
+for _n in ("CB", "SWB", "WD") + tuple(DIAG) + tuple(LATER) + tuple(SWAP):
     SCRATCH[_n] = ("sbuf", [128, 128], B)
-for _n in ("TN0", "TN1", "AL0", "AL1", "NMV", "NGT", "ON"):
+for _n in ("TH0", "TL0", "AL0", "AL1", "NMV"):
     SCRATCH[_n] = ("sbuf", [128, BW], B)
-for _n in ("TB0", "DLO", "LK"):
-    SCRATCH[_n] = ("sbuf", [128, 264], B)
-for _n in ("TU", "C", "DC", "ALO", "SELF", "D1", "GT", "SN"):
+for _n in ("H", "L", "EQ", "C", "SELF", "SN"):
     SCRATCH[_n] = ("sbuf", [128, 256], B)
-for _n in ("EW", "EN", "D0", "DUM", "KEY", "T1"):
+for _n in ("EW", "EN", "DUM", "KEY"):
     SCRATCH[_n] = ("sbuf", [128, 256], F)
-for _n in ("BI", "J1", "J2"):
-    SCRATCH[_n] = ("sbuf", [128, 256], I)
-for _n in ("L0", "L1", "L2", "L3", "L4", "LS"):
+SCRATCH["BI"] = ("sbuf", [128, 256], I)
+for _n in ("L0", "L1", "L2", "LS"):
     SCRATCH[_n] = ("sbuf", [128, 258], U)
-for _n in ("LT", "LB", "LU", "LC"):
+LEVEL = ("L0", "L1", "L2", "L1", "L2")
+LT, LC = "L1", "L2"
+for _n in ("LB", "LU"):
     SCRATCH[_n] = ("sbuf", [128, 256], U)
 PSUM = ("X0", "X1", "X2", "X3", "SW", "CG", "PT", "SL")
 for _n in PSUM:
@@ -95,8 +106,8 @@ def transfer(topo, cores, engines, sem, src, dsts):
 
 
 def ghost_place(T, k, d):
-    o = (Q0, R0)[k] + E + GH * (d - 1)
-    return T.BIG[:, o:o + GH]
+    o = (Q0, 0)[k] + E + GH * (d - 1)
+    return T[("BIG", "RB")[k]][:, o:o + GH]
 
 
 def relay_place(T, k, r):
@@ -176,11 +187,11 @@ def rank_program(g, core, T, topo):
         else:
             note(("c" + q, cnt[q] + 1), q, R, W)
 
-    def dma(q, out, in_, R, W):
+    def dma(q, out, in_, R, W, **how):
         s = "d%d" % nd[0]
         nd[0] += 1
         deps(q, s, R, W)
-        eng[q].dma_start(out, in_).then_inc(T.sem[s], 16)
+        eng[q].dma_start(out, in_, **how).then_inc(T.sem[s], 16)
         note((s, 16), s, R, W)
 
     engs = far_engines(core, rank, T, topo)
@@ -197,8 +208,13 @@ def rank_program(g, core, T, topo):
         note((loc, (ne if ds else 0) + (len(near) if relay else 0)), loc, [src], [])
         note((arr, ne * (N - 1)), arr, [], land)
 
+    PG, MK, PAY = [("BIG", PG0 + 512 * k, PG0 + 512 * k + 512) for k in range(3)]
+
+    def part(x, lo, hi):
+        return (x[0], x[1] + lo, x[1] + hi)
+
     def show(k, r, land):
-        src = ("PAY", GH * k, GH * k + GH)
+        src = part(PAY, GH * k, GH * k + GH)
         relay = ("h%d%d" % (k, r), relay_place(T, k, r)) if len(DIRECT[r][k]) < N - 1 else None
         send(src, DIRECT[r][k], lambda d: ghost_place(T, k, d), "a%d%d" % (k, r), "l%d%d" % (k, r), 1, [land], relay=relay)
 
@@ -240,15 +256,14 @@ def rank_program(g, core, T, topo):
         r = ap(rhs) if rap is None else rap
         op("p", lambda: g.tensor.matmul(ap(out), ap(lhs), r, start, stop), [lhs, rhs], [out], inc=stop or inc)
 
-    def lin(out, terms):
+    def lin(out, terms, start=True, stop=True):
         for k, (lhs, rhs) in enumerate(terms):
-            mm(out, lhs, rhs, k == 0, k == len(terms) - 1)
+            mm(out, lhs, rhs, start and k == 0, stop and k == len(terms) - 1)
 
-    def extract(out, row, c0, c1, Z="ZE", flip=0, start=True, stop=True):
+    def extract(out, row, c0, c1, Z="ZE", start=True, stop=True, step=1, first=0):
         for i in range(16):
-            j = i ^ flip
-            mm(out, (Z, 16 - j, 144 - j), (row, 16 * c0, 16 * c1), start and i == 0, stop and i == 15,
-               rap=T[row][:, 16 * c0 + i:16 * c1:16])
+            mm(out, (Z, 16 - i, 144 - i), (row, 16 * step * c0, 16 * step * c1), start and i == 0, stop and i == 15,
+               rap=T[row][:, step * (16 * c0 + i) + first:16 * step * c1:16 * step])
 
     def gi(out, oap, pat, base, cm, flt=True):
         if flt:
@@ -270,85 +285,94 @@ def rank_program(g, core, T, topo):
     def big(o, c0, c1):
         return ("BIG", o + 16 * c0, o + 16 * c1)
 
+    def row(n, c0, c1):
+        return (n, 16 * c0, 16 * c1)
+
     def upto(n, k=256):
         return (n, 0, k)
+
+    def upper(n):
+        return (n, 256, 512)
 
     def row_out(q, region, ch, tile):
         dma(q, T.P0[ch:128:16, region * P:(region + 1) * P], T[tile][:], [tile], [("P0", region * P, (region + 1) * P, 1 << ch)])
 
-    ID, IDF = ("IB", 0, 128), ("IW", 0, 128)
+    ID, IDF, INF = ("IB", 0, 128), ("IW", 0, 128), ("IN", 0, 128)
     SL = ("SL", 0, 256)
     NAMES = ("P0", P, 2 * P)
+    NAMESD = ("P0", P, 2 * P + GH + SP)
     BK = ["X0", "X1", "X2", "X3"]
     S16 = ("BIG", S1, S1 + ES)
-    QA, RA = ("BIG", Q0, Q0 + P), ("BIG", R0, R0 + P)
-    QG, RG = ("BIG", Q0 + E, Q0 + P), ("BIG", R0 + E, R0 + P)
+    QA = ("BIG", Q0, Q0 + P)
+    QG, RG = ("BIG", Q0 + E, Q0 + P), ("RB", E, P)
     tab = mean_table()
 
-    def products(step, pair):
-        for i in pair:
-            ts(("PT", 256 * (i % 2), 256 * (i % 2) + 256), "C", 0.25 * ((i - step) % 4), OP.is_equal)
-        for i in pair:
-            h = (256 * (i % 2), 256 * (i % 2) + 256)
-            tt(("MK",) + h, ("PT",) + h, ("CI", 256 * i, 256 * i + 256), OP.mult)
+    def cursors(cur, step, i):
+        ts(("PT", 256 * (i % 2), 256 * (i % 2) + 256), cur, float((i - step) % 4), OP.is_equal)
 
-    def chosen(pair):
-        for i in pair:
-            mm(SL, IDF, ("MK", 256 * (i % 2), 256 * (i % 2) + 256), i == 0, i == 3, inc=True)
+    def chosen(cur, step, done=0):
+        a, b, p0, p1 = upto("MB"), ("MB", 256, 512), upto("PT"), upper("PT")
+        for i in range(done, 2):
+            cursors(cur, step, i)
+        tt(a, p0, ("CI", 0, 256), OP.mult)
+        tt(p1, p1, ("CI", 256, 512), OP.mult)
+        cursors(cur, step, 2)
+        tt(b, p1, a, OP.add)
+        tt(p0, p0, ("CI", 512, 768), OP.mult)
+        cursors(cur, step, 3)
+        tt(a, p0, b, OP.add)
+        tt(p1, p1, ("CI", 768, 1024), OP.mult)
 
-    def digits():
-        cp("BI", SL)
+    def digits(region, channels, whole="BI"):
+        tt(SL, upper("PT"), upto("MB"), OP.add)
+        ts(whole, SL, -7.5 - E, OP.add, 1.0 / 16, OP.mult)
         tt("SELF", SL, "EN", OP.is_equal)
-        ts("J1", "BI", 4, OP.arith_shift_right)
+        ts("KEY", whole, -16.0, OP.mult, -float(E), OP.add)
+        cp(upto("AL0"), whole)
+        row_out("s", region, channels[0], "AL0")
+        tt(upto("AL1"), SL, "KEY", OP.add)
+        row_out("s", region, channels[1], "AL1")
 
-    def channels():
-        ts("J2", "BI", 15, OP.bitwise_and)
-        ts(upto("AL0"), "J1", -256.0, OP.add)
-        row_out("s", 1, 3, "AL0")
-        ts("J1", "BI", 14, OP.bitwise_and)
-        cp(upto("AL1"), "J2")
-        row_out("s", 1, 6, "AL1")
-        lin(upto("SW"), [(ID, upto("AL0")), ("IBW", upto("AL1"))])
-        ts(upto("PT"), "J1", 2.0, OP.mult, 1.0, OP.add)
-
-    def other_end(other):
-        tt(other, upto("PT"), upto("AL1"), OP.subtract)
+    def blocks():
+        lin(upper("SL"), [(ID, upto("AL0")), ("IBW", upto("AL1"))])
 
     def stamps(r):
-        act("STB", ("XC", 0, NST), AF.Identity, scale=0.0, bias=STAMP[r])
+        act("STF", ("XC", 0, NSA), AF.Silu, scale=0.0, bias=STAMP[r])
 
-    def vote_constants():
-        dma("s", T.P2[:, E // 2:E], T.XC[:, 0:E // 2], [("XC", 0, E // 2)], [("P2", E // 2, E)])
-        act("STF", ("XC", 0, 4 * CA), AF.Silu, scale=0.0, bias=1e20)
-
-    def cut_constants():
-        act("ZC", "ZC", AF.Identity, scale=-K)
-        act(("DUM", 0, CA), ("EW", 0, CA), AF.Identity, bias=float(E + KEYS))
-        act(("DUM", CA, 256), ("EW", CA, 256), AF.Identity, bias=float(E + KEYS - 16 * CA))
-        act("DH", ("EW", 0, 32), AF.Identity, bias=float(2 * E))
-        act("YT", "YT", AF.Identity, scale=0.5)
-
-    def table_scales():
-        for e in sorted(set(tab[m][1] for m in tab)):
-            t = [t for t in range(32) if tab[32 - t][1] == e]
-            act(("RT", t[0], t[-1] + 1), ("RT", t[0], t[-1] + 1), AF.Identity, scale=2.0 ** -e)
+    def reads(t):
+        return t if t else 32
 
     def shown_lists():
-        ts("SA", ("CG", 0, 16), -1.0, OP.mult)
-        ts("SB", "SA", 4, OP.arith_shift_right)
-        ts("SF", "SA", float(BW), OP.mult)
-        ts("SG", "SB", -float(P - 1), OP.mult)
-        ts("SB", "SA", 1, OP.bitwise_and)
-        tt("SF", "SF", "SG", OP.add)
-        ts("SG", "SB", -2.0, OP.mult, 1.0 - E, OP.add)
-        cp("SS", "SF")
-        tt("SUM", "SG", "SA", OP.add)
-        ts(("LW", 0, 16), "SUM", float(E), OP.add)
-        ts(("KH", 0, 16), "SUM", float(E), OP.add)
+        ts("SA", "SH", 15, OP.bitwise_and)
+        ts("SB", "SH", 4, OP.arith_shift_right)
+        cp(("LW", 0, 16), "SH")
+        ts("SF", "SA", float(BW), OP.mult, -256.0, OP.add)
+        ts(("KB", 0, 16), "SH", -float(E), OP.add)
+        ts("SA", "SH", 1, OP.bitwise_and)
+        tt(("KB", 32, 48), "SF", "SB", OP.add)
 
-    def keep(q, o):
-        c0, c1 = CHS[q]
+    def shown_places(k):
+        if k == 0:
+            ts("SG", "SA", -2.0 * BW, OP.mult, BW + 256.0, OP.add)
+            ts(("KU", 0, 16), ("KB", 32, 48), 256.0, OP.add)
+            tt("SF", ("KB", 32, 48), "SG", OP.add)
+        else:
+            cp("SS", "SF")
+
+    def stop_chain():
+        ts(("SF", 0, 2), ("EW", 0, 2), float(E - 1), OP.add, 0.0, OP.max)
+        cp(("SA", 0, 2), ("SF", 0, 2))
+        ts(("L0", 256, 258), ("SF", 0, 2), float(E), OP.add)
+        ts(("SB", 0, 2), ("SA", 0, 2), 4, OP.arith_shift_right)
+        ts(("SA", 2, 4), ("SA", 0, 2), 15, OP.bitwise_and)
+        cp(("TH0", 256, 258), ("SB", 0, 2))
+        cp(("TL0", 256, 258), ("SA", 2, 4))
+
+    def keep(q, o, end=258):
+        c0, c1 = CHS[q][0], min(CHS[q][1], end)
         a = big(o, c0, c1)
+        if c1 <= c0:
+            return
         if q % 2 == 0:
             gcopy(big(A0, c0, c1), a)
         else:
@@ -359,330 +383,430 @@ def rank_program(g, core, T, topo):
             c0, c1 = CH[q]
             c = c0 + share[q]
             if c > c0:
-                gv(("P1", 16 * c0, 16 * c), win, (lst, c0, c))
-            ga(("P1", 16 * c, 16 * c1), win, (lst, c, c1))
+                gv(row("P1", c0, c), win, (lst, c0, c))
+            ga(row("P1", c, c1), win, (lst, c, c1))
 
     dma("s", T.BI[:], T.cur0[:], [], ["BI"])
     dma("a", T.CI[:, 0:512], T.cand[:, 0:512], [], [("CI", 0, 512)])
     dma("s", T.CI[:, 512:1024], T.cand[:, 512:1024], [], [("CI", 512, 1024)])
-    COV = ("P2", 0, E // 2)
+    COV = ("W1", 0, E // 2)
     dma("s", ap(COV), T.cov[:], [], [COV])
     dma("s", T.SH[:], T.shown[:], [], ["SH"])
+    dma("s", T.P0[:, P - E // 2:P], T.cov[:], [], [("P0", P - E // 2, P)])
     gi(("COLI", 0, 1), T.COLI[:, 0:1], [[0, 1]], 0, 1, False)
     gi("CB", T.CB[:], [[0, 128]], 1, 0)
-    gs(("IB", 0, 128), T.IB[:, 0:128], "CB", T.CB[:], [[-1, 128]], OP.is_equal, 0.0, 0, 1)
-    gi("T1", T.T1[:], [[16, 256]], -E, 0)
-    gs(("IB", 128, 256), T.IB[:, 128:256], "CB", T.CB[:], [[-1, 128]], OP.is_equal, 0.0, 0, 1)
-    picker("ZA", {3: 16.0, 6: 1.0, 7: 2.0 * E})
+    for h in range(2):
+        gs(("IB", 128 * h, 128 * h + 128), T.IB[:, 128 * h:128 * h + 128], "CB", T.CB[:], [[-1, 128]], OP.is_equal, 0.0, 0, 1)
+    act("IW", "IB", AF.Copy)
+    gi("KEY", T.KEY[:], [[16, 256]], -E, 0)
     gs("SWB", T.SWB[:, 0:128:2], "CB", T.CB[:, 0:64], [[-2, 64]], OP.is_equal, 0.0, -1, 1)
     gs("SWB", T.SWB[:, 1:128:2], "CB", T.CB[:, 0:64], [[-2, 64]], OP.is_equal, 0.0, 0, 1)
-    gi("ON", T.ON[:], [[0, BW]], 1, 0)
     picker("ZE", {0: 16.0, 1: 1.0})
-    picker("ZG", {2: 16.0})
-    gi("YT", T.YT[:], [[-255, 32]], 255 * 32, 0)
-    gi("ZC", T.ZC[:], [[0, 144]], 0, 0)
-    gs("ZC", T.ZC[:, 0:144:16], "CB", T.CB[:, 0:9], [[-16, 9]], OP.is_ge, 0.0, 16, 1)
-    gs("ZC", T.ZC[:, 0:144:16], "ZC", T.ZC[:, 0:144:16], [[16, 9]], OP.is_ge, 0.0, -1, -1)
-    picker("ZH", {ch: 1.0 for ch in range(16) if ch % 4 < 2})
+    for t in (0, 16, 32) + tuple(range(1, 32, 2)):
+        gs(("RT", t, t + 1, 1), T.RT[:, t:t + 1], ("IW", 0, 1), T.IW[:, 0:1], [[0, 1]], OP.is_gt, tab[reads(t)][0] * 2.0 ** -tab[reads(t)][1], 0, 0)
     ts(("COLI", 1, 2), ("COLI", 0, 1), 15, OP.bitwise_and)
+    ms(("P0", 0, P - E // 2), 0.0)
     cp(("COL", 0, 1), ("COLI", 1, 2))
-    ms(NAMES, 0.0)
-    for n in ("AL0", "AL1", "TN0", "TN1", "NMV", "NGT"):
-        ms((n, 256, BW), 0.0)
-    ts("C", "BI", 0.25, OP.mult)
-    act(IDF, ID, AF.Copy)
     for n in DIAG:
         act(n, ID, AF.Identity, scale=DIAG[n])
-    act("EW", "T1", AF.Identity, bias=T.COL[:, 0:1], extra=[("COL", 0, 1)])
-    act("EN", "EW", AF.Identity, bias=float(E))
-    act("SWN", "SWB", AF.Identity, scale=-1.0)
-    act("SW16", "SWB", AF.Identity, scale=16.0)
-    act(("IW", 128, 256), ID, AF.Copy)
-    act("IN", ("IW", 0, 160), AF.Identity, scale=-1.0)
-    dma("s", T.W1[0:128:16, 0:KEYS], T.P0[:, P:P + KEYS // 16], [("P0", P, P + KEYS // 16)], ["W1"])
-    row_out("s", 1, 1, "ON")
-    for pair in ((0, 1), (2, 3)):
-        products(0, pair)
-        chosen(pair)
+        if n == "IK":
+            act("EW", "KEY", AF.Identity, bias=T.COL[:, 0:1], extra=[("COL", 0, 1)])
+            act("EN", "EW", AF.Identity, bias=float(E))
+    for n in SWAP:
+        act(n, "SWB", AF.Identity, scale=SWAP[n])
+    act("IN", upto("IB", 160), AF.Identity, scale=-1.0)
+    for n in ("AL0", "AL1"):
+        ms((n, 256, BW), 0.0)
+    cp("C", "BI")
+    chosen("C", 0)
+    digits(0, (0, 1))
+    for n in ("TH0", "TL0", "NMV"):
+        ms((n, 256, BW), 0.0)
+    blocks()
     ms(("XB", E, ES), 0.0)
-    ms(("P0", 0, P // 4), 0.0)
+    ts("LB", upper("SL"), 256.0, OP.add)
     for c0, c1 in ((0, E // 2), (E // 2, E)):
         for h in range(2):
-            op("a", lambda h=h: g.scalar.activation(T.XB[:, c0 + h:c1:2], T.P2[:, c0 // 2:c1 // 2], AF.Identity, bias=-127.5), [COV], [("XB", c0, c1)])
+            op("a", lambda h=h: g.scalar.activation(T.XB[:, c0 + h:c1:2], T.W1[:, c0 // 2:c1 // 2], AF.Identity, bias=-127.5), [COV], [("XB", c0, c1, 1 << h)])
         c1 += ES - E if c0 else 0
-        dma("g", T.XC[:, c0:c1], T.XB[:, c0:c1], [("XB", c0, c1)], [("XC", c0, c1)])
-    digits()
-    channels()
-    cp("SG", "SH")
-    lin(("CG", 0, 16), [("SWN", "SG")])
-    ts("LB", upto("SW"), 256.0, OP.add)
-    other_end(upto("DLO"))
-    dma("s", T.P0[:, P // 4:P], T.P0[:, P:P + 3 * P // 4], [("P0", P, P + 3 * P // 4)], [("P0", P // 4, P)])
-    act(upto("TB0"), upto("AL0"), AF.Copy)
-    ms(("LK", 256, 258), 1.0)
-    ts(("SF", 0, 2), ("EW", 0, 2), float(E + 1), OP.add, 31.0, OP.min)
-    cp(("SA", 0, 2), ("SF", 0, 2))
-    ts(("SB", 0, 2), ("SA", 0, 2), 4, OP.arith_shift_right)
-    ts(("SA", 2, 4), ("SA", 0, 2), 15, OP.bitwise_and)
-    for n in ("TN0", "TB0"):
-        cp((n, 256, 258), ("SB", 0, 2))
-    for n in ("TN1", "DLO"):
-        cp((n, 256, 258), ("SA", 2, 4))
+        dma("g", T.XC[:, c0:c1], T.XB[:, c0:c1], [("XB", c0, c1), "LB"], [("XC", c0, c1)])
+    stop_chain()
     shown_lists()
-    for t in range(32):
-        gi(("RT", t, t + 1), T.RT[:, t:t + 1], [[0, 1]], tab[32 - t][0], 0)
+    picker("ZB", {0: 1.0, 1: float(BW)})
+    gi("DB", T.DB[:], [[P - 256 - (ES - E), 2], [0, 2], [16, 16]], ES - E, 1)
+
+    def even_means():
+        for k in (2, 4, 8):
+            op("v", lambda k=k: g.vector.tensor_scalar(T.RT[:, k:32:2 * k], T.RT[:, 1:32 // k:2], 1.0 / k, None, OP.mult), [("RT", 0, 33, 1)], [("RT", 0, 33, k)])
+
+    def cut_constants():
+        gi(upto("YT", 33), T.YT[:, 0:33], [[255, 33]], 0, 0)
+        gi(upto("YT", 1), T.YT[:, 0:1], [[0, 1]], 255 * 32, 0)
+        gi("ZC", T.ZC[:], [[0, 144]], 0, 0)
+        gi("ZC", T.ZC[:, 0:144:16], [[0, 9]], -int(K), 0)
+        gs("ZC", T.ZC[:, 0:144:16], "ZC", T.ZC[:, 0:144:16], [[-16, 9]], OP.is_ge, 0.0, 16, 1)
+        gs("ZC", T.ZC[:, 0:144:16], "ZC", T.ZC[:, 0:144:16], [[16, 9]], OP.is_ge, 0.0, -1, -1)
+        for c0, c1 in SC + VC:
+            gi(("DUM", c0, c1), T.DUM[:, c0:c1], [[16, c1 - c0]], KEYS, 1)
+        picker("ZH", {ch: 1.0 for ch in range(16) if ch % 4 < 2})
+        picker("ZA", {3: 16.0, 6: 1.0, FLAG: 2.0 * E})
+        dma("s", T.W1[0:128:16, 0:KEYS], T.XC[:, 0:KEYS // 16], [("XC", 0, KEYS // 16)], ["W1"])
+        for c0, c1 in ((P, P + E), (P + E, NAMESD[2])):
+            dma("s", T.P0[:, c0:c1], T.XC[:, 0:c1 - c0], [("XC", 0, c1 - c0)], [("P0", c0, c1)])
 
     for r in range(RO):
         last = r == RO - 1
         stamp = STAMP[r]
         thr = 0.4 * stamp
+        H, L = ("H", "L") if r else ("AL0", "AL1")
+        kept = ["NMV"] if r else []
 
         def sums(c0, c1):
-            return ("XB", 16 * c0, 16 * c1) if last else big(S0, c0, c1)
+            return row("XB", c0, c1) if last else big(S0, c0, c1)
+
+        def unlinked(h):
+            a, b = HALF[h]
+            lin((BK[2 + h], 0, 128), [("SW16", (H, a, b)), ("SWB", (L, a, b))] + [("SWK", (n, a, b)) for n in kept], stop=False)
+
+        def linked(h):
+            c0, c1 = HALF[h]
+            tt(("EQ", c0, c1), (BK[h], 0, 128), ("EW", c0, c1), OP.is_equal)
+            mm((BK[2 + h], 0, 128), "SWK", ("EQ", c0, c1), False, True)
+
+        def entries(h):
+            ts(("L0",) + HALF[h], (BK[2 + h], 0, 128), E + UNL, OP.add, E + 31.0, OP.min)
+
+        def first(c0, c1):
+            gt(big(S0, c0, c1), "XB", ("L0", c0, c1), row("XC", c0, c1), OP.add)
 
         for h, (c0, c1) in enumerate(HALF):
             mm((BK[h], 0, 128), "IK", ("SELF", c0, c1), True, False)
-        shared(NAMES, "LB", SHARE_A)
+        shared(NAMES if r else ("P0", 0, P), "LB", SHARE_A if r else SHARE_0)
+        if r > 0:
+            for n in (upto("PT"), upper("PT")):
+                tt(n, n, upto("NMV"), OP.mult)
+            tt("H", upto("PT"), upto("AL0"), OP.add)
+            tt("L", upper("PT"), upto("AL1"), OP.add)
         for q, (c0, c1) in enumerate(CH):
-            extract((BK[q // 2], c0 % 128, c0 % 128 + 64), "P1", c0, c1, "ZA", start=False, stop=q % 2 == 1)
+            extract((BK[q // 2], c0 % 128, c0 % 128 + 64), "P1", c0, c1, "ZA" if r else "ZE", start=False, stop=q % 2 == 1 and r == 0)
+            if q % 2 == 1 and r > 0:
+                mm((BK[q // 2], 0, 128), "IK", ("NMV",) + HALF[q // 2], False, True)
+        lin(upto("SW"), [("SWB", upto(L))])
+        lin(upto("CG"), [("SWB", upto(H))] + [("SWK", upto(n)) for n in kept], stop=False)
+        unlinked(0)
+        act(upto("TL0"), upto("SW"), AF.Copy)
+        row_out("s", 0, 1, "TL0")
+        linked(0)
+        ts("SN", upto(H), 0.0, OP.is_ge)
         if r == 0:
-            cut_constants()
-        act("SN", upto("TB0"), AF.Sign, bias=0.5)
-        for h, (c0, c1) in enumerate(HALF):
-            lk = (BK[h], 128, 256)
-            tt(lk, (BK[h], 0, 128), ("EW", c0, c1), OP.is_equal)
-            if r > 0:
-                moved = ("PT", c0, c1)
-                tt(moved, ("PT", 256 + c0, 256 + c1), ("DC", c0, c1), OP.mult)
-                tt(lk, lk, ("NMV", c0, c1), OP.max)
-                tt(("C", c0, c1), moved, ("C", c0, c1), OP.add)
-            tt(("TN0", c0, c1), lk, ("TB0", c0, c1), OP.mult)
-            tt(("TN1", c0, c1), lk, ("DLO", c0, c1), OP.mult)
-            cp(("LK", c0, c1), lk)
-            c2 = c1 + 2 * h
-            lin((BK[2 + h], 0, c2 - c0), [("I16", ("TN0", c0, c2)), (ID, ("TN1", c0, c2))])
-        row_out("s", 0, 0, "TN0")
-        row_out("s", 0, 1, "TN1")
-        lin(upto("SW"), [("SWB", upto("LK"))])
-        act(upto("NGT"), upto("SW"), AF.Identity, scale=-1.0, bias=1.0)
-        row_out("a", 1, 2, "NGT")
-        lin(upto("CG", 258), [(ID, upto("TB0", 258)), ("IBW", upto("DLO", 258)), ("IP", upto("LK", 258))])
-        lin(SL, [("IC", "C"), ("ID15", upto("TB0")), ("ID191", upto("DLO")), ("IK", "SN")])
-        act("T1", SL, AF.Relu, bias=G0 + E - K)
-        lin(SL, [("IA", "C"), ("I16", upto("TB0")), (ID, upto("DLO")), (("IN", 0, 128), "T1")])
+            even_means()
+        tt(("EQ", 128, 256), ("X1", 0, 128), ("EW", 128, 256), OP.is_equal)
+        mm(upto("CG"), "SWK", "EQ", False, True)
+        act(upto("TH0"), upto("CG"), AF.Identity, bias=UNL)
+        row_out("a", 0, 0, "TH0")
+        entries(0)
+        unlinked(1)
+        mm(("X3", 0, 128), "SWK", ("EQ", 128, 256), False, True)
+        lin(upto("SW", 258), [(ID, upto("TH0", 258)), ("IBW", upto("TL0", 258))])
+        first(0, 64)
+        keep(0, S0)
+        ts("LS", upto("SW", 258), 256.0, OP.add, 15.0 * BW + 257.0, OP.min)
+        entries(1)
+        if r > 0:
+            lin(upto("SL"), [(ID, "C"), ("IM", upto("NMV"))])
+            act("SELF", upto("SL"), AF.Sign, bias=-2.5)
+        lin(upto("PT"), [("I16", upto(H)), (ID, upto(L))])
+        if r > 0:
+            lin(upto("SL"), [(ID, "C"), ("IM", upto("NMV")), ("IM", "SELF"), ("IM", "SELF")])
+            act("C", upto("SL"), AF.Identity, bias=-1.0)
+        else:
+            for n in LATER:
+                act(n, ID, AF.Identity, scale=LATER[n])
 
-        def first(q):
-            c0, c1 = CHS[q]
-            gt(big(S0, c0, c1), "XB", ("L0", c0, c1), ("XC", 16 * c0, 16 * c1), OP.add)
+        for q in (1, 2, 3):
+            first(*CHS[q])
             keep(q, S0)
-
-        ts(("L0", 0, 128), ("X2", 0, 128), float(E), OP.add)
-        ts(("L0", 128, 258), ("X3", 0, 130), float(E), OP.add)
-        first(0)
-        ts("LS", upto("CG", 258), 256.0 + P, OP.add)
-        first(1)
-        lin(upto("SW"), [("SW16", upto("TB0")), ("SWB", upto("DLO"))])
-        first(2)
-        ts("LU", upto("SW"), float(E), OP.add)
-        first(3)
+            if q > 1 and r == 0:
+                shown_places(q - 2)
+            if q == 3:
+                ts("LU", upto("PT"), float(E), OP.add)
+        if r == 0:
+            dma("s", T.BIG[0:128:16, PG0 + 1536:Q0], T.XB[0:128:16, 0:Q0 - PG0 - 1536], [("XB", 0, Q0 - PG0 - 1536)], [("BIG", PG0 + 1536, Q0)])
 
         def offs(s, q):
             c0, c1 = CHS[q] if s < 5 else CH[q]
             if s < 5:
-                ts(("L%d" % s, c0, c1), (BK[q], 0, c1 - c0), float(E), OP.add)
+                ts((LEVEL[s], c0, c1), (BK[q], 0, c1 - c0), float(E), OP.add, E + 31.0, OP.min)
             else:
-                ts(("LT", c0, c1), (BK[q], 0, c1 - c0), 0.0, OP.max)
+                ts((LT, c0, c1), (BK[q], 0, c1 - c0), 1.0, OP.add, 32.0, OP.min)
 
         for s in range(1, 6):
             src = S0 if s % 2 == 0 else S1
             dst = S0 if s % 2 == 1 else S1
             pin, pout = ("P0", "P1") if s % 2 == 1 else ("P1", "P0")
-            lst = "L%d" % (s - 1)
+            lst = LEVEL[s - 1]
 
             def pointers(q):
                 c0, c1 = (CHS if s < 5 else CH)[q]
-                ga((pout, 16 * c0, 16 * c1), (pin, 0, 2 * P if s == 1 else ES), ("LS" if s == 1 else lst, c0, c1))
+                c = c0 + (HELP if (s, q) == (1, 1) else 0)
+                if c > c0:
+                    gv(row(pout, c0, c), (pin, 0, P), ("LS", c0, c))
+                if c < c1:
+                    ga(row(pout, c, c1), (pin, 0, P if s == 1 else ES), ("LS" if s == 1 else lst, c, c1))
                 extract((BK[q], 0, c1 - c0), pout, c0, c1)
 
-            if s == 1:
-                mm(("SL", 256, 512), "I16", upto("LK"), True, False)
-            if s == 5:
+            def double(c0, c1):
+                gt(big(dst, c0, c1) if s < 5 else sums(c0, c1), ("BIG", src, src + ES), (lst, c0, c1), big(A0, c0, c1), OP.add)
+
+            if s < 5:
+                for q, (c0, c1) in enumerate(CHS):
+                    if s > 1:
+                        if (s, q) == (2, 0):
+                            offs(1, 0)
+                        if s < SPLIT:
+                            double(c0, c0 + 40)
+                        if q < 3:
+                            offs(s - 1, q + 1)
+                        else:
+                            offs(s, 0)
+                        double(c0 + 40 * (s < SPLIT), c1)
+                        if (s, q) != (4, 1):
+                            keep(q, dst)
+                    pointers(q)
+            else:
+                offs(4, 1)
                 ga("PS", ("P0", 0, ES), "LW")
                 extract(("CG", 0, 32), "PS", 0, 32)
-                ga(("P1", 0, 512), ("P0", 0, ES), ("L4", 0, 32))
-            for q, (c0, c1) in enumerate(CHS if s < 5 else CH):
-                if s > 1:
-                    if (s, q) == (2, 0):
-                        offs(1, 0)
-                    if q < 3:
-                        offs(s - 1, q + 1)
-                    elif s < 5:
-                        offs(s, 0)
-                    if (s, q) == (5, 2):
-                        ts("LX", ("CG", 0, 32), float(E), OP.add)
-                        ga("PS", ("P0", 0, ES), "LX")
-                        extract(("CG", 0, 32), "PS", 0, 32)
-                        gv("PG", S16, "LW")
-                        gt("MK", S16, "LX", "PG", OP.add)
-                        ts("LY", ("CG", 0, 32), 0.0, OP.max)
-                        gt("PG", "RT", "LY", "MK", OP.mult)
-                        ga(("P1", 512, 1024), ("P0", 0, ES), ("L4", 32, 64))
-                        extract(("X0", 0, 64), "P1", 0, 64)
-                        lin(upto("SW"), [(("IW", 32, 160), upto("PG"))])
-                        pointers(1)
-                        act(upto("PAY"), upto("SW"), AF.Copy)
-                        show(0, r, QG)
-                        lin(upto("CG"), [(("IW", 32, 160), ("PG", 256, 512)), (("IN", 32, 160), upto("PG"))])
-                        pointers(2)
-                        act(("PAY", 256, 512), upto("CG"), AF.Abs)
-                        show(1, r, RG)
-                        pointers(3)
-                    gt(big(dst, c0, c1) if s < 5 else sums(c0, c1), ("BIG", src, src + ES), (lst, c0, c1), big(A0, c0, c1), OP.add)
-                    if s < 5:
-                        keep(q, dst)
-                if s < 5:
-                    pointers(q)
-                if s == 1:
-                    extract(("SL", 256 + CH[q][0], 256 + CH[q][1]), "P1", CH[q][0], CH[q][1], "ZG", start=False, stop=q == 3)
+                (ga if PGS else gv)(PG, S16, "LW")
+                double(0, 64)
+                offs(4, 2)
+                ga(sums(64, XA), S16, (lst, 64, XA))
+                double(128, XB)
+                ts("LX", ("CG", 0, 32), float(E), OP.add, E + 31.0, OP.min)
+                ga("PS", ("P0", 0, ES), "LX")
+                extract(("CG", 0, 32), "PS", 0, 32)
+                if XA < 128:
+                    ga(sums(XA, 128), S16, (lst, XA, 128))
+                dma("g", ap(sums(64, 128)), ap(big(S1, 64, 128)), [big(S1, 64, 128), sums(64, 128)], [sums(64, 128)], accum_op=OP.add)
+                offs(4, 3)
+                double(XB, XB + 16)
+                gt(MK, S16, "LX", PG, OP.add)
+                pointers(0)
+                double(XB + 16, YA)
+                ts("LY", ("CG", 0, 32), 1.0, OP.add, 32.0, OP.min)
+                double(YA, YA + 16)
+                gt(PG, upto("RT", 33), "LY", MK, OP.mult)
+                ga(row("P1", 128, 192), ("P0", 0, ES), (lst, 128, 192))
+                lin(upto("SW"), [(("IW", 32, 160), part(PG, 0, 256))])
+                extract(("X2", 0, 64), "P1", 128, 192)
+                act(part(PAY, 0, 256), upto("SW"), AF.Copy)
+                show(0, r, QG)
+                pointers(3)
+                lin(upto("CG"), [(("IW", 32, 160), part(PG, 256, 512)), (("IN", 32, 160), part(PG, 0, 256))])
+                ga(row("P1", 64, 128), ("P0", 0, ES), (lst, 64, 128))
+                act(part(PAY, 256, 512), upto("CG"), AF.Abs)
+                show(1, r, RG)
+                extract(("X1", 0, 64), "P1", 64, 128)
+                double(YA + 16, 256)
             if s == 1:
                 ga(upto("PS"), ("P0", 0, P), "SS")
-                extract(("PT", 32, 48), "PS", 0, 16)
+                extract(("PT", 0, 16), "PS", 0, 16)
+                if not last:
+                    extract(("PT", 16, 32), "PS", 0, 16, "ZB")
+            if s == 2:
+                lin(SL, [("IC", "C"), ("ID15", upto(H)), ("ID191", upto(L)), ("IK", "SN")])
             if s == 3:
-                ts("SF", ("PT", 32, 48), 0.0, OP.is_ge)
-                ts("SG", ("PT", 32, 48), float(E), OP.add)
-                tt("SF", "SF", "SUM", OP.mult)
-                if r == 0:
-                    table_scales()
-                tt(("KH", 16, 32), "SG", "SF", OP.add)
-                cp(("LW", 16, 32), ("KH", 16, 32))
+                ts(("LW", 16, 32), ("PT", 0, 16), float(E), OP.add, E + 31.0, OP.min)
+                if last:
+                    tt(("KB", 16, 32), ("PT", 0, 16), ("DB", 16, 32), OP.min)
+                else:
+                    tt(("KB", 48, 64), ("PT", 16, 32), ("DB", 48, 64), OP.min)
+            if s == 4 and not last:
+                ts(("KU", 16, 32), ("KB", 48, 64), 256.0, OP.add)
+        act("KEY", SL, AF.Relu, bias=G0 + E - K)
+        lin(SL, [("IA", "C"), ("I16", upto(H)), (ID, upto(L)), (INF, "KEY")])
+        if last:
+            for h in range(2):
+                extract(("SW", 128 * h, 128 * h + 128), "P1", 0, 128, step=2, first=1 - h)
         offs(5, 0)
-        for q, (c0, c1) in enumerate(CH):
+        for q, (c0, c1) in enumerate(CH[k] for k in LATE):
+            c = c0 + (MS if q < 3 else 0)
+            if c > c0:
+                gt(big(Q0, c0, c), upto("RT", 33), (LT, c0, c), sums(c0, c), OP.mult)
             if q < 3:
-                offs(5, q + 1)
-            gt(big(Q0, c0, c1), "RT", ("LT", c0, c1), sums(c0, c1), OP.mult)
-            if q < 2:
+                offs(5, LATE[q + 1])
+            gt(big(Q0, c, c1), upto("RT", 33), (LT, c, c1), sums(c, c1), OP.mult)
+            if q < QS and QS - q < 3:
                 act(big(S1, c0, c1), big(Q0, c0, c1), AF.Copy)
-            elif q == 2:
+            elif q % 2 == 0:
                 gcopy(big(S1, c0, c1), big(Q0, c0, c1))
             else:
                 dma("s", ap(big(S1, c0, c1)), ap(big(Q0, c0, c1)), [big(Q0, c0, c1)], [big(S1, c0, c1)])
-            if q == 1:
-                act("GT", ("SL", 256, 512), AF.Identity, bias=8.5)
+            if q == 0:
                 act("KEY", SL, AF.Identity, bias=float(G0 + E))
-                if r == 0:
-                    vote_constants()
+            if q == 1 and r == 0:
+                stamps(0)
+        if r == 0:
+            cut_constants()
 
         def margin(c0, c1):
-            act(big(A0, c0, c1), big(R0, c0, c1), AF.Identity, bias=MARGIN)
+            act(row("MB", c0, c1), row("RB", c0, c1), AF.Identity, bias=MARGIN)
 
-        ts("DC", "C", 0.6, OP.is_lt, 0.75, OP.subtract)
         for q, (c0, c1) in enumerate(C1):
             gt(big(S1, c0, c1), QA, ("LU", c0, c1), big(S1, c0, c1), OP.subtract)
-            act(big(R0, c0, c1), big(S1, c0, c1), AF.Abs)
-        ts(big(A0, *C2[0]), big(R0, *C2[0]), MARGIN, OP.add)
-        for c in C2[1:]:
-            margin(*c)
-        act("TU", upto("LK"), AF.Identity, scale=-stamp, bias=stamp)
+            act(row("RB", c0, c1), big(S1, c0, c1), AF.Abs)
+            if q in EARLYM:
+                margin(*EARLYM[q])
+        if MV:
+            ts(row("MB", 0, MV), row("RB", 0, MV), MARGIN, OP.add)
+        if last:
+            ts("LB", upto("SW"), 1.0, OP.add, 32.0, OP.min)
         if r == 0:
-            stamps(0)
+            ms("STB", STAMP[0])
+            ts(("COL", 1, 2), ("COL", 0, 1), float(FLAG), OP.not_equal)
+        for c in LATEM:
+            margin(*c)
 
-        def offsets(bank, c0, c1):
-            halves = [(c0, (c0 + c1) // 2), ((c0 + c1) // 2, c1)]
-            for a, b in halves:
-                tt((bank, 256 + a - c0, 256 + b - c0), (bank, a - c0, b - c0), ("KEY", a, b), OP.max)
-            for a, b in halves:
-                tt((bank, 256 + a - c0, 256 + b - c0), (bank, 256 + a - c0, 256 + b - c0), ("DUM", a, b), OP.min)
-            for a, b in halves:
-                cp(("LC", a, b), (bank, 256 + a - c0, 256 + b - c0))
+        def votes(c0, c1):
+            b = [b for b in range(4) if GR[b][0] <= c0 < GR[b][1]][0]
+            b0, b1 = GR[b]
+            if c0 == b0:
+                lin((BK[b], 0, b1 - b0), [("I8K", upto("CB", b1 - b0))] + [("I16K", (n, b0, b1)) for n in ["EQ"] + kept], stop=False)
+            gt(row("P1", c0, c1), "RB", ("LU", c0, c1), row("MB", c0, c1), OP.is_gt)
+            if c1 == b1:
+                extract((BK[b], 0, b1 - b0), "P1", b0, b1, "ZC", False)
+
+        def offsets(b, k):
+            b0, b1 = GR[b]
+            x = (BK[b], 256, 256 + b1 - b0)
+            if k == 0:
+                tt(x, (BK[b], 0, b1 - b0), ("KEY", b0, b1), OP.max)
+            elif k == 1:
+                tt(x, x, ("DUM", b0, b1), OP.min)
+            else:
+                cp((LC, b0, b1), x)
+
+        def scalar_stamps(c0, c1):
+            n = 16 * (c1 - c0)
+            op("a", lambda: g.scalar.activation(T.BIG[:].indirect(T[LC][:, c0:c1]), T.STF[:, 0:n], AF.Silu), ["STF", (LC, c0, c1)], ["BIG"])
+
+        def vector_stamps(c0, c1):
+            put("W1", (LC, c0, c1), ("STB", 0, 16 * (c1 - c0)))
+
+        for c in ((0, 48), (48, 64), (64, 112)):
+            votes(*c)
+        for b, pieces in enumerate((((112, 128), (128, 144), (144, 192)), ((192, 204), (204, 216), (216, 256)))):
+            for k, c in enumerate(pieces):
+                offsets(b, k)
+                votes(*c)
+        for c in SC[:2]:
+            scalar_stamps(*c)
+        vector_stamps(*VC[0])
+        for k in range(3):
+            offsets(2, k)
+            offsets(3, k)
+        for c in SC[2:]:
+            scalar_stamps(*c)
+        WG2 = ("RB", 1024, 1216)
+        dma("a", ap(WG2), T.BIG[0:128:16, 0:G0], [("BIG", 0, G0)], [WG2])
+        for n in ("P0", "P1")[:1 + VADD]:
+            dma("g", T[n][1:128:4, 0:E], T.BIG[0:128:16, G0:KEYS], [("BIG", G0, KEYS)], [(n, 0, E, 0x2222)])
+        for k, c in enumerate(VC[1:]):
+            if not last:
+                cursors("C", 1, k)
+            vector_stamps(*c)
+        dma("s", T.WG1[:], T.W1[0:128:16, 0:G0], [("W1", 0, G0)], ["WG1"])
+        for n in ("P0", "P1")[:1 + VADD]:
+            dma("s", T[n][0:128:4, 0:E], T.W1[0:128:16, G0:KEYS], [("W1", G0, KEYS)], [(n, 0, E, 0x1111)])
 
         def sums_out(c0, c1):
-            gt(sums(c0, c1), "YT", ("LT", c0, c1), sums(c0, c1), OP.add)
-            dma("a", T.ys[:, 16 * c0:16 * c1], T.XB[:, 16 * c0:16 * c1], [sums(c0, c1)], [])
+            for h in range(2):
+                op("v", lambda h=h: g.vector.tensor_tensor(T.MB[:, 32 * c0 + h:32 * c1:2], T.YT[:, 0:33].indirect(T.LB[:, 128 * h + c0:128 * h + c1]),
+                                                           T.XB[:, 32 * c0 + 1 - h:32 * c1:2], OP.add),
+                   ["YT", "LB", row("XB", 2 * c0, 2 * c1)], [("MB", 32 * c0, 32 * c1, 1 << h)])
 
-        for q, (c0, c1) in enumerate(C2):
-            bank, b0, b1 = ("X0", 0, 192) if q < 4 else ("X1", 192, 256)
-            if q in (0, 4):
-                mm((bank, 0, b1 - b0), "IK", ("GT", b0, b1), True, False)
-            gt(("P1", 16 * c0, 16 * c1), RA, ("LU", c0, c1), big(A0, c0, c1), OP.is_gt)
-            extract((bank, c0 - b0, c1 - b0), "P1", c0, c1, "ZC", 1, False, q in (3, 5))
-            if q == 4:
-                offsets("X0", 0, 192)
-        for k in range(4):
-            c0 = k * CA // 4
-            op("a", lambda c0=c0: g.scalar.activation(T.BIG[:].indirect(T.LC[:, c0:c0 + CA // 4]), T.STF[:], AF.Silu),
-               ["STF", ("LC", c0, c0 + CA // 4)], ["BIG"])
-        dma("a", T.WG2[:], T.BIG[0:128:16, 0:G0], [("BIG", 0, G0)], ["WG2"])
-        dma("g", T.P0[1:128:4, 0:E], T.BIG[0:128:16, G0:KEYS], [("BIG", G0, KEYS)], [("P0", 0, E, 0x2222)])
-        dma("a", T.P2[1:128:4, 0:E], T.P0[1:128:4, 0:E], [("P0", 0, E, 0x2222)], [("P2", 0, E, 0x2222)])
-        put("W1", ("LC", CA, 192), ("STB", 0, 16 * (192 - CA)))
-        offsets("X1", 192, 256)
-        put("W1", ("LC", 192, 256), ("STB", 0, 1024))
-        dma("s", T.WG1[:], T.W1[0:128:16, 0:G0], [("W1", 0, G0)], ["WG1"])
-        for n in ("P0", "P2"):
-            dma("s", T[n][0:128:4, 0:E], T.W1[0:128:16, G0:KEYS], [("W1", G0, KEYS)], [(n, 0, E, 0x1111)])
+        def store(c0, c1):
+            wait("s", ("lh%d" % r, ne))
+            dma("s", T.ys[:, 32 * c0:32 * c1], T.MB[:, 32 * c0:32 * c1], [row("MB", 2 * c0, 2 * c1)], [])
+
+        kb = 0 if last else 32
+        mm(("X2", 0, 32), IDF, ("DB", kb, kb + 32), True, False)
+        act("WD", ID, AF.Identity, scale=-stamp)
         if last:
-            sums_out(0, 96)
+            sums_out(0, 48)
+            sums_out(48, 88)
+            act("SN", "C", AF.Relu, bias=-2.0)
+            act("SN", "SN", AF.Identity, scale=-4.0, bias=1.0)
         else:
-            products(1, (0, 1))
-            chosen((0, 1))
-            products(1, (2, 3))
+            if r == 0:
+                act("H", upto("AL0"), AF.Copy)
+                act("L", upto("AL1"), AF.Copy)
+                act(upto("YT", 33), upto("YT", 33), AF.Identity, scale=0.5)
+            stamps(r + 1)
+            chosen("C", 1, 2)
+            digits(1, (3, 6))
         for k in range(4):
-            mm(("CG", 0, 48), ("IW", 96, 224), ("WG2", 48 * k, 48 * k + 48), k == 0, False)
+            mm(("CG", 0, 48), ("IW", 96, 224), part(WG2, 48 * k, 48 * k + 48), k == 0, False)
         for k in range(4):
             mm(("CG", 0, 48), ("IB", 96, 224), ("WG1", 48 * k, 48 * k + 48), False, k == 3)
         ts("HG", ("CG", 0, 48), thr, OP.is_ge, -1.0, OP.mult)
-        send("HG", range(1, N), lambda d: T.RH[:, (3 * r + d - 1) * 48:(3 * r + d) * 48], "ah%d" % r, "lh%d" % r, -1, [("RH", 144 * r, 144 * r + 144)], [QG, RG])
-        if last:
-            sums_out(96, 144)
-            act("KEY", "C", AF.Identity, scale=4.0)
-            act("T1", "DC", AF.Identity, scale=4.0)
-        else:
-            chosen((2, 3))
-        mm(("X2", 0, 32), IDF, "DH", True, False)
-        mm(upto("X0"), ID, "TU", True, False)
+        send("HG", range(1, N), lambda d: T.RH[:, (d - 1) * 48:d * 48], "ah%d" % r, "lh%d" % r, -1, ["RH"], [QG, RG])
+        for h, (c0, c1) in enumerate(HALF):
+            lin((BK[h], 0, 128), [("WD", (n, c0, c1)) for n in ["EQ"] + kept], stop=False)
+            if h or not VADD:
+                extract((BK[h], 0, 128), "P0", c0, c1, "ZH", start=False, stop=False)
 
-        def partners(q, stop=False):
-            extract(("X0",) + CH[q], "P1", CH[q][0], CH[q][1], "ZH", start=False, stop=stop)
+        def partners(share):
+            if not VADD:
+                shared(("P0", 0, P), "LU", share)
+                return
+            for q in range(2):
+                ga(row("P1", *CH[2 + q]), ("P0", 0, P), ("LU",) + CH[2 + q])
+                gt(row("P1", *CH[q]), ("P0", 0, P), ("LU",) + CH[q], row("P1", *CH[q]), OP.add)
 
-        shared(("P0", 0, ES), "L0", SHARE_H)
-        partners(0)
-        b = 144 * r
-        for h in range(2):
-            for d in range(3):
-                mm(("X2", 16 * h, 16 * h + 16), "IK", ("RH", b + 64 * d, b + 64 * d + 16), False, (h, d) == (1, 2))
-        partners(1)
-        partners(2)
-        partners(3)
-        for c0 in (0, 16):
-            tt(("TH", c0, c0 + 16), ("X2", c0, c0 + 16), ("KH", c0, c0 + 16), OP.max)
-        for c0 in (0, 16):
-            cp(("LH", c0, c0 + 16), ("TH", c0, c0 + 16))
-        for c0 in (0, 16):
-            put("P2", ("LH", c0, c0 + 16), upto("STB"))
-        extract(upto("X0"), "P2", 0, 256, "ZH", 1, start=False)
+        def returned():
+            for h in range(2):
+                for d in range(3):
+                    mm(("X2", 16 * h, 16 * h + 16), "IK", ("RH", 64 * d, 64 * d + 16), False, (h, d) == (1, 2))
+            for c0 in (0, 16):
+                tt(("TH", c0, c0 + 16), ("X2", c0, c0 + 16), ("KB", kb + c0, kb + c0 + 16), OP.max)
+            for c0 in (0, 16):
+                ts(("LH", c0, c0 + 16), ("TH", c0, c0 + 16), float(E) if last else 256.0, OP.add)
+
         if last:
-            sums_out(144, 256)
-            ts(upto("PT"), upto("X0"), thr, OP.is_ge)
-            tt(upto("PT"), upto("PT"), "T1", OP.mult)
-            tt("KEY", upto("PT"), "KEY", OP.add)
-            dma("s", T.yc[:], T.KEY[:], ["KEY"], [])
+            partners(SHARE_0)
+            store(0, 88)
+            sums_out(88, 104)
+            returned()
+            for c0 in (0, 16):
+                put("P1", ("LH", c0, c0 + 16), upto("STB"))
+            sums_out(104, 128)
+            store(88, 128)
+            for h, (c0, c1) in enumerate(HALF):
+                extract((BK[h], 0, 128), "P1", c0, c1, "ZH", start=False)
+            for h, (c0, c1) in enumerate(HALF):
+                x = (BK[h], 128, 256)
+                ts(x, (BK[h], 0, 128), thr - stamp, OP.is_ge)
+                tt(x, x, ("SN", c0, c1), OP.mult)
+                tt(("KEY", c0, c1), x, ("C", c0, c1), OP.add)
+                dma("sa"[h], T.yc[:, c0:c1], T.KEY[:, c0:c1], [("KEY", c0, c1)], [])
         else:
-            stamps(r + 1)
-            digits()
-            channels()
-            lin(upto("CG"), [(ID, upto("AL0")), ("IM", upto("TB0"))])
-            act("D0", upto("CG"), AF.Copy)
-            ts(upto("NMV"), upto("X0"), thr, OP.is_lt)
-            row_out("s", 1, 7, "NMV")
-            other_end("ALO")
-            lin(SL, [(ID, "ALO"), ("IM", upto("DLO"))])
-            act("D1", SL, AF.Copy)
-            ts(("PT", 256, 512), upto("X0"), thr, OP.is_ge)
-            ts("LB", upto("SW"), 256.0, OP.add)
-            tt(upto("PT"), ("PT", 256, 512), "D0", OP.mult)
-            tt(upto("X3"), ("PT", 256, 512), "D1", OP.mult)
-            tt(upto("TB0"), upto("PT"), upto("TB0"), OP.add)
-            tt(upto("DLO"), upto("X3"), upto("DLO"), OP.add)
+            partners(SHARE_H)
+            op("a", lambda: g.scalar.activation(T.PS[:], ap(NAMESD).indirect(T.KU[:]), AF.Identity, scale=T.COL[:, 1:2]), [NAMESD, "KU", "COL"], ["PS"])
+            for k, q in enumerate((2, 0, 3, 1) if VADD else range(4)):
+                extract((BK[q // 2], 64 * (q % 2), 64 * (q % 2) + 64), "P1", CH[q][0], CH[q][1], "ZH", start=False, stop=q % 2 == 1)
+            for h in (1, 0) if VADD else (0, 1):
+                ts(("NMV",) + HALF[h], (BK[h], 0, 128), thr - stamp, OP.is_lt)
+            row_out("s", 1, FLAG, "NMV")
+            blocks()
+            ts("LB", upper("SL"), 256.0, OP.add)
+            returned()
+            lin(upto("PT"), [(ID, "H"), ("IM", upto("AL0"))])
+            lin(upper("PT"), [(ID, "L"), ("IM", upto("AL1"))])
+            act("STB", ("XC", 0, NSV), AF.Identity, scale=0.0, bias=STAMP[r + 1])
+            for h in range(2):
+                put(NAMESD, ("LH", 16 * h, 16 * h + 16), ("PS", 256 * h, 256 * h + 256))
+            dma("s", T.NMV[:], T.P0[FLAG:128:16, P:2 * P], [NAMES + (1 << FLAG,)], ["NMV"])
 
     for s in total:
         if max([0] + [waited[k] for k in waited if k[1] == s]) < total[s]:

from concourse.bass import DstId, RemoteDMATransfer
from concourse.mybir import AluOpType as OP, ActivationFunctionType as AF

E, GH, P, RO, N = 4096, 256, 4864, 3, 4
BW = P // 16
ES = E + 32
G0 = 4 * (P - E)
KEYS = G0 + 4 * E
SC = [(0, 48), (48, 96), (216, 256), (192, 216)]
VC = [(96, 128), (128, 160), (160, 192)]
GR = [(0, 48), (48, 128), (128, 216), (216, 256)]
NSA, NSV = 16 * max(b - a for a, b in SC), 16 * max(b - a for a, b in VC)
SP = 112
S0, S1, A0, PG0, Q0, BIGW = 0, ES, 2 * ES, 3 * ES, KEYS - E, KEYS + NSA + SP
SCALE10 = 168199201
MARGIN = 2.2
K = 65536.0
UNL = 8192.0
STAMP = (1e10, 1e14, 1e18)
NDMA = 80
ALL = 0xFFFF
CH = [(0, 64), (64, 128), (128, 192), (192, 256)]
CHS = CH[:3] + [(192, 258)]
HALF = [(0, 128), (128, 256)]
LATE = (0, 2, 3, 1)
C1 = [(0, 64), (128, 192), (192, 256), (64, 104), (104, 128)]
SHARE_0, SHARE_A, SHARE_H = (32, 32, 32, 32), (32, 32, 32, 24), (0, 32, 40, 40)
HELP, MV, MS = 0, 48, 48
XA, XB, YA, PGS, SPLIT, QS, VADD = 128, 136, 192, 0, 3, 2, 1
EARLYM, LATEM = {}, [(48, 112), (112, 180), (180, 256)]
FLAG = 7

F, B, I, U = "float32", "bfloat16", "int32", "uint16"
SCRATCH = {
    "BIG": ("sbuf", [128, BIGW], F), "RB": ("sbuf", [128, P], F), "MB": ("sbuf", [128, E], F),
    "W1": ("sbuf", [128, KEYS + NSV + SP], B), "XB": ("sbuf", [128, ES], F),
    "XC": ("sbuf", [128, ES], B), "P0": ("sbuf", [128, 2 * P + GH + SP], B), "P1": ("sbuf", [128, ES + GH + SP], B),
    "WG1": ("sbuf", [128, 192], B), "CI": ("sbuf", [128, 1024], I), "STF": ("sbuf", [128, NSA], F), "STB": ("sbuf", [128, NSV], B),
    "IW": ("sbuf", [128, 256], F), "IB": ("sbuf", [128, 256], B), "IN": ("sbuf", [128, 160], F),
    "RT": ("sbuf", [128, 33], F), "YT": ("sbuf", [128, 33], F),
    "RH": ("sbuf", [128, 3 * 48], B), "HG": ("sbuf", [128, 48], B),
    "COL": ("sbuf", [128, 8], F), "COLI": ("sbuf", [128, 8], I),
    "PS": ("sbuf", [128, 512], B), "SS": ("sbuf", [128, 16], U),
}
for _n in ("LW", "LX", "LY", "KU", "LH"):
    SCRATCH[_n] = ("sbuf", [128, 32], U)
SCRATCH["TH"] = ("sbuf", [128, 32], F)
for _n in ("KB", "DB"):
    SCRATCH[_n] = ("sbuf", [128, 64], F)
for _n in ("SH", "SA", "SB"):
    SCRATCH[_n] = ("sbuf", [128, 16], I)
for _n in ("SF", "SG"):
    SCRATCH[_n] = ("sbuf", [128, 16], F)
for _n in ("ZE", "ZA", "ZB", "ZC", "ZH"):
    SCRATCH[_n] = ("sbuf", [128, 144], B)
DIAG = {"IK": K, "IBW": float(BW), "I16": 16.0}
LATER = {"IA": float(E), "IC": E - 48.0, "ID15": 15.0, "ID191": -191.0, "IM": -1.0, "I8K": 8.5 * K, "I16K": 16 * K}
SWAP = {"SW16": 16.0, "SWK": -UNL}
for _n in ("CB", "SWB", "WD") + tuple(DIAG) + tuple(LATER) + tuple(SWAP):
    SCRATCH[_n] = ("sbuf", [128, 128], B)
for _n in ("TH0", "TL0", "AL0", "AL1", "NMV"):
    SCRATCH[_n] = ("sbuf", [128, BW], B)
for _n in ("H", "L", "EQ", "C", "SELF", "SN"):
    SCRATCH[_n] = ("sbuf", [128, 256], B)
for _n in ("EW", "EN", "DUM", "KEY"):
    SCRATCH[_n] = ("sbuf", [128, 256], F)
SCRATCH["BI"] = ("sbuf", [128, 256], I)
for _n in ("L0", "L1", "L2", "LS"):
    SCRATCH[_n] = ("sbuf", [128, 258], U)
LEVEL = ("L0", "L1", "L2", "L1", "L2")
LT, LC = "L1", "L2"
for _n in ("LB", "LU"):
    SCRATCH[_n] = ("sbuf", [128, 256], U)
PSUM = ("X0", "X1", "X2", "X3", "SW", "CG", "PT", "SL")
for _n in PSUM:
    SCRATCH[_n] = ("psum", [128, 512], F)
SEMAPHORES = ["cv", "ca", "cp", "cg"] + ["d%d" % i for i in range(NDMA)] + \
    ["%s%d" % (k, r) for k in ("a0", "a1", "ah", "l0", "l1", "lh", "h0", "h1") for r in range(RO)]
DIRECT = [((1, 2, 3), (3,))] + [((1, 2), (3,))] * (RO - 1)


def mean_table():
    out = {}
    for m in range(1, 33):
        e = 0
        while SCALE10 * 2 ** e < 2 ** 23 * 1280 * m:
            e += 1
        out[m] = ((2 * SCALE10 * 2 ** e + 1280 * m) // (2 * 1280 * m), e)
    return out


def helper_of(rank, T, topo):
    core = T.cores[rank]
    return [c for c in topo.cores_of(core) if topo.die(c) != topo.die(core)
            and all(topo.may_write(c, o) for o in T.cores if o != core)][0]


def far_engines(core, rank, T, topo):
    reach = [topo.engines(core, T.cores[(rank + d) % N]) for d in range(1, N)]
    return [e for e in reach[0] if all(e in x for x in reach)]


def transfer(topo, cores, engines, sem, src, dsts):
    ids = [DstId(rid=topo.addr(c)[0], pnc=topo.addr(c)[1]) for c in cores]
    return RemoteDMATransfer(dst_ids=ids, dma_engine_mask=sum(1 << e for e in engines), remote_sem=sem, src=src, dsts=dsts)


def ghost_place(T, k, d):
    o = (Q0, 0)[k] + E + GH * (d - 1)
    return T[("BIG", "RB")[k]][:, o:o + GH]


def relay_place(T, k, r):
    o = GH * (2 * r + k)
    return T.BIG[:, o:o + GH]


def helper_program(g, core, rank, T, topo):
    engs = far_engines(core, rank, T, topo)
    near = [e for e in topo.engines(T.cores[rank], core) if e not in far_engines(T.cores[rank], rank, T, topo)]
    sent = []
    for r in range(RO):
        for k in range(2):
            ds = [d for d in range(1, N) if d not in DIRECT[r][k]]
            if ds:
                g.wait_ge(T.sem["h%d%d" % (k, r)], len(near))
                g.remote_dma_fused([transfer(topo, [T.cores[(rank + d) % N] for d in ds], engs, T.sem["a%d%d" % (k, r)],
                                             relay_place(T, k, r), [ghost_place(T, k, d) for d in ds])], local_sem=T.sem["l%d%d" % (k, r)])
                sent.append("l%d%d" % (k, r))
    for s in sent:
        g.wait_ge(T.sem[s], len(engs))


def rank_program(g, core, T, topo):
    rank = T.rank_of(core)
    if rank is None:
        for k in range(N):
            if core == helper_of(k, T, topo):
                helper_program(g, core, k, T, topo)
        return
    eng = {"v": g.vector, "a": g.scalar, "p": g.tensor, "g": g, "s": g.sync}
    cnt = {"v": 0, "a": 0, "p": 0, "g": 0}
    rec, waited, total, nd = {}, {}, {}, [0]

    def span(x):
        if isinstance(x, str):
            x = (x, 0, SCRATCH[x][1][1])
        return x if len(x) == 4 else x + (ALL,)

    def wait(q, ev):
        s, v = ev
        if waited.get((q, s), 0) < v:
            eng[q].wait_ge(T.sem[s], v)
            waited[(q, s)] = v

    def note(ev, src, R, W):
        for x in R:
            n, lo, hi, ch = span(x)
            rec.setdefault(n, []).append((lo, hi, ev, False, src, ch))
        for x in W:
            n, lo, hi, ch = span(x)
            rec[n] = [r for r in rec.get(n, []) if not (lo <= r[0] and r[1] <= hi and r[5] & ch == r[5])] + [(lo, hi, ev, True, src, ch)]
        total[ev[0]] = max(total.get(ev[0], 0), ev[1])

    def deps(q, src, R, W):
        need = {}
        for x, wr in [(x, False) for x in R] + [(x, True) for x in W]:
            n, lo, hi, ch = span(x)
            for r in rec.get(n, []):
                meet = r[0] < hi and lo < r[1] and r[5] & ch
                if r[4] == src:
                    must = meet and (wr or r[3]) and src != "p"
                else:
                    must = n in PSUM or (meet and (wr or r[3]))
                if must:
                    need[r[2][0]] = max(need.get(r[2][0], 0), r[2][1])
        for s in need:
            wait(q, (s, need[s]))

    def op(q, fn, R, W, inc=True):
        deps(q, q, R, W)
        ins = fn()
        if inc:
            ins.then_inc(T.sem["c" + q], 1)
            cnt[q] += 1
            note(("c" + q, cnt[q]), q, R, W)
        else:
            note(("c" + q, cnt[q] + 1), q, R, W)

    def dma(q, out, in_, R, W, **how):
        s = "d%d" % nd[0]
        nd[0] += 1
        deps(q, s, R, W)
        eng[q].dma_start(out, in_, **how).then_inc(T.sem[s], 16)
        note((s, 16), s, R, W)

    engs = far_engines(core, rank, T, topo)
    aide = helper_of(rank, T, topo)
    near = [e for e in topo.engines(core, aide) if e not in engs]
    ne = len(engs)

    def send(src, ds, dst_of, arr, loc, step, land, freed=(), relay=None):
        deps("g", loc, [src], list(freed))
        parts = [transfer(topo, [T.cores[(rank + step * d) % N] for d in ds], engs, T.sem[arr], ap(src), [dst_of(d) for d in ds])] if ds else []
        if relay is not None:
            parts.append(transfer(topo, [aide], near, T.sem[relay[0]], ap(src), [relay[1]]))
        g.remote_dma_fused(parts, local_sem=T.sem[loc])
        note((loc, (ne if ds else 0) + (len(near) if relay else 0)), loc, [src], [])
        note((arr, ne * (N - 1)), arr, [], land)

    PG, MK, PAY = [("BIG", PG0 + 512 * k, PG0 + 512 * k + 512) for k in range(3)]

    def part(x, lo, hi):
        return (x[0], x[1] + lo, x[1] + hi)

    def show(k, r, land):
        src = part(PAY, GH * k, GH * k + GH)
        relay = ("h%d%d" % (k, r), relay_place(T, k, r)) if len(DIRECT[r][k]) < N - 1 else None
        send(src, DIRECT[r][k], lambda d: ghost_place(T, k, d), "a%d%d" % (k, r), "l%d%d" % (k, r), 1, [land], relay=relay)

    def ap(x):
        n, lo, hi = (x, 0, SCRATCH[x][1][1]) if isinstance(x, str) else x[:3]
        return T[n][:, lo:hi]

    def ts(out, a, s1, o0, s2=None, o1=None):
        if o1 is None:
            op("v", lambda: g.vector.tensor_scalar(ap(out), ap(a), s1, None, o0), [a], [out])
        else:
            op("v", lambda: g.vector.tensor_scalar(ap(out), ap(a), s1, s2, o0, o1), [a], [out])

    def tt(out, a, b, o):
        op("v", lambda: g.vector.tensor_tensor(ap(out), ap(a), ap(b), o), [a, b], [out])

    def cp(out, a):
        op("v", lambda: g.vector.tensor_copy(ap(out), ap(a)), [a], [out])

    def ms(out, val):
        op("v", lambda: g.vector.memset(ap(out), val), [], [out])

    def act(out, a, func, bias=0.0, scale=1.0, extra=()):
        op("a", lambda: g.scalar.activation(ap(out), ap(a), func, bias=bias, scale=scale), [a] + list(extra), [out])

    def gt(out, win, lst, b, o):
        op("v", lambda: g.vector.tensor_tensor(ap(out), ap(win).indirect(ap(lst)), ap(b), o), [win, lst, b], [out])

    def gv(out, win, lst):
        op("v", lambda: g.vector.tensor_copy(ap(out), ap(win).indirect(ap(lst))), [win, lst], [out])

    def ga(out, win, lst):
        op("a", lambda: g.scalar.activation(ap(out), ap(win).indirect(ap(lst)), AF.Copy), [win, lst], [out])

    def put(win, lst, src):
        op("v", lambda: g.vector.tensor_copy(ap(win).indirect(ap(lst)), ap(src)), [src, lst], [win])

    def mm(out, lhs, rhs, start, stop, rap=None, inc=False):
        r = ap(rhs) if rap is None else rap
        op("p", lambda: g.tensor.matmul(ap(out), ap(lhs), r, start, stop), [lhs, rhs], [out], inc=stop or inc)

    def lin(out, terms, start=True, stop=True):
        for k, (lhs, rhs) in enumerate(terms):
            mm(out, lhs, rhs, start and k == 0, stop and k == len(terms) - 1)

    def extract(out, row, c0, c1, Z="ZE", start=True, stop=True, step=1, first=0):
        for i in range(16):
            mm(out, (Z, 16 - i, 144 - i), (row, 16 * step * c0, 16 * step * c1), start and i == 0, stop and i == 15,
               rap=T[row][:, step * (16 * c0 + i) + first:16 * step * c1:16 * step])

    def gi(out, oap, pat, base, cm, flt=True):
        if flt:
            op("g", lambda: g.iota(oap, pat, base, cm, allow_small_or_imprecise_dtypes=True), [], [out])
        else:
            op("g", lambda: g.iota(oap, pat, base, cm), [], [out])

    def gs(out, oap, a, iap, pat, cmp, fill, base, cm):
        op("g", lambda: g.affine_select(oap, iap, pat, cmp, fill, base, cm), [a], [out])

    def gcopy(out, a):
        gs(out, ap(out), a, ap(a), [[0, out[2] - out[1]]], OP.is_ge, 0.0, 0, 0)

    def picker(Z, weights):
        gi(Z, T[Z][:], [[0, 144]], 0, 0)
        for ch in weights:
            gs(Z, T[Z][:, 0:144:16], Z, T[Z][:, 0:144:16], [[-16, 9]], OP.not_equal, weights[ch], 16 - ch, 1)

    def big(o, c0, c1):
        return ("BIG", o + 16 * c0, o + 16 * c1)

    def row(n, c0, c1):
        return (n, 16 * c0, 16 * c1)

    def upto(n, k=256):
        return (n, 0, k)

    def upper(n):
        return (n, 256, 512)

    def row_out(q, region, ch, tile):
        dma(q, T.P0[ch:128:16, region * P:(region + 1) * P], T[tile][:], [tile], [("P0", region * P, (region + 1) * P, 1 << ch)])

    ID, IDF, INF = ("IB", 0, 128), ("IW", 0, 128), ("IN", 0, 128)
    SL = ("SL", 0, 256)
    NAMES = ("P0", P, 2 * P)
    NAMESD = ("P0", P, 2 * P + GH + SP)
    BK = ["X0", "X1", "X2", "X3"]
    S16 = ("BIG", S1, S1 + ES)
    QA = ("BIG", Q0, Q0 + P)
    QG, RG = ("BIG", Q0 + E, Q0 + P), ("RB", E, P)
    tab = mean_table()

    def cursors(cur, step, i):
        ts(("PT", 256 * (i % 2), 256 * (i % 2) + 256), cur, float((i - step) % 4), OP.is_equal)

    def chosen(cur, step, done=0):
        a, b, p0, p1 = upto("MB"), ("MB", 256, 512), upto("PT"), upper("PT")
        for i in range(done, 2):
            cursors(cur, step, i)
        tt(a, p0, ("CI", 0, 256), OP.mult)
        tt(p1, p1, ("CI", 256, 512), OP.mult)
        cursors(cur, step, 2)
        tt(b, p1, a, OP.add)
        tt(p0, p0, ("CI", 512, 768), OP.mult)
        cursors(cur, step, 3)
        tt(a, p0, b, OP.add)
        tt(p1, p1, ("CI", 768, 1024), OP.mult)

    def digits(region, channels, whole="BI"):
        tt(SL, upper("PT"), upto("MB"), OP.add)
        ts(whole, SL, -7.5 - E, OP.add, 1.0 / 16, OP.mult)
        tt("SELF", SL, "EN", OP.is_equal)
        ts("KEY", whole, -16.0, OP.mult, -float(E), OP.add)
        cp(upto("AL0"), whole)
        row_out("s", region, channels[0], "AL0")
        tt(upto("AL1"), SL, "KEY", OP.add)
        row_out("s", region, channels[1], "AL1")

    def blocks():
        lin(upper("SL"), [(ID, upto("AL0")), ("IBW", upto("AL1"))])

    def stamps(r):
        act("STF", ("XC", 0, NSA), AF.Silu, scale=0.0, bias=STAMP[r])

    def reads(t):
        return t if t else 32

    def shown_lists():
        ts("SA", "SH", 15, OP.bitwise_and)
        ts("SB", "SH", 4, OP.arith_shift_right)
        cp(("LW", 0, 16), "SH")
        ts("SF", "SA", float(BW), OP.mult, -256.0, OP.add)
        ts(("KB", 0, 16), "SH", -float(E), OP.add)
        ts("SA", "SH", 1, OP.bitwise_and)
        tt(("KB", 32, 48), "SF", "SB", OP.add)

    def shown_places(k):
        if k == 0:
            ts("SG", "SA", -2.0 * BW, OP.mult, BW + 256.0, OP.add)
            ts(("KU", 0, 16), ("KB", 32, 48), 256.0, OP.add)
            tt("SF", ("KB", 32, 48), "SG", OP.add)
        else:
            cp("SS", "SF")

    def stop_chain():
        ts(("SF", 0, 2), ("EW", 0, 2), float(E - 1), OP.add, 0.0, OP.max)
        cp(("SA", 0, 2), ("SF", 0, 2))
        ts(("L0", 256, 258), ("SF", 0, 2), float(E), OP.add)
        ts(("SB", 0, 2), ("SA", 0, 2), 4, OP.arith_shift_right)
        ts(("SA", 2, 4), ("SA", 0, 2), 15, OP.bitwise_and)
        cp(("TH0", 256, 258), ("SB", 0, 2))
        cp(("TL0", 256, 258), ("SA", 2, 4))

    def keep(q, o, end=258):
        c0, c1 = CHS[q][0], min(CHS[q][1], end)
        a = big(o, c0, c1)
        if c1 <= c0:
            return
        if q % 2 == 0:
            gcopy(big(A0, c0, c1), a)
        else:
            dma("s", ap(big(A0, c0, c1)), ap(a), [a], [big(A0, c0, c1)])

    def shared(win, lst, share, qs=range(4)):
        for q in qs:
            c0, c1 = CH[q]
            c = c0 + share[q]
            if c > c0:
                gv(row("P1", c0, c), win, (lst, c0, c))
            ga(row("P1", c, c1), win, (lst, c, c1))

    dma("s", T.BI[:], T.cur0[:], [], ["BI"])
    dma("a", T.CI[:, 0:512], T.cand[:, 0:512], [], [("CI", 0, 512)])
    dma("s", T.CI[:, 512:1024], T.cand[:, 512:1024], [], [("CI", 512, 1024)])
    COV = ("W1", 0, E // 2)
    dma("s", ap(COV), T.cov[:], [], [COV])
    dma("s", T.SH[:], T.shown[:], [], ["SH"])
    dma("s", T.P0[:, P - E // 2:P], T.cov[:], [], [("P0", P - E // 2, P)])
    gi(("COLI", 0, 1), T.COLI[:, 0:1], [[0, 1]], 0, 1, False)
    gi("CB", T.CB[:], [[0, 128]], 1, 0)
    for h in range(2):
        gs(("IB", 128 * h, 128 * h + 128), T.IB[:, 128 * h:128 * h + 128], "CB", T.CB[:], [[-1, 128]], OP.is_equal, 0.0, 0, 1)
    act("IW", "IB", AF.Copy)
    gi("KEY", T.KEY[:], [[16, 256]], -E, 0)
    gs("SWB", T.SWB[:, 0:128:2], "CB", T.CB[:, 0:64], [[-2, 64]], OP.is_equal, 0.0, -1, 1)
    gs("SWB", T.SWB[:, 1:128:2], "CB", T.CB[:, 0:64], [[-2, 64]], OP.is_equal, 0.0, 0, 1)
    picker("ZE", {0: 16.0, 1: 1.0})
    for t in (0, 16, 32) + tuple(range(1, 32, 2)):
        gs(("RT", t, t + 1, 1), T.RT[:, t:t + 1], ("IW", 0, 1), T.IW[:, 0:1], [[0, 1]], OP.is_gt, tab[reads(t)][0] * 2.0 ** -tab[reads(t)][1], 0, 0)
    ts(("COLI", 1, 2), ("COLI", 0, 1), 15, OP.bitwise_and)
    ms(("P0", 0, P - E // 2), 0.0)
    cp(("COL", 0, 1), ("COLI", 1, 2))
    for n in DIAG:
        act(n, ID, AF.Identity, scale=DIAG[n])
        if n == "IK":
            act("EW", "KEY", AF.Identity, bias=T.COL[:, 0:1], extra=[("COL", 0, 1)])
            act("EN", "EW", AF.Identity, bias=float(E))
    for n in SWAP:
        act(n, "SWB", AF.Identity, scale=SWAP[n])
    act("IN", upto("IB", 160), AF.Identity, scale=-1.0)
    for n in ("AL0", "AL1"):
        ms((n, 256, BW), 0.0)
    cp("C", "BI")
    chosen("C", 0)
    digits(0, (0, 1))
    for n in ("TH0", "TL0", "NMV"):
        ms((n, 256, BW), 0.0)
    blocks()
    ms(("XB", E, ES), 0.0)
    ts("LB", upper("SL"), 256.0, OP.add)
    for c0, c1 in ((0, E // 2), (E // 2, E)):
        for h in range(2):
            op("a", lambda h=h: g.scalar.activation(T.XB[:, c0 + h:c1:2], T.W1[:, c0 // 2:c1 // 2], AF.Identity, bias=-127.5), [COV], [("XB", c0, c1, 1 << h)])
        c1 += ES - E if c0 else 0
        dma("g", T.XC[:, c0:c1], T.XB[:, c0:c1], [("XB", c0, c1), "LB"], [("XC", c0, c1)])
    stop_chain()
    shown_lists()
    picker("ZB", {0: 1.0, 1: float(BW)})
    gi("DB", T.DB[:], [[P - 256 - (ES - E), 2], [0, 2], [16, 16]], ES - E, 1)

    def even_means():
        for k in (2, 4, 8):
            op("v", lambda k=k: g.vector.tensor_scalar(T.RT[:, k:32:2 * k], T.RT[:, 1:32 // k:2], 1.0 / k, None, OP.mult), [("RT", 0, 33, 1)], [("RT", 0, 33, k)])

    def cut_constants():
        gi(upto("YT", 33), T.YT[:, 0:33], [[255, 33]], 0, 0)
        gi(upto("YT", 1), T.YT[:, 0:1], [[0, 1]], 255 * 32, 0)
        gi("ZC", T.ZC[:], [[0, 144]], 0, 0)
        gi("ZC", T.ZC[:, 0:144:16], [[0, 9]], -int(K), 0)
        gs("ZC", T.ZC[:, 0:144:16], "ZC", T.ZC[:, 0:144:16], [[-16, 9]], OP.is_ge, 0.0, 16, 1)
        gs("ZC", T.ZC[:, 0:144:16], "ZC", T.ZC[:, 0:144:16], [[16, 9]], OP.is_ge, 0.0, -1, -1)
        for c0, c1 in SC + VC:
            gi(("DUM", c0, c1), T.DUM[:, c0:c1], [[16, c1 - c0]], KEYS, 1)
        picker("ZH", {ch: 1.0 for ch in range(16) if ch % 4 < 2})
        picker("ZA", {3: 16.0, 6: 1.0, FLAG: 2.0 * E})
        dma("s", T.W1[0:128:16, 0:KEYS], T.XC[:, 0:KEYS // 16], [("XC", 0, KEYS // 16)], ["W1"])
        for c0, c1 in ((P, P + E), (P + E, NAMESD[2])):
            dma("s", T.P0[:, c0:c1], T.XC[:, 0:c1 - c0], [("XC", 0, c1 - c0)], [("P0", c0, c1)])

    for r in range(RO):
        last = r == RO - 1
        stamp = STAMP[r]
        thr = 0.4 * stamp
        H, L = ("H", "L") if r else ("AL0", "AL1")
        kept = ["NMV"] if r else []

        def sums(c0, c1):
            return row("XB", c0, c1) if last else big(S0, c0, c1)

        def unlinked(h):
            a, b = HALF[h]
            lin((BK[2 + h], 0, 128), [("SW16", (H, a, b)), ("SWB", (L, a, b))] + [("SWK", (n, a, b)) for n in kept], stop=False)

        def linked(h):
            c0, c1 = HALF[h]
            tt(("EQ", c0, c1), (BK[h], 0, 128), ("EW", c0, c1), OP.is_equal)
            mm((BK[2 + h], 0, 128), "SWK", ("EQ", c0, c1), False, True)

        def entries(h):
            ts(("L0",) + HALF[h], (BK[2 + h], 0, 128), E + UNL, OP.add, E + 31.0, OP.min)

        def first(c0, c1):
            gt(big(S0, c0, c1), "XB", ("L0", c0, c1), row("XC", c0, c1), OP.add)

        for h, (c0, c1) in enumerate(HALF):
            mm((BK[h], 0, 128), "IK", ("SELF", c0, c1), True, False)
        shared(NAMES if r else ("P0", 0, P), "LB", SHARE_A if r else SHARE_0)
        if r > 0:
            for n in (upto("PT"), upper("PT")):
                tt(n, n, upto("NMV"), OP.mult)
            tt("H", upto("PT"), upto("AL0"), OP.add)
            tt("L", upper("PT"), upto("AL1"), OP.add)
        for q, (c0, c1) in enumerate(CH):
            extract((BK[q // 2], c0 % 128, c0 % 128 + 64), "P1", c0, c1, "ZA" if r else "ZE", start=False, stop=q % 2 == 1 and r == 0)
            if q % 2 == 1 and r > 0:
                mm((BK[q // 2], 0, 128), "IK", ("NMV",) + HALF[q // 2], False, True)
        lin(upto("SW"), [("SWB", upto(L))])
        lin(upto("CG"), [("SWB", upto(H))] + [("SWK", upto(n)) for n in kept], stop=False)
        unlinked(0)
        act(upto("TL0"), upto("SW"), AF.Copy)
        row_out("s", 0, 1, "TL0")
        linked(0)
        ts("SN", upto(H), 0.0, OP.is_ge)
        if r == 0:
            even_means()
        tt(("EQ", 128, 256), ("X1", 0, 128), ("EW", 128, 256), OP.is_equal)
        mm(upto("CG"), "SWK", "EQ", False, True)
        act(upto("TH0"), upto("CG"), AF.Identity, bias=UNL)
        row_out("a", 0, 0, "TH0")
        entries(0)
        unlinked(1)
        mm(("X3", 0, 128), "SWK", ("EQ", 128, 256), False, True)
        lin(upto("SW", 258), [(ID, upto("TH0", 258)), ("IBW", upto("TL0", 258))])
        first(0, 64)
        keep(0, S0)
        ts("LS", upto("SW", 258), 256.0, OP.add, 15.0 * BW + 257.0, OP.min)
        entries(1)
        if r > 0:
            lin(upto("SL"), [(ID, "C"), ("IM", upto("NMV"))])
            act("SELF", upto("SL"), AF.Sign, bias=-2.5)
        lin(upto("PT"), [("I16", upto(H)), (ID, upto(L))])
        if r > 0:
            lin(upto("SL"), [(ID, "C"), ("IM", upto("NMV")), ("IM", "SELF"), ("IM", "SELF")])
            act("C", upto("SL"), AF.Identity, bias=-1.0)
        else:
            for n in LATER:
                act(n, ID, AF.Identity, scale=LATER[n])

        for q in (1, 2, 3):
            first(*CHS[q])
            keep(q, S0)
            if q > 1 and r == 0:
                shown_places(q - 2)
            if q == 3:
                ts("LU", upto("PT"), float(E), OP.add)
        if r == 0:
            dma("s", T.BIG[0:128:16, PG0 + 1536:Q0], T.XB[0:128:16, 0:Q0 - PG0 - 1536], [("XB", 0, Q0 - PG0 - 1536)], [("BIG", PG0 + 1536, Q0)])

        def offs(s, q):
            c0, c1 = CHS[q] if s < 5 else CH[q]
            if s < 5:
                ts((LEVEL[s], c0, c1), (BK[q], 0, c1 - c0), float(E), OP.add, E + 31.0, OP.min)
            else:
                ts((LT, c0, c1), (BK[q], 0, c1 - c0), 1.0, OP.add, 32.0, OP.min)

        for s in range(1, 6):
            src = S0 if s % 2 == 0 else S1
            dst = S0 if s % 2 == 1 else S1
            pin, pout = ("P0", "P1") if s % 2 == 1 else ("P1", "P0")
            lst = LEVEL[s - 1]

            def pointers(q):
                c0, c1 = (CHS if s < 5 else CH)[q]
                c = c0 + (HELP if (s, q) == (1, 1) else 0)
                if c > c0:
                    gv(row(pout, c0, c), (pin, 0, P), ("LS", c0, c))
                if c < c1:
                    ga(row(pout, c, c1), (pin, 0, P if s == 1 else ES), ("LS" if s == 1 else lst, c, c1))
                extract((BK[q], 0, c1 - c0), pout, c0, c1)

            def double(c0, c1):
                gt(big(dst, c0, c1) if s < 5 else sums(c0, c1), ("BIG", src, src + ES), (lst, c0, c1), big(A0, c0, c1), OP.add)

            if s < 5:
                for q, (c0, c1) in enumerate(CHS):
                    if s > 1:
                        if (s, q) == (2, 0):
                            offs(1, 0)
                        if s < SPLIT:
                            double(c0, c0 + 40)
                        if q < 3:
                            offs(s - 1, q + 1)
                        else:
                            offs(s, 0)
                        double(c0 + 40 * (s < SPLIT), c1)
                        if (s, q) != (4, 1):
                            keep(q, dst)
                    pointers(q)
            else:
                offs(4, 1)
                ga("PS", ("P0", 0, ES), "LW")
                extract(("CG", 0, 32), "PS", 0, 32)
                (ga if PGS else gv)(PG, S16, "LW")
                double(0, 64)
                offs(4, 2)
                ga(sums(64, XA), S16, (lst, 64, XA))
                double(128, XB)
                ts("LX", ("CG", 0, 32), float(E), OP.add, E + 31.0, OP.min)
                ga("PS", ("P0", 0, ES), "LX")
                extract(("CG", 0, 32), "PS", 0, 32)
                if XA < 128:
                    ga(sums(XA, 128), S16, (lst, XA, 128))
                dma("g", ap(sums(64, 128)), ap(big(S1, 64, 128)), [big(S1, 64, 128), sums(64, 128)], [sums(64, 128)], accum_op=OP.add)
                offs(4, 3)
                double(XB, XB + 16)
                gt(MK, S16, "LX", PG, OP.add)
                pointers(0)
                double(XB + 16, YA)
                ts("LY", ("CG", 0, 32), 1.0, OP.add, 32.0, OP.min)
                double(YA, YA + 16)
                gt(PG, upto("RT", 33), "LY", MK, OP.mult)
                ga(row("P1", 128, 192), ("P0", 0, ES), (lst, 128, 192))
                lin(upto("SW"), [(("IW", 32, 160), part(PG, 0, 256))])
                extract(("X2", 0, 64), "P1", 128, 192)
                act(part(PAY, 0, 256), upto("SW"), AF.Copy)
                show(0, r, QG)
                pointers(3)
                lin(upto("CG"), [(("IW", 32, 160), part(PG, 256, 512)), (("IN", 32, 160), part(PG, 0, 256))])
                ga(row("P1", 64, 128), ("P0", 0, ES), (lst, 64, 128))
                act(part(PAY, 256, 512), upto("CG"), AF.Abs)
                show(1, r, RG)
                extract(("X1", 0, 64), "P1", 64, 128)
                double(YA + 16, 256)
            if s == 1:
                ga(upto("PS"), ("P0", 0, P), "SS")
                extract(("PT", 0, 16), "PS", 0, 16)
                if not last:
                    extract(("PT", 16, 32), "PS", 0, 16, "ZB")
            if s == 2:
                lin(SL, [("IC", "C"), ("ID15", upto(H)), ("ID191", upto(L)), ("IK", "SN")])
            if s == 3:
                ts(("LW", 16, 32), ("PT", 0, 16), float(E), OP.add, E + 31.0, OP.min)
                if last:
                    tt(("KB", 16, 32), ("PT", 0, 16), ("DB", 16, 32), OP.min)
                else:
                    tt(("KB", 48, 64), ("PT", 16, 32), ("DB", 48, 64), OP.min)
            if s == 4 and not last:
                ts(("KU", 16, 32), ("KB", 48, 64), 256.0, OP.add)
        act("KEY", SL, AF.Relu, bias=G0 + E - K)
        lin(SL, [("IA", "C"), ("I16", upto(H)), (ID, upto(L)), (INF, "KEY")])
        if last:
            for h in range(2):
                extract(("SW", 128 * h, 128 * h + 128), "P1", 0, 128, step=2, first=1 - h)
        offs(5, 0)
        for q, (c0, c1) in enumerate(CH[k] for k in LATE):
            c = c0 + (MS if q < 3 else 0)
            if c > c0:
                gt(big(Q0, c0, c), upto("RT", 33), (LT, c0, c), sums(c0, c), OP.mult)
            if q < 3:
                offs(5, LATE[q + 1])
            gt(big(Q0, c, c1), upto("RT", 33), (LT, c, c1), sums(c, c1), OP.mult)
            if q < QS and QS - q < 3:
                act(big(S1, c0, c1), big(Q0, c0, c1), AF.Copy)
            elif q % 2 == 0:
                gcopy(big(S1, c0, c1), big(Q0, c0, c1))
            else:
                dma("s", ap(big(S1, c0, c1)), ap(big(Q0, c0, c1)), [big(Q0, c0, c1)], [big(S1, c0, c1)])
            if q == 0:
                act("KEY", SL, AF.Identity, bias=float(G0 + E))
            if q == 1 and r == 0:
                stamps(0)
        if r == 0:
            cut_constants()

        def margin(c0, c1):
            act(row("MB", c0, c1), row("RB", c0, c1), AF.Identity, bias=MARGIN)

        for q, (c0, c1) in enumerate(C1):
            gt(big(S1, c0, c1), QA, ("LU", c0, c1), big(S1, c0, c1), OP.subtract)
            act(row("RB", c0, c1), big(S1, c0, c1), AF.Abs)
            if q in EARLYM:
                margin(*EARLYM[q])
        if MV:
            ts(row("MB", 0, MV), row("RB", 0, MV), MARGIN, OP.add)
        if last:
            ts("LB", upto("SW"), 1.0, OP.add, 32.0, OP.min)
        if r == 0:
            ms("STB", STAMP[0])
            ts(("COL", 1, 2), ("COL", 0, 1), float(FLAG), OP.not_equal)
        for c in LATEM:
            margin(*c)

        def votes(c0, c1):
            b = [b for b in range(4) if GR[b][0] <= c0 < GR[b][1]][0]
            b0, b1 = GR[b]
            if c0 == b0:
                lin((BK[b], 0, b1 - b0), [("I8K", upto("CB", b1 - b0))] + [("I16K", (n, b0, b1)) for n in ["EQ"] + kept], stop=False)
            gt(row("P1", c0, c1), "RB", ("LU", c0, c1), row("MB", c0, c1), OP.is_gt)
            if c1 == b1:
                extract((BK[b], 0, b1 - b0), "P1", b0, b1, "ZC", False)

        def offsets(b, k):
            b0, b1 = GR[b]
            x = (BK[b], 256, 256 + b1 - b0)
            if k == 0:
                tt(x, (BK[b], 0, b1 - b0), ("KEY", b0, b1), OP.max)
            elif k == 1:
                tt(x, x, ("DUM", b0, b1), OP.min)
            else:
                cp((LC, b0, b1), x)

        def scalar_stamps(c0, c1):
            n = 16 * (c1 - c0)
            op("a", lambda: g.scalar.activation(T.BIG[:].indirect(T[LC][:, c0:c1]), T.STF[:, 0:n], AF.Silu), ["STF", (LC, c0, c1)], ["BIG"])

        def vector_stamps(c0, c1):
            put("W1", (LC, c0, c1), ("STB", 0, 16 * (c1 - c0)))

        for c in ((0, 48), (48, 64), (64, 112)):
            votes(*c)
        for b, pieces in enumerate((((112, 128), (128, 144), (144, 192)), ((192, 204), (204, 216), (216, 256)))):
            for k, c in enumerate(pieces):
                offsets(b, k)
                votes(*c)
        for c in SC[:2]:
            scalar_stamps(*c)
        vector_stamps(*VC[0])
        for k in range(3):
            offsets(2, k)
            offsets(3, k)
        for c in SC[2:]:
            scalar_stamps(*c)
        WG2 = ("RB", 1024, 1216)
        dma("a", ap(WG2), T.BIG[0:128:16, 0:G0], [("BIG", 0, G0)], [WG2])
        for n in ("P0", "P1")[:1 + VADD]:
            dma("g", T[n][1:128:4, 0:E], T.BIG[0:128:16, G0:KEYS], [("BIG", G0, KEYS)], [(n, 0, E, 0x2222)])
        for k, c in enumerate(VC[1:]):
            if not last:
                cursors("C", 1, k)
            vector_stamps(*c)
        dma("s", T.WG1[:], T.W1[0:128:16, 0:G0], [("W1", 0, G0)], ["WG1"])
        for n in ("P0", "P1")[:1 + VADD]:
            dma("s", T[n][0:128:4, 0:E], T.W1[0:128:16, G0:KEYS], [("W1", G0, KEYS)], [(n, 0, E, 0x1111)])

        def sums_out(c0, c1):
            for h in range(2):
                op("v", lambda h=h: g.vector.tensor_tensor(T.MB[:, 32 * c0 + h:32 * c1:2], T.YT[:, 0:33].indirect(T.LB[:, 128 * h + c0:128 * h + c1]),
                                                           T.XB[:, 32 * c0 + 1 - h:32 * c1:2], OP.add),
                   ["YT", "LB", row("XB", 2 * c0, 2 * c1)], [("MB", 32 * c0, 32 * c1, 1 << h)])

        def store(c0, c1):
            wait("s", ("lh%d" % r, ne))
            dma("s", T.ys[:, 32 * c0:32 * c1], T.MB[:, 32 * c0:32 * c1], [row("MB", 2 * c0, 2 * c1)], [])

        kb = 0 if last else 32
        mm(("X2", 0, 32), IDF, ("DB", kb, kb + 32), True, False)
        act("WD", ID, AF.Identity, scale=-stamp)
        if last:
            sums_out(0, 48)
            sums_out(48, 88)
            act("SN", "C", AF.Relu, bias=-2.0)
            act("SN", "SN", AF.Identity, scale=-4.0, bias=1.0)
        else:
            if r == 0:
                act("H", upto("AL0"), AF.Copy)
                act("L", upto("AL1"), AF.Copy)
                act(upto("YT", 33), upto("YT", 33), AF.Identity, scale=0.5)
            stamps(r + 1)
            chosen("C", 1, 2)
            digits(1, (3, 6))
        for k in range(4):
            mm(("CG", 0, 48), ("IW", 96, 224), part(WG2, 48 * k, 48 * k + 48), k == 0, False)
        for k in range(4):
            mm(("CG", 0, 48), ("IB", 96, 224), ("WG1", 48 * k, 48 * k + 48), False, k == 3)
        ts("HG", ("CG", 0, 48), thr, OP.is_ge, -1.0, OP.mult)
        send("HG", range(1, N), lambda d: T.RH[:, (d - 1) * 48:d * 48], "ah%d" % r, "lh%d" % r, -1, ["RH"], [QG, RG])
        for h, (c0, c1) in enumerate(HALF):
            lin((BK[h], 0, 128), [("WD", (n, c0, c1)) for n in ["EQ"] + kept], stop=False)
            if h or not VADD:
                extract((BK[h], 0, 128), "P0", c0, c1, "ZH", start=False, stop=False)

        def partners(share):
            if not VADD:
                shared(("P0", 0, P), "LU", share)
                return
            for q in range(2):
                ga(row("P1", *CH[2 + q]), ("P0", 0, P), ("LU",) + CH[2 + q])
                gt(row("P1", *CH[q]), ("P0", 0, P), ("LU",) + CH[q], row("P1", *CH[q]), OP.add)

        def returned():
            for h in range(2):
                for d in range(3):
                    mm(("X2", 16 * h, 16 * h + 16), "IK", ("RH", 64 * d, 64 * d + 16), False, (h, d) == (1, 2))
            for c0 in (0, 16):
                tt(("TH", c0, c0 + 16), ("X2", c0, c0 + 16), ("KB", kb + c0, kb + c0 + 16), OP.max)
            for c0 in (0, 16):
                ts(("LH", c0, c0 + 16), ("TH", c0, c0 + 16), float(E) if last else 256.0, OP.add)

        if last:
            partners(SHARE_0)
            store(0, 88)
            sums_out(88, 104)
            returned()
            for c0 in (0, 16):
                put("P1", ("LH", c0, c0 + 16), upto("STB"))
            sums_out(104, 128)
            store(88, 128)
            for h, (c0, c1) in enumerate(HALF):
                extract((BK[h], 0, 128), "P1", c0, c1, "ZH", start=False)
            for h, (c0, c1) in enumerate(HALF):
                x = (BK[h], 128, 256)
                ts(x, (BK[h], 0, 128), thr - stamp, OP.is_ge)
                tt(x, x, ("SN", c0, c1), OP.mult)
                tt(("KEY", c0, c1), x, ("C", c0, c1), OP.add)
                dma("sa"[h], T.yc[:, c0:c1], T.KEY[:, c0:c1], [("KEY", c0, c1)], [])
        else:
            partners(SHARE_H)
            op("a", lambda: g.scalar.activation(T.PS[:], ap(NAMESD).indirect(T.KU[:]), AF.Identity, scale=T.COL[:, 1:2]), [NAMESD, "KU", "COL"], ["PS"])
            for k, q in enumerate((2, 0, 3, 1) if VADD else range(4)):
                extract((BK[q // 2], 64 * (q % 2), 64 * (q % 2) + 64), "P1", CH[q][0], CH[q][1], "ZH", start=False, stop=q % 2 == 1)
            for h in (1, 0) if VADD else (0, 1):
                ts(("NMV",) + HALF[h], (BK[h], 0, 128), thr - stamp, OP.is_lt)
            row_out("s", 1, FLAG, "NMV")
            blocks()
            ts("LB", upper("SL"), 256.0, OP.add)
            returned()
            lin(upto("PT"), [(ID, "H"), ("IM", upto("AL0"))])
            lin(upper("PT"), [(ID, "L"), ("IM", upto("AL1"))])
            act("STB", ("XC", 0, NSV), AF.Identity, scale=0.0, bias=STAMP[r + 1])
            for h in range(2):
                put(NAMESD, ("LH", 16 * h, 16 * h + 16), ("PS", 256 * h, 256 * h + 256))
            dma("s", T.NMV[:], T.P0[FLAG:128:16, P:2 * P], [NAMES + (1 << FLAG,)], ["NMV"])

    for s in total:
        if max([0] + [waited[k] for k in waited if k[1] == s]) < total[s]:
            wait("g", (s, total[s]))
